import numpy as np, ml_dtypes
CORES = [2,3,42,43,82,83,122,123]
N = 8
import mx_ref
BF = ml_dtypes.bfloat16
def gentries(a):
    return np.ascontiguousarray(a.reshape(8, 16, -1).transpose(0, 2, 1)).reshape(8, -1)
def gtable(e):
    e = np.asarray(e); return np.ascontiguousarray(e.reshape(8, -1, 16).transpose(0, 2, 1)).reshape(128, -1).astype(np.int32)
def gcols(t, e):
    v = np.concatenate([t.reshape(8, 16, -1, 4), np.zeros((8, 16, 1, 4), BF)], axis=2)
    return np.ascontiguousarray(np.stack([v[g][:, e[g]] for g in range(8)])).reshape(128, -1)
def gpick(z, e):
    return np.concatenate([z[16 * g:16 * g + 16][:, e[g]] for g in range(8)])
def tile(rs):
    return np.stack(rs, axis=2).reshape(128, -1).astype(BF)
def pick(q, e):
    c = np.concatenate([q[0].reshape(128, -1, 4), np.zeros((128, 1, 4), np.uint8)], axis=1); s = np.concatenate([q[1], np.ones((16, 1), np.uint8)], axis=1)
    return (np.ascontiguousarray(c[:, e].reshape(128, -1)), np.ascontiguousarray(s[:, e]))
def join(*qs):
    return (np.concatenate([q[0] for q in qs], axis=1), np.concatenate([q[1] for q in qs], axis=1))
def put(q, e, v):
    c, s = q[0].reshape(128, -1, 4).copy(), q[1].copy(); c[:, e] = v[0].reshape(128, -1, 4); s[:, e] = v[1]
    return (c.reshape(128, -1), s)
def pk(c, s):
    return (np.ascontiguousarray(c), mx_ref.live(s))
def emit(q):
    return q[0], q[1]
def packed(v, rng):
    q = [mx_ref.quantize(np.ascontiguousarray(v[r])) for r in range(N)]
    return np.stack([a for a, b in q]), np.stack([mx_ref.plane(b, rng) for a, b in q])
def values_of_codes():
    e, c = np.zeros((128, 128, 4), np.float32), np.zeros((128, 2, 4), np.uint8)
    e[np.arange(128), np.arange(128), 0] = 1
    c[:127, :, 0] = np.arange(256).reshape(2, 128).T[:127]
    return mx_ref.matmul(mx_ref.quantize(e.reshape(128, 512).astype(BF)), (c.reshape(128, 8), np.full((16, 2), 127, np.uint8))).T.reshape(-1).astype(np.float64)
CODE_VALUE, SCALE_VALUE = values_of_codes(), 2.0 ** (np.arange(256) - 127.0)
def decode(q):
    return (CODE_VALUE[q[0]].reshape(16, 8, -1, 4) * SCALE_VALUE[q[1]][:, None, :, None] + 0.0).reshape(128, -1).astype(np.float32)
def f(rng, *shape):
    return mx_ref.flush((rng.standard_normal(shape, dtype=np.float32) * np.exp2(rng.integers(-2, 3, shape[:-1] + (1,)))).astype(BF))
def wide(rng, *shape, cols=0):
    v = rng.standard_normal(shape, dtype=np.float32) * np.exp2(rng.integers(-12, 13, shape)).astype(np.float32)
    if cols: v *= np.repeat(np.exp2(rng.integers(-cols, cols + 1, shape[:-2] + (1, shape[-1] // 4))) * (rng.random(shape[:-2] + (1, shape[-1] // 4)) > 0.0625), 4, axis=-1).astype(np.float32)
    return mx_ref.flush(v.astype(BF))
C, H = 320, 160
STEP = [1, 2, 4]
G, OWN = np.arange(8)[:, None], np.tile(np.arange(C), (8, 1))
def numbers_of(rng):
    return {"x": np.array(f(rng, N, 128, 4 * C)), "u": np.array(f(rng, N, 128, 512)), "v": np.array(f(rng, N, 128, 512))}
def stored(a, m):
    return {"fl": np.stack([gtable(a[r]) for r in range(N)]), "ml": np.stack([gtable(m[r]) for r in range(N)])}
def pairs(o):
    m = np.zeros(o.shape, np.int64)
    np.put_along_axis(m, o[..., ::2], o[..., 1::2], axis=-1)
    np.put_along_axis(m, o[..., 1::2], o[..., ::2], axis=-1)
    return m
def ring(o):
    a = np.zeros(C, np.int64)
    a[o] = np.roll(o, -1)
    return a
def lists(rng):
    e = np.tile(np.arange(C), (N, 8, 1))
    return rng.permuted(e, axis=2), pairs(rng.permuted(e, axis=2))
def layers(rng, still=[]):
    w = np.array(f(rng, N, 128, 2048)).reshape(N, 8, 16, 4, 8, 16, 4)
    for i in still:
        w[:, :, i] = 0
        w[:, :, :, :, :, i] = 0
    return w
def weights(rng, w):
    c, s = packed(np.ascontiguousarray(w).reshape(N, 128, 2048), rng)
    return {"wc": c, "ws": s}
def parity():
    i = np.arange(N)
    return (i ^ (i >> 1) ^ (i >> 2)) % 2
def setup_inputs(rng):
    return {**numbers_of(rng), **stored(*lists(rng)), **weights(rng, layers(rng))}
def setup_inputs_ties(rng):
    d = numbers_of(rng)
    o = rng.permutation(N)
    k = rng.integers(0, 4, (N, 8, C))
    k[o[1]] += 1
    k[o[2], rng.permutation(8)[:4]] = 1
    a, m = lists(rng)
    g = int(rng.integers(8))
    a[:, g] = np.arange(C)
    m[:, g] = (np.arange(C) + H) % C
    k[o[3], g] = np.arange(C) >= H
    x = d["x"].reshape(N, 8, 16, C, 4)
    x[:, :, 0] = 0
    x[:, :, 0, :, 0] = k.astype(np.float32).astype(BF)
    u = d["u"].reshape(N, 128, 128, 4)
    u[:, :, ::16] = 0
    for r in range(N):
        for h in range(0, 128, 16): u[r, h, h, 0] = 0.0 if r == o[0] else -1.0 if r == o[1] else 1.0
    return {"x": x.reshape(N, 128, 4 * C), "u": u.reshape(N, 128, 512), "v": d["v"], **stored(a, m), **weights(rng, layers(rng, [0]))}
def setup_inputs_near(rng):
    d = numbers_of(rng)
    x = d["x"].astype(np.float32).reshape(N, 8, 16, C, 4)
    x[:, :, 0] = 0
    x[:, :, 8:] = 0
    x[:, :, 15, :, 0] = 2.0 ** -26
    u = d["u"].reshape(N, 128, 128, 4)
    u[:, :, ::16] = 0
    o = rng.permutation(N) % 4
    for r in range(N):
        c = rng.choice([-1.0, 1.0], (8, 1))
        s = rng.integers(0, 16, (8, C))
        digits = ((s[:, :, None] >> np.arange(4)) & 1) * np.exp2(np.arange(4) - 23.0)
        if o[r] < 2:
            x[r, :, 0, :, 0] = c
            x[r, :, 8] = digits
            x[r, :, 11, :, 0] = 2.0 ** -10
        elif o[r] == 2: x[r, :, 8] = digits * rng.choice([-1.0, 1.0], (8, C, 1))
        else:
            x[r, :, 8, :, 0] = np.where(s < 8, 1.25, 0.0) * 2.0 ** -30 * c
            x[r, :, 9, :, 0] = np.where(s < 8, 0.0, 1.125) * 2.0 ** -30 * c
            for g in rng.permutation(8)[:4]:
                e = rng.choice([-1.0, 1.0], C) * 2.0 ** -30
                x[r, g, 8, :, 0] = 1.25 * e
                x[r, g, 9, :, 0] = -1.125 * e
            x[r, :, 13, :, 0] = rng.choice([-1.0, 1.0], (8, C)) * 2.0 ** -30
        at = [0, C - 1, int(rng.integers(C)), int(rng.integers(C))]
        for g, j in zip(rng.permutation(8)[:4], at): x[r, g, 0, j, 0] = 2.0 ** 29 * rng.choice([-1.0, 1.0])
        k = 1.0 if o[r] == 0 else 2.0 ** -30
        for h in range(0, 128, 16):
            u[r, h, h, 0] = k if o[r] < 2 else 1.0
            if o[r] < 2: u[r, h + 11, h, 0] = k
            if o[r] < 3: u[r, h + 8, h] = k
            else:
                u[r, h + 8, h, 0] = k
                u[r, h + 9, h, 0] = 1.125 * k
                u[r, h + 14, h, 0] = k
    w = layers(rng, [0, 8, 9, 10, 11, 12, 13, 14, 15])
    for g in range(8): w[:, g, 13, 0, g, 14, 0] = 2.0 ** -5
    return {"x": x.reshape(N, 128, 4 * C).astype(BF), "u": u.reshape(N, 128, 512), "v": d["v"], **stored(*lists(rng)), **weights(rng, w)}
def setup_inputs_odd(rng):
    d = numbers_of(rng)
    x = (1.0 + (2 * rng.integers(0, 64, (N, 16, 8, C, 4)) + 1) * 2.0 ** -7) * np.exp2(-rng.integers(0, 7, (N, 16, 8, C, 4)).astype(np.float64)) * rng.choice([-1.0, 1.0], (N, 16, 8, C, 4))
    x[:, :, 0, :, 0] = (np.where((parity()[:, None] + np.arange(16)) % 2 == 0, 1.96875, 1.875) * 2.0 ** 8)[:, :, None]
    x[:, :, 1, :, 0] = rng.integers(8, 16, (N, 16, C)) * 2.0 ** -8
    u = d["u"].reshape(N, 16, 8, 128, 4)
    u[:, :, 0, ::16] = 0
    for r in range(N):
        for g in rng.permutation(8)[:2]:
            u[r, :, :, 16 * g] = 0
            u[r, 2 * g + parity()[r], 1, 16 * g, 0] = 1.0
    w = layers(rng, [0, 1, 8, 9])
    for g in range(8):
        for i in (0, 8): w[:, g, i, 0, g, i, 0] = -0.5
    return {"x": x.astype(np.float32).reshape(N, 128, 4 * C).astype(BF), "u": u.reshape(N, 128, 512), "v": d["v"], **stored(*lists(rng)), **weights(rng, w)}
def setup_inputs_ends(rng):
    d = numbers_of(rng)
    r0 = int(rng.integers(N))
    a = rng.permutation(np.array([r0, r0 ^ STEP[0], r0 ^ STEP[1], r0 ^ STEP[0] ^ STEP[1]]))
    z = rng.permutation(np.setdiff1d(np.arange(N), a))
    x = np.where(rng.random((N, 128, C, 4)) < 0.5, -1.0, -0.9375) * 2.0 ** 30
    x[:, 5] *= 2.0 ** -10
    c = rng.choice([-1.0, 1.0], (128, 1, 4))
    for r in z[:2]: x[r] = c * (1.0 + 0.125 * rng.integers(0, 8, (128, C, 4))) * 2.0 ** -30
    for r in z[2:]: x[r] = x[r] * rng.choice([-1.0, 1.0], (1, C, 1))
    size = np.full(N, 2.0 ** 30)
    size[a[2:]] = 2.0 ** -30
    size[z[1::2]] = 2.0 ** -30
    u = d["u"].astype(np.float32).reshape(N, 128, 128, 4)
    w = np.zeros((N, 128, 4, 128, 4), np.float32)
    i = np.arange(128)
    for b in range(4): w[:, i, b, i, b] = 32.0
    w[a[2], 5, 0, 5, 0] = 2.0 ** 8
    w[a[2], 6, 0, 6, 0] = 2.0 ** -8
    k = np.array([[0, 0, 2, 2, 1, 1, 3, 3], [2, 1, 0, 3, 0, 3, 2, 1]])[parity()][:, rng.permutation(8)]
    e, m = lists(rng)
    j = np.arange(C)
    for r in range(N):
        h = rng.permutation(8)
        u[r, :, ::16] = (np.where(h < 2, 0.0, h % 2 * 2.0 - 1.0) * size[r])[None, :, None]
        for g in range(8):
            t = int(rng.integers(4))
            if t: m[r, g] = [C - 1 - j, j ^ 1, (j + H) % C][t - 1]
            e[r, g] = [ring(rng.permutation(C)), j, ring(j), m[r, g]][k[r, g]]
    u[:, 5, ::16] = 0
    v = rng.choice([-1.0, 1.0], (N, 128, 512)) * size[:, None, None]
    return {"x": x.astype(np.float32).reshape(N, 128, 4 * C).astype(BF), "u": u.reshape(N, 128, 512).astype(BF), "v": v.astype(np.float32).astype(BF), **stored(e, m), **weights(rng, w.astype(BF))}
def setup_inputs_spread(rng):
    d = setup_inputs(rng)
    d["x"] = wide(rng, N, 128, 4 * C, cols=6)
    return d
def check_inputs(d):
    b = []
    for k in ("x", "u", "v"):
        a = np.abs(d[k].astype(np.float32))
        if not (np.isfinite(a).all() and ((a == 0) | (a >= 2.0 ** -30) & (a <= 2.0 ** 30)).all()): b.append("a value of " + k)
    none, least, most = [emit(mx_ref.quantize(np.full((128, 16), k, np.float32).astype(BF)))[1][0, 0] for k in (0.0, 2.0 ** -8, 2.0 ** 8)]
    for r in range(N):
        if (np.sort(gentries(d["fl"][r]), axis=1) != OWN).any(): b.append("fl: a group that doesn't name every column once")
        m = gentries(d["ml"][r])
        if ((m < 0) | (m >= C)).any() or (m == OWN).any() or (m[G, m] != OWN).any(): b.append("ml: columns that aren't each other's mates")
        if ((d["wc"][r] == 0x7F) | (d["wc"][r] == 0xFF)).any(): b.append("wc: a code that is no number")
        s = mx_ref.live(d["ws"][r])
        if ((s != none) & ((s < least) | (s > most))).any(): b.append("ws: a scale out of range")
    return b
def leaders(a, s):
    best, w = OWN, a
    for _ in range(C - 1):
        p, o = s[G, w], s[G, best]
        best = np.where((p > o) | (p == o) & (w < best), w, best)
        w = a[G, w]
    return best
def hops(a, best):
    n, w = np.zeros((8, C), np.int64), best
    for _ in range(C - 1):
        go = w != OWN
        n, w = n + go, np.where(go, a[G, w], w)
    return n
def walk(a, at, n):
    for i in range(C - 1): at = np.where(i < n, a[G, at], at)
    return at
def reference(x, u, v, fl, ml, wc, ws):
    qu = [mx_ref.quantize(u[r]) for r in range(N)]
    lay = [pk(wc[r], ws[r]) for r in range(N)]
    cyc, mate = [gentries(fl[r]) for r in range(N)], [gentries(ml[r]) for r in range(N)]
    now = [x[r] for r in range(N)]
    for step in STEP:
        q = [mx_ref.quantize(now[r]) for r in range(N)]
        t = [decode(q[r]).astype(BF) for r in range(N)]
        made, after = [], []
        for r in range(N):
            p = r ^ step
            s = mx_ref.matmul(qu[r], q[r])[::16] + np.float32(0.0)
            lead = leaders(cyc[r], s)
            far = walk(cyc[p], lead, hops(cyc[r], lead))
            mine = s[G, far]
            other = mine[G, mate[r]]
            swap = np.where(OWN < mate[r], mine < other, other < mine)
            new = cyc[r][G, np.where(swap, mate[r], OWN)]
            back = np.argsort(new, axis=1)
            z = mx_ref.quantize(((gcols(t[r], new).astype(np.float32) + gcols(t[p], far).astype(np.float32)) * np.float32(0.5)).astype(BF))
            res = [mx_ref.matmul(pick(lay[r], np.arange(128 * b, 128 * b + 128)), z) * np.float32(0.03125) for b in range(4)]
            made.append(tile([(t[r][:, b::4].astype(np.float32) + gpick(res[b], back)) * np.float32(0.5) for b in range(4)]))
            after.append(new)
        now, cyc = made, after
    y, nl = np.zeros((N, 128, C), np.float32), np.zeros((N, 8, C), np.float32)
    oc, osc = np.zeros((N, 128, 4 * C), np.uint8), np.zeros((N, 16, C), np.uint8)
    for r in range(N):
        q = mx_ref.quantize(now[r])
        y[r] = mx_ref.matmul(mx_ref.quantize(v[r]), q)
        nl[r] = cyc[r]
        oc[r], osc[r] = emit(q)
    return {"y": y, "nl": nl, "oc": oc, "osc": osc}

@@ -1,0 +1,472 @@
+from concourse.mybir import dt, AluOpType as A, ActivationFunctionType as AF
+
+C = 320
+ROUNDS = 3
+MASKS = (1, 2, 4)
+MID = 160
+TINY = 2.0 ** -102
+STEPB = 12
+UNIT = 2048.0
+
+NF, NB, NT, NI, NU = 34, 118, 54, 18, 36
+SCRATCH = {
+    "rowf": ("sbuf", [128, C * NF], "float32"),
+    "rowb": ("sbuf", [128, C * NB], "bfloat16"),
+    "tabf": ("sbuf", [128, 20 * NT], "float32"),
+    "tabi": ("sbuf", [128, 20 * NI], "int32"),
+    "tabu": ("sbuf", [128, 20 * NU], "uint16"),
+    "fli": ("sbuf", [128, 20], "int32"),
+    "mli": ("sbuf", [128, 20], "int32"),
+    "jm": ("sbuf", [128, 2 * C], "float32"),
+    "dcon": ("sbuf", [128, 2 * C], "bfloat16"),
+    "pcol": ("sbuf", [128, 8], "int32"),
+    "pcolf": ("sbuf", [128, 16], "float32"),
+    "ui": ("sbuf", [128, 8], "int32"),
+    "u16": ("sbuf", [128, 8], "uint16"),
+    "half": ("sbuf", [128, 512], "bfloat16"),
+    "et": ("sbuf", [128, 2048], "bfloat16"),
+    "eq": ("sbuf", [128, 512], "float8_e4m3fn_x4"),
+    "es": ("sbuf", [128, 512], "uint8"),
+    "uin": ("sbuf", [128, 512], "bfloat16"),
+    "vin": ("sbuf", [128, 512], "bfloat16"),
+    "xin": ("sbuf", [128, 4 * C], "bfloat16"),
+    "uq": ("sbuf", [128, 128], "float8_e4m3fn_x4"),
+    "us": ("sbuf", [128, 128], "uint8"),
+    "up": ("sbuf", [128, 128], "float8_e4m3fn_x4"),
+    "ups": ("sbuf", [128, 128], "uint8"),
+    "vq": ("sbuf", [128, 128], "float8_e4m3fn_x4"),
+    "vs": ("sbuf", [128, 128], "uint8"),
+    "wq": ("sbuf", [128, 512], "float8_e4m3fn_x4"),
+    "wsc": ("sbuf", [128, 512], "uint8"),
+    "ys": ("sbuf", [128, C], "float32"),
+    "nls": ("sbuf", [128, C], "float32"),
+    "ps": ("psum", [128, 512 * 8], "float32"),
+}
+for _r in range(ROUNDS + 1):
+    SCRATCH["xq%d" % _r] = ("sbuf", [128, C], "float8_e4m3fn_x4")
+    SCRATCH["xs%d" % _r] = ("sbuf", [128, C], "uint8")
+for _r in range(ROUNDS):
+    SCRATCH["lq%d" % _r] = ("sbuf", [128, C], "float8_e4m3fn_x4")
+    SCRATCH["ls%d" % _r] = ("sbuf", [128, C], "uint8")
+    SCRATCH["la%d" % _r] = ("sbuf", [128, 60], "uint16")
+    SCRATCH["lb%d" % _r] = ("sbuf", [128, 20], "uint16")
+    SCRATCH["sa%d" % _r] = ("sbuf", [128, 80], "uint16")
+    SCRATCH["sb%d" % _r] = ("sbuf", [128, 20], "uint16")
+for _h in range(2):
+    for _k in ("fh", "fs", "gp", "zt", "xt"): SCRATCH["%s%d" % (_k, _h)] = ("sbuf", [128, 4 * C], "bfloat16")
+    SCRATCH["rs%d" % _h] = ("sbuf", [128, 4 * C], "float32")
+    SCRATCH["zq%d" % _h] = ("sbuf", [128, C], "float8_e4m3fn_x4")
+    SCRATCH["zs%d" % _h] = ("sbuf", [128, C], "uint8")
+
+LOADS = ("fl", "ml", "x", "u", "v", "wc", "ws")
+STORES = ("oc", "os0", "os1", "os2", "os3", "y", "nl")
+SEMAPHORES = ["ev", "es", "et", "eg", "rl"] + ["ld_" + n for n in LOADS] + ["st_" + n for n in STORES] \
+    + ["%s%d" % (k, r) for k in ("aq", "aa", "ab") for r in range(ROUNDS)]
+
+CY, GA, WAKE = 0.83 * 1.2, 1.5, 130.0
+VB, LOOK, PW = 500.0, 150.0, 5.0
+OFFS = "imdgjjbagglflfmjmjmjfhfbjgaggadgcabadamlfgfliaaefgcgfafhhmmgbhdgalbjdeadbmabldmfkmchgagjcmfmlajmamkmafmigcmdlihghblhcckekacmgeehjbiaahifjabajfgdagjmigacmiaakjmgfhjhjlihgcaagaaajbklmmifjadkelmgdgaagflhcimfajflmfmjedhdfgaimfmmhelghmjkhkmgemfkfgejeblmlkmfjhljlmmdmaaimfeigeccjmdlblcgjkbkhikhfgfafjbggfekaddhaamfgfegllajgaamgbmlfihiiaihgjklgmjhhhghgigaaaigajlckmakmammbadbgjkmkcliejmkcmeccbjaedjkkhffmjggcmjhadmikglamgkaahmfgmfbgaimaagjfkmmddafjgaecajbflhjelammlcmdeafjmlkjmhejdhbjikaddfajkgiiafdaadfbgfggflegkjeelmfgefeeffmccdbhbegkdbagmgekechddajdfmmahfmaddllhggblmmgegmamlecmhmehgljm"
+FLEX = "----------------------------------------------------------------s-v---sv-----s---ss---------s---ss----s---s-s------------ss---------------sss--------------s--s--v------------------------s--s----------s---s--------------s--------------s---s-s---s---ss---ss----s---s----------------s-------------s---------------s------------v-----sv--s---v-------------------vs------------s---ss--ss--s-------v--s--s------s---s---sssss---ss---s-----s---s----ss---ss-----s------------------------------s------v-------s-vsv---v--s-------------------v-------------s---s----s--ss------s--s--s------------"
+
+
+def add(P, cost, call, reads, writes, sem=None, val=16, after=(), lat=0.0):
+    i = len(P["ops"])
+    deps = set(after)
+    for k in reads:
+        if k in P["last"]: deps.add(P["last"][k])
+    for k in writes:
+        deps.update(P["readers"].get(k, []))
+        if k in P["last"]: deps.add(P["last"][k])
+    for k in reads: P["readers"].setdefault(k, []).append(i)
+    for k in writes:
+        P["last"][k] = i
+        P["readers"][k] = []
+    P["ops"].append({"c": cost, "f": call, "d": sorted(deps), "sem": sem, "val": val, "lat": lat})
+    return i
+
+
+def order(P):
+    ops = P["ops"]
+    n = len(ops)
+    succ = [[] for _ in range(n)]
+    for i in range(n):
+        for j in ops[i]["d"]: succ[j].append(i)
+    way = [0.0] * n
+    for i in range(n - 1, -1, -1):
+        best = 0.0
+        for s in succ[i]: best = max(best, way[s] + WAKE)
+        way[i] = best + min(ops[i]["c"].values()) + ops[i]["lat"]
+    way = [x + 500.0 * (ord(OFFS[i]) - 103) if i < len(OFFS) else x for i, x in enumerate(way)]
+    free = {"v": 0.0, "s": 0.0, "t": 0.0, "g": 0.0, "y": 0.0}
+    done, seq = [0.0] * n, []
+    left = [len(o["d"]) for o in ops]
+    at = {}
+
+    def open_(i):
+        at[i] = max([done[j] + WAKE for j in ops[i]["d"]], default=0.0)
+    for i in range(n):
+        if left[i] == 0: open_(i)
+    while at:
+        cand = []
+        for i, t in at.items():
+            c = ops[i]["c"]
+            if len(c) == 1:
+                e = next(iter(c))
+            elif i < len(FLEX) and FLEX[i] != "-":
+                e = FLEX[i]
+            else:
+                tv = max(t, free["v"])
+                busy = any(len(ops[j]["c"]) == 1 and "v" in ops[j]["c"] and u <= tv + c["v"] for j, u in at.items())
+                e = "s" if max(t, free["s"]) + c["s"] <= tv + c["v"] + (VB if busy else 0.0) else "v"
+            cand.append((t if e == "n" else max(t, free[e]), i, e))
+        t0 = min(x[0] for x in cand)
+        eng = max((x for x in cand if x[0] <= t0), key=lambda x: way[x[1]])[2]
+        st, i, e = max((x for x in cand if x[2] == eng and x[0] <= t0 + LOOK), key=lambda x: way[x[1]] - PW * (x[0] - t0))
+        del at[i]
+        c = ops[i]["c"][e]
+        if e != "n": free[e] = st + c
+        done[i] = st + c + ops[i]["lat"]
+        seq.append((st, i, e))
+        for s in succ[i]:
+            left[s] -= 1
+            if left[s] == 0: open_(s)
+    return seq, done
+
+
+def emit(P, g, T, seq):
+    ops = P["ops"]
+    queue = {"v": g.vector, "s": g.scalar, "t": g.tensor, "g": g, "y": g.sync}
+    name = {"v": "ev", "s": "es", "t": "et", "g": "eg"}
+    count = {e: 0 for e in name}
+    know = {e: {} for e in queue}
+    clock, own = {}, {}
+    for st, i, e in seq:
+        o = ops[i]
+        if e == "n":
+            clock[i], own[i] = {o["sem"]: o["val"]}, (o["sem"], o["val"])
+            continue
+        want = {}
+        for j in o["d"]:
+            s, v = own[j]
+            if v and know[e].get(s, 0) < v: want[s] = max(want.get(s, 0), v)
+        for j in o["d"]:
+            s, v = own[j]
+            if want.get(s, 0) >= v > 0:
+                for k, x in clock[j].items():
+                    if k != s and k in want and want[k] <= x: del want[k]
+        for s, v in want.items():
+            queue[e].wait_ge(T.sem[s], v)
+            know[e][s] = v
+        for j in o["d"]:
+            for k, x in clock[j].items(): know[e][k] = max(know[e].get(k, 0), x)
+        ins = o["f"](e)
+        clock[i] = dict(know[e])
+        if o["sem"] is None:
+            count[e] += 1
+            own[i] = (name[e], count[e])
+            ins.then_inc(T.sem[name[e]], 1)
+        else:
+            own[i] = (o["sem"], o["val"])
+            if o["val"]: ins.then_inc(T.sem[o["sem"]], o["val"])
+        if own[i][1]: clock[i][own[i][0]] = own[i][1]
+    return count
+
+
+def rank_program(g, core, T, topo):
+    rank = T.rank_of(core)
+    if rank is None: return
+    P = {"ops": [], "last": {}, "readers": {}}
+    slots = {"rowf": {}, "rowb": {}, "tabf": {}, "tabi": {}, "tabu": {}}
+    top = {k: 0 for k in slots}
+
+    def view(buf, unit, nm, w, a, b, s):
+        d = slots[buf]
+        if nm not in d:
+            d[nm] = top[buf]
+            top[buf] += (w + unit - 1) // unit * unit
+        o = d[nm]
+        b = w if b is None else b
+        return T[buf][:, o + a:o + b:s] if s else T[buf][:, o + a:o + b]
+
+    def F(nm, w=C, a=0, b=None, s=None): return view("rowf", C, nm, w, a, b, s)
+    def B(nm, w=C, a=0, b=None, s=None): return view("rowb", C, nm, w, a, b, s)
+    def tf(nm, w=20, a=0, b=None): return view("tabf", 20, nm, w, a, b, None)
+    def ti(nm, w=20, a=0, b=None): return view("tabi", 20, nm, w, a, b, None)
+    def tu(nm, w=20, a=0, b=None): return view("tabu", 20, nm, w, a, b, None)
+
+    def ts(out, in0, s1, s2, op0, op1, rd, wr, n=20):
+        def call(e): return g.vector.tensor_scalar(out, in0, s1, None, op0) if op1 is None else g.vector.tensor_scalar(out, in0, s1, s2, op0, op1)
+        return add(P, {"v": max(60.0, n * CY)}, call, rd, wr)
+
+    def tt(out, a, b, op, rd, wr, n=20, ind=False):
+        return add(P, {"v": 55 + n * CY * GA if ind else max(60.0, 2 * n * CY)}, lambda e: g.vector.tensor_tensor(out, a, b, op), rd, wr)
+
+    def scan(out, d0, d1, init, op0, op1, rd, wr, n=C, half=False):
+        return add(P, {"v": n * CY * (0.5 if half else 1.0)}, lambda e: g.vector.tensor_tensor_scan(out, d0, d1, init, op0, op1), rd, wr)
+
+    def vcopy(out, in_, rd, wr, n=20): return add(P, {"v": max(60.0, n * CY)}, lambda e: g.vector.tensor_copy(out, in_), rd, wr)
+
+    def scatter(out, in_, rd, wr): return add(P, {"v": 1300.0}, lambda e: g.vector.tensor_copy(out, in_), rd, wr)
+
+    def act(out, in_, func, rd, wr, scale=1.0, bias=None, ind=False):
+        def call(e): return g.scalar.activation(out, in_, func, scale=scale) if bias is None else g.scalar.activation(out, in_, func, bias=bias, scale=scale)
+        return add(P, {"s": 68 + C * CY * GA if ind else C * CY}, call, rd, wr)
+
+    def either(call, rd, wr, ind, n=C): return add(P, {"v": 55 + n * CY * GA, "s": 68 + n * CY * GA} if ind else {"v": n * CY, "s": n * CY}, call, rd, wr)
+
+    def move(out, in_, rd, wr, ind=False, scale=None):
+        def call(e):
+            if e == "s": return g.scalar.activation(out, in_, AF.Copy) if scale is None else g.scalar.activation(out, in_, AF.Copy, scale=scale)
+            return g.vector.tensor_copy(out, in_) if scale is None else g.vector.tensor_scalar(out, in_, scale, None, A.mult)
+        return either(call, rd, wr, ind)
+
+    def affine(out, in_, a, b, rd, wr, ind=False):
+        def call(e):
+            if e == "s": return g.scalar.activation(out, in_, AF.Identity, bias=b, scale=a)
+            return g.vector.tensor_scalar(out, in_, a, b, A.mult, A.add)
+        return either(call, rd, wr, ind)
+
+    def shift(out, in_, x, rd, wr):
+        def call(e):
+            if e == "s": return g.scalar.activation(out, in_, AF.Identity, bias=x)
+            return g.vector.tensor_scalar(out, in_, x, None, A.add)
+        return either(call, rd, wr, False)
+
+    def quant(q, s, in_, n, rd, wr): return add(P, {"v": 12 + 0.22 * 4 * n * 1.2}, lambda e: g.vector.quantize_mx(q, s, in_), rd, wr)
+
+    def bank(b): return T.ps[:, 512 * b:512 * b + C]
+
+    def mm(b, w, ws, x, xs, rd):
+        return add(P, {"t": 1.4 * 0.83 * (C + 16)}, lambda e: g.tensor.matmul_mx(bank(b), w, ws, x, xs, True, True), rd, ["ps%d" % b])
+
+    def load(q, nm, out, in_):
+        return add(P, {q: 60.0}, lambda e: (g.sync if e == "y" else g.scalar).dma_start(out, in_), [], [nm], sem="ld_" + nm, lat=2300.0)
+
+    load("y", "fl", T.fli[:], T.fl[:, :])
+    load("y", "ml", T.mli[:], T.ml[:, :])
+    load("s", "x", T.xin[:], T.x[:, :])
+    load("y", "u", T.uin[:], T.u[:, :])
+    load("y", "wc", T.wq[:].bitcast(dt.uint8), T.wc[:, :])
+    load("y", "ws", T.wsc[:], T.ws[:, :])
+    load("y", "v", T.vin[:], T.v[:, :])
+
+    def iota(out, pat, base, cm, wr, n, fl):
+        def call(e): return g.iota(out, pat, base, cm, allow_small_or_imprecise_dtypes=True) if fl else g.iota(out, pat, base, cm)
+        return add(P, {"g": 130 + 2 * n * CY}, call, [], wr)
+    iota(T.pcol[:, 0:1], [[1, 1]], 0, 1, ["pcol"], 1, False)
+    iota(F("iof"), [[1, C]], 0, 0, ["iof"], C, True)
+    iota(T.jm[:], [[0, 40], [1, 16]], 0, 0, ["jm"], 2 * C, True)
+    iota(T.ui[:], [[16, 8]], 0, 0, ["ui"], 8, False)
+    ts(B("iob"), F("iof"), -float(MID), TINY, A.add, A.mult, ["iof"], ["iob"], C)
+    pc, pf = T.pcol, T.pcolf
+    for b in range(4):
+        ts(pc[:, b + 1:b + 2], pc[:, 0:1], b, 1, A.logical_shift_right, A.bitwise_and, ["pcol"], ["pb%d" % b])
+        ts(pf[:, b:b + 1], pc[:, b + 1:b + 2], 2.0 ** (STEPB << b) - 1, 1.0, A.mult, A.add, ["pb%d" % b], ["pf%d" % b])
+    tt(pf[:, 4:5], pf[:, 0:1], pf[:, 1:2], A.mult, ["pf0", "pf1"], ["pf4"])
+    ts(pf[:, 5:6], pf[:, 2:3], 2.0 ** (102 - 15 * STEPB), None, A.mult, None, ["pf2"], ["pf5"])
+    tt(pf[:, 6:7], pf[:, 3:4], pf[:, 5:6], A.mult, ["pf3", "pf5"], ["pf6"])
+    tt(pf[:, 7:8], pf[:, 4:5], pf[:, 6:7], A.mult, ["pf4", "pf6"], ["sc"])
+    SC = pf[:, 7:8]
+    ts(pc[:, 5:6], pc[:, 0:1], 15, None, A.bitwise_and, None, ["pcol"], ["p15"])
+    vcopy(pf[:, 8:9], pc[:, 5:6], ["p15"], ["p15f"])
+    ts(T.dcon[:], T.jm[:], pf[:, 8:9], 2.0 ** STEPB, A.is_gt, A.mult, ["jm", "p15f"], ["dcon"], 2 * C)
+    ts(F("lab"), F("iof"), UNIT * TINY, -(MID + 1) * TINY, A.mult, A.add, ["iof"], ["lab"], C)
+    ts(F("lab2"), F("iof"), UNIT * TINY, (UNIT - MID - 1) * TINY, A.mult, A.add, ["iof"], ["lab2"], C)
+    for h in range(2):
+        add(P, {"v": 300.0}, lambda e, h=h: g.vector.memset(F("gw%d" % h, 2 * C, 0, C + 8), 0.0), [], ["gw%d" % h])
+        add(P, {"v": 150.0}, lambda e, h=h: g.vector.memset(B("eb%d" % h, 2 * C, 0, C + 16), -MID * TINY), [], ["eb%d" % h])
+    add(P, {"v": 250.0}, lambda e: g.vector.memset(T.half[:], 0.5), [], ["half"])
+    for b in range(4):
+        add(P, {"g": 170 + 1024 * CY}, lambda e, b=b: g.affine_select(T.et[:, 512 * b:512 * b + 512], T.half[:], [[1, 512]], A.is_equal, 0.0, -b, -4),
+            ["half"], ["et%d" % b])
+        quant(T.eq[:, 128 * b:128 * b + 128], T.es[:, 128 * b:128 * b + 128], T.et[:, 512 * b:512 * b + 512], 128, ["et%d" % b], ["eq%d" % b])
+
+    quant(T.xq0[:], T.xs0[:], T.xin[:], C, ["x"], ["X0"])
+    vcopy(T.u16[:], T.ui[:], ["ui"], ["u16"])
+    quant(T.uq[:], T.us[:], T.uin[:], 128, ["u"], ["uq"])
+    add(P, {"v": 250.0}, lambda e: g.vector.tensor_copy(T.up[:].bitcast(dt.uint32), T.uq[:].bitcast(dt.uint32).indirect(T.u16[:])), ["uq", "u16"], ["up"])
+    add(P, {"v": 250.0}, lambda e: g.vector.tensor_copy(T.ups[:], T.us[:].indirect(T.u16[:])), ["uq", "u16"], ["ups"])
+    quant(T.vq[:], T.vs[:], T.vin[:], 128, ["v"], ["vq"])
+
+    def compact(out, nm, bias, rd, wr, w=1):
+        n = w * C
+        scan(B(nm + "k", n), T.dcon[:, 0:n], B(nm, n), 0.0, A.mult, A.add, rd + ["dcon"], [nm + "k"], n, True)
+        if out is not None: ts(out, B(nm + "k", n, 15, n, 16), SC, bias, A.mult, A.add, [nm + "k", "sc"], wr, 20 * w)
+
+    vcopy(tu("LG0", 40, 0, 20), T.fli[:], ["fl"], ["L0_0"])
+    vcopy(tu("M16"), T.mli[:], ["ml"], ["M16"])
+    scatter(B("gl0").indirect(tu("LG0", 40, 0, 20)), B("iob"), ["L0_0", "iob"], ["gl0"])
+    compact(tu("LG0", 40, 20, 40), "gl0", MID + 0.25, ["gl0"], ["GL_0"])
+    move(B("mr"), B("iob").indirect(tu("M16")), ["iob", "M16"], ["mr"], ind=True)
+    tt(F("sgd"), B("mr"), B("iob"), A.subtract, ["mr", "iob"], ["sgd"], C)
+    act(F("sg"), F("sgd"), AF.Sign, ["sgd"], ["sg"], scale=2.0 ** 97)
+
+    sent = [0]
+    peers = [T.cores[rank ^ m] for m in MASKS]
+    common = [e for e in topo.engines(core, peers[0]) if all(e in topo.engines(core, p) and e in topo.engines(p, core) for p in peers)]
+    for r in range(ROUNDS):
+        h = r % 2
+        R = lambda nm: "%s_%d" % (nm, h)
+        partner = T.cores[rank ^ MASKS[r]]
+        rid, pid, _s = topo.addr(partner)
+        msk, ne = sum(1 << e for e in common), len(common)
+        X, Xq, Xs = "X%d" % r, T["xq%d" % r], T["xs%d" % r]
+
+        def send(sem, pieces, rd, key, lat):
+            for dst, src in pieces:
+                last = add(P, {"g": 300.0}, lambda e, dst=dst, src=src, sem=sem, rid=rid, pid=pid, msk=msk: g.remote_dma(dst, src, T.sem[sem], T.sem.rl, pid, rid, msk),
+                           rd, ["net"], sem="rl", val=0)
+                sent[0] += ne
+            add(P, {"n": 0.0}, None, [], [key], sem=sem, val=ne * len(pieces), after=[last], lat=lat)
+
+        send("aq%d" % r, [(T["lq%d" % r][:].bitcast(dt.uint8), Xq[:].bitcast(dt.uint8)), (T["ls%d" % r][:], Xs[:])], [X], "Y%d" % r, 9000.0)
+
+        mm(0, T.up[:], T.ups[:], Xq[:], Xs[:], ["up", "ups", X])
+        move(F(R("s")), bank(0), ["ps0"], [R("s")])
+        for b in range(4):
+            mm(1 + b, T.eq[:, 128 * b:128 * b + 128], T.es[:, 128 * b:128 * b + 128], Xq[:], Xs[:], ["eq%d" % b, X])
+            move(T["fh%d" % h][:, C * b:C * b + C], bank(1 + b), ["ps%d" % (1 + b)], ["fh%d%d" % (h, b)])
+
+        LG, LN = "LG%d" % r, "LG%d" % (r + 1)
+        FL, GL, FN, GN = "L0_%d" % r, "GL_%d" % r, "L0_%d" % (r + 1), "GL_%d" % (r + 1)
+        fl_, gl_, fn_, gn_ = tu(LG, 40, 0, 20), tu(LG, 40, 20, 40), tu(LN, 40, 0, 20), tu(LN, 40, 20, 40)
+        L = [FL] + [R("L%d" % k) for k in range(1, 8)]
+        lists = [fl_] + [tu(k) for k in L[1:]]
+        move(B(R("fr0")), B("iob").indirect(fl_), ["iob", FL], [R("fr0")], ind=True)
+        for nm, x in (("key0", 0.0), ("w0", 1.0)):
+            affine(F(R(nm)), B("iob").indirect(fl_), UNIT, (UNIT * MID - MID + x) * TINY, ["iob", FL], [R(nm)], ind=True)
+        for k in range(9):
+            if k < 7:
+                nx = R("fr%d" % (k + 1))
+                move(B(nx), B(R("fr%d" % k)).indirect(lists[k]), [R("fr%d" % k), L[k]], [nx], ind=True)
+                compact(lists[k + 1], nx, MID + 0.25, [nx], [L[k + 1]])
+            q = k if k < 8 else 6
+            a, b = R("key%d" % (k % 2)), R("key%d" % ((k + 1) % 2))
+            w, wn = R("w%d" % (k % 2)), R("w%d" % ((k + 1) % 2))
+            tt(F(b), F(w).indirect(lists[q]), F(a), A.min, [w, L[q], a], [b], C, True)
+            if k < 8: shift(F(wn), F(b), (2.0 ** (k + 1) if k < 7 else 64.0) * TINY, [b], [wn])
+        key = R("key1")
+
+        act(B(R("kb")), F(key), AF.Identity, [key], [R("kb")], scale=1 / UNIT, bias=-MID * TINY)
+        RL = R("RL")
+        compact(tu(RL, 40, 0, 20), R("kb"), MID + 0.25, [R("kb")], [RL + "a"])
+        ts(tu(RL, 40, 20, 40), B(R("kb") + "k", C, 15, C, 16), SC, MID + 1.25, A.mult, A.add, [R("kb") + "k", "sc"], [RL + "b"])
+        tt(F(R("mx")), F(key), F("lab"), A.max, [key, "lab"], [R("mx")], C)
+        eb, be = "eb%d" % h, R("be")
+        scan(B(eb, 2 * C, 1, C + 1), F(R("mx")), F("lab"), -MID * TINY, A.add, A.subtract, [R("mx"), "lab"], [eb])
+        gw, prow = "gw%d" % h, R("prow")
+        scan(F(gw, 2 * C, 1, C + 1), F(R("mx")), F("lab2"), 0.0, A.add, A.subtract, [R("mx"), "lab2"], [gw])
+        tt(B(prow), F(gw, 2 * C, 0, C + 1).indirect(tu(RL, 40, 0, 20)), F(key), A.add, [gw, RL + "a", key], [prow], C, True)
+        compact(tu(R("P16")), prow, MID + 0.25, [prow], [R("P16")])
+        ts(ti(R("pos")), B(prow + "k", C, 15, C, 16), SC, float(MID), A.mult, A.add, [prow + "k", "sc"], [R("pos")])
+        it = R("it")
+        move(B(be, 2 * C, 0, C), B(eb, 2 * C, 0, C + 1).indirect(tu(RL, 40, 0, 20)), [eb, RL + "a"], [be + "b"], ind=True)
+        affine(B(be, 2 * C, C, 2 * C), B(eb, 2 * C, 0, C + 1).indirect(tu(RL, 40, 20, 40)), 1.0, -TINY, [eb, RL + "b"], [be + "e"], ind=True)
+        compact(ti(it, 80, 40, 80), be, float(MID), [be + "b", be + "e"], [it + "b"], 2)
+        tt(ti(it, 80, 20, 40), ti(R("pos")), ti(it, 80, 40, 60), A.subtract, [R("pos"), it + "b"], [it + "c"])
+        tt(ti(it, 80, 0, 20), ti(it, 80, 60, 80), ti(it, 80, 40, 60), A.subtract, [it + "b"], [it + "n"])
+        sa, sb, SA, O16 = T["sa%d" % r], T["sb%d" % r], "sa%d" % r, "sb%d" % r
+        vcopy(sa[:], ti(it, 80), [it + "n", it + "c", it + "b"], [SA], 80)
+        E16 = sa[:, 60:80]
+        send("aa%d" % r, [(T["la%d" % r][:], sa[:, 0:60])], [SA], "la%d" % r, 4500.0)
+        ts(tf(R("nf")), ti(it, 80, 0, 20), 1.0, None, A.add, None, [it + "n"], [R("nf")])
+        ol = R("ol")
+        scatter(B(ol).indirect(tu(R("P16"))), B("iob"), [R("P16"), "iob"], [ol])
+        compact(sb[:], ol, MID + 0.25, [ol], [O16])
+        send("ab%d" % r, [(T["lb%d" % r][:], sb[:])], [O16], "lb%d" % r, 4500.0)
+        act(B(R("flag")), B("iob").indirect(sa[:, 20:40]), AF.Relu, ["iob", SA], [R("flag")], scale=-2.0 ** 97, bias=(1.0 - MID) * TINY * 2.0 ** 97, ind=True)
+        act(B(R("d0")), B(R("flag")).indirect(sb[:]), AF.Copy, [R("flag"), O16], [R("d0")], scale=-2.0 ** 97, ind=True)
+        move(B(R("d1")), B(R("d0")), [R("d0")], [R("d1")], scale=-1.0)
+        fg = R("fg")
+        move(B(fg, 2 * C, 0, C), B(R("fr0")).indirect(tu("M16")), [R("fr0"), "M16"], [fg + "f"], ind=True)
+        move(B(fg, 2 * C, C, 2 * C), B("mr").indirect(gl_), ["mr", GL], [fg + "g"], ind=True)
+        compact(tf(R("fgv"), 40), fg, MID + 0.25, [fg + "f", fg + "g"], [R("fgv")], 2)
+        ts(tf(R("fg0"), 40), tu(LG, 40), 0.25, None, A.add, None, [FL, GL], [R("fg0")], 40)
+        tt(tf(R("fgd"), 40), tf(R("fgv"), 40), tf(R("fg0"), 40), A.subtract, [R("fgv"), R("fg0")], [R("fgd")], 40)
+        ts(tf(R("fgs"), 40), tf(R("fgd"), 40), SC, None, A.mult, None, [R("fgd"), "sc"], [R("fgs")], 40)
+
+        move(F(R("so")), F(R("s")).indirect(sb[:]), [R("s"), O16], [R("so")], ind=True)
+        scan(F(R("pm")), B(R("d0")), F(R("so")), -2.0 ** 92, A.add, A.max, [R("d0"), R("so")], [R("pm")])
+        tt(F(R("eq")), F(R("pm")).indirect(E16), F(R("s")), A.subtract, [R("pm"), SA, R("s")], [R("eq")], C, True)
+        tt(B(R("cd")), F(R("eq")).indirect(sb[:]), B(ol), A.add, [R("eq"), O16, ol], [R("cd")], C, True)
+        scan(B(R("cs")), B(R("d1")), B(R("cd")), 0.0, A.add, A.min, [R("d1"), R("cd")], [R("cs")], C, True)
+        move(B(R("gk")), B(R("cs")).indirect(E16), [R("cs"), SA], [R("gk")], ind=True)
+        l16 = R("l16")
+        compact(tu(l16), R("gk"), MID + 0.25, [R("gk")], [l16])
+
+        xa = R("xa")
+        for q in range(3):
+            move(B(xa, 3 * C, C * q, C * q + C), B("iob").indirect(T["la%d" % r][:, 20 * q:20 * q + 20]), ["iob", "la%d" % r], [xa + str(q)], ind=True)
+        move(B(R("oe")), B("iob").indirect(T["lb%d" % r][:]), ["iob", "lb%d" % r], [R("oe")], ind=True)
+        move(B(R("xn")), B(xa, 3 * C, 0, C).indirect(tu(l16)), [xa + "0", l16], [R("xn")], ind=True)
+        compact(ti(R("xni")), R("xn"), MID + 1.0, [R("xn")], [R("xni")])
+        xd = R("xd")
+        for q in (1, 2): move(B(xd, 2 * C, C * q - C, C * q), B(xa, 3 * C, C * q, C * q + C).indirect(tu(l16)), [xa + str(q), l16], [xd + str(q)], ind=True)
+        compact(None, xd, 0.0, [xd + "1", xd + "2"], None, 2)
+        ts(tf(R("xb")), B(xd + "k", 2 * C, C + 15, 2 * C, 16), SC, float(MID), A.mult, A.add, [xd + "k", "sc"], [R("xb")])
+        move(B(R("xp")), B(R("prow")).indirect(tu(l16)), [R("prow"), l16], [R("xp")], ind=True)
+        compact(None, R("xp"), 0.0, [R("xp")], None)
+        tt(tf(R("dl")), B(R("xp") + "k", C, 15, C, 16), B(prow + "k", C, 15, C, 16), A.subtract, [R("xp") + "k", prow + "k"], [R("dl")])
+        ts(tf(R("ng")), tf(R("dl")), SC, -0.5, A.mult, A.is_lt, [R("dl"), "sc"], [R("ng")])
+        tt(tf(R("nn")), tf(R("ng")), tf(R("nf")), A.mult, [R("ng"), R("nf")], [R("nn")])
+        vcopy(tf(R("ne")), ti(R("xni")), [R("xni")], [R("ne")])
+        add(P, {"v": 300.0}, lambda e, a=R("rn"), b=R("ne"): g.vector.reciprocal(tf(a), tf(b)), [R("ne")], [R("rn")])
+        tt(tf(R("zr")), B(xd + "k", 2 * C, 15, C, 16), tf(R("dl")), A.subtract, [xd + "k", R("dl")], [R("zr")])
+        ts(tf(R("z0")), tf(R("zr")), SC, MID + 0.5, A.mult, A.add, [R("zr"), "sc"], [R("z0")])
+        tt(tf(R("zh")), tf(R("z0")), tf(R("nn")), A.subtract, [R("z0"), R("nn")], [R("zh")])
+        tt(tf(R("tq")), tf(R("zh")), tf(R("rn")), A.mult, [R("zh"), R("rn")], [R("tq")])
+        ts(ti(R("qi")), tf(R("tq")), -0.5, None, A.add, None, [R("tq")], [R("qi")])
+        tt(tf(R("zb")), tf(R("zh")), tf(R("xb")), A.add, [R("zh"), R("xb")], [R("zb")])
+        tt(tf(R("m1")), ti(R("qi")), tf(R("ne")), A.mult, [R("qi"), R("ne")], [R("m1")])
+        tt(tf(R("pp")), tf(R("zb")), tf(R("m1")), A.subtract, [R("zb"), R("m1")], [R("pp")])
+        ts(tu(R("PL")), tf(R("pp")), -0.25, None, A.add, None, [R("pp")], [R("PL")])
+        move(B(R("tr")), B(R("oe")).indirect(tu(R("PL"))), [R("oe"), R("PL")], [R("tr")], ind=True)
+        T16 = R("T16")
+        compact(tu(T16), R("tr"), MID + 0.25, [R("tr")], [T16])
+
+        tt(F(R("st")), F(R("s")).indirect(tu(T16)), F("sg"), A.mult, [R("s"), T16, "sg"], [R("st")], C, True)
+        for c in range(2):
+            a, b = C // 2 * c, C // 2 * c + C // 2
+            either(lambda e, o=F(R("su"), C, a, b), i=F(R("st"), C, a, b): g.vector.tensor_copy(o, i) if e == "v" else g.scalar.activation(o, i, AF.Copy),
+                   [R("st")], [R("su") + "ab"[c]], False, C // 2)
+        tt(F(R("sv")), F(R("st")).indirect(tu("M16")), F(R("su")), A.add, [R("st"), R("su") + "a", R("su") + "b", "M16"], [R("sv")], C, True)
+        ts(B(R("sw")), F(R("sv")), 0.0, TINY, A.is_lt, A.mult, [R("sv")], [R("sw")], C)
+        move(B(R("swg")), B(R("sw")).indirect(gl_), [R("sw"), GL], [R("swg")], ind=True)
+        for nm, a, out, kk in (("sw", 0, fn_, FN), ("swg", 20, gn_, GN)):
+            compact(None, R(nm), 0.0, [R(nm)], None)
+            tt(tf(R(nm + "x")), B(R(nm) + "k", C, 15, C, 16), tf(R("fgs"), 40, a, a + 20), A.mult, [R(nm) + "k", R("fgs")], [R(nm + "x")])
+            tt(tf(R(nm + "y")), tf(R(nm + "x")), tf(R("fg0"), 40, a, a + 20), A.add, [R(nm + "x"), R("fg0")], [R(nm + "y")])
+            vcopy(out, tf(R(nm + "y")), [R(nm + "y")], [kk])
+
+        fh, fs, gp, zt, xt, rs = [T["%s%d" % (k, h)] for k in ("fh", "fs", "gp", "zt", "xt", "rs")]
+        for b in range(4):
+            bk, c = (5, 6, 7, 0)[b], slice(C * b, C * b + C)
+            mm(bk, T.eq[:, 128 * b:128 * b + 128], T.es[:, 128 * b:128 * b + 128], T["lq%d" % r][:], T["ls%d" % r][:], ["eq%d" % b, "Y%d" % r])
+            move(fs[:, c], bank(bk), ["ps%d" % bk], ["fs%d%d" % (h, b)])
+            move(gp[:, c], fs[:, c].indirect(tu(T16)), ["fs%d%d" % (h, b), T16], ["gp%d%d" % (h, b)], ind=True)
+            tt(zt[:, b:4 * C:4], fh[:, c].indirect(fn_), gp[:, c], A.add, ["fh%d%d" % (h, b), FN, "gp%d%d" % (h, b)], ["zt%d%d" % (h, b)], C, True)
+        zq, zs = T["zq%d" % h], T["zs%d" % h]
+        quant(zq[:], zs[:], zt[:], C, ["zt%d%d" % (h, b) for b in range(4)], ["zq%d" % h])
+        for b in range(4):
+            c = slice(C * b, C * b + C)
+            mm(1 + b, T.wq[:, 128 * b:128 * b + 128], T.wsc[:, 128 * b:128 * b + 128], zq[:], zs[:], ["wc", "ws", "zq%d" % h])
+            move(rs[:, c], bank(1 + b), ["ps%d" % (1 + b)], ["rs%d%d" % (h, b)], scale=2.0 ** -6)
+            tt(xt[:, b:4 * C:4], rs[:, c].indirect(gn_), fh[:, c], A.add, ["rs%d%d" % (h, b), GN, "fh%d%d" % (h, b)], ["xt%d%d" % (h, b)], C, True)
+        quant(T["xq%d" % (r + 1)][:], T["xs%d" % (r + 1)][:], xt[:], C, ["xt%d%d" % (h, b) for b in range(4)], ["X%d" % (r + 1)])
+
+    q, s, X = T["xq%d" % ROUNDS], T["xs%d" % ROUNDS], "X%d" % ROUNDS
+
+    def store(nm, out, in_, rd): add(P, {"y": 60.0}, lambda e: g.sync.dma_start(out, in_), rd, [], sem="st_" + nm, lat=2000.0)
+    act(T.nls[:], F("iof").indirect(tu("LG%d" % ROUNDS, 40, 0, 20)), AF.Copy, ["iof", "L0_%d" % ROUNDS], ["nls"], ind=True)
+    store("nl", T.nl[:, :], T.nls[0:128:16, :], ["nls"])
+    mm(1, T.vq[:], T.vs[:], q[:], s[:], ["vq", X])
+    move(T.ys[:], bank(1), ["ps1"], ["ys"])
+    store("oc", T.oc[:, :], q[:].bitcast(dt.uint8), [X])
+    for k in range(4): store("os%d" % k, T.osc[4 * k:4 * k + 4, :], s[32 * k:32 * k + 4, :], [X])
+    store("y", T.y[:, :], T.ys[:], ["ys"])
+
+    seq, done = order(P)
+    count = emit(P, g, T, seq)
+    for nm in STORES: g.sync.wait_ge(T.sem["st_" + nm], 16)
+    g.wait_ge(T.sem.rl, sent[0])
+    for e, nm in (("v", "ev"), ("s", "es"), ("t", "et"), ("g", "eg")): g.sync.wait_ge(T.sem[nm], count[e])

@@ -6,9 +6,11 @@ MASKS = (1, 2, 4)
 MID = 160
 TINY = 2.0 ** -102
 STEPB = 12
-UNIT = 2048.0
+UNIT = 1024.0
+RISE = 512 * UNIT
+WHOLE = 1.5 * 2.0 ** 23
 
-NF, NB, NT, NI, NU = 34, 118, 54, 18, 36
+NF, NB, NT, NI, NU = 36, 126, 90, 18, 36
 SCRATCH = {
     "rowf": ("sbuf", [128, C * NF], "float32"),
     "rowb": ("sbuf", [128, C * NB], "bfloat16"),
@@ -20,7 +22,7 @@ SCRATCH = {
     "jm": ("sbuf", [128, 2 * C], "float32"),
     "dcon": ("sbuf", [128, 2 * C], "bfloat16"),
     "pcol": ("sbuf", [128, 8], "int32"),
-    "pcolf": ("sbuf", [128, 16], "float32"),
+    "pcolf": ("sbuf", [128, 32], "float32"),
     "ui": ("sbuf", [128, 8], "int32"),
     "u16": ("sbuf", [128, 8], "uint16"),
     "half": ("sbuf", [128, 512], "bfloat16"),
@@ -63,10 +65,10 @@ STORES = ("oc", "os0", "os1", "os2", "os3", "y", "nl")
 SEMAPHORES = ["ev", "es", "et", "eg", "rl"] + ["ld_" + n for n in LOADS] + ["st_" + n for n in STORES] \
     + ["%s%d" % (k, r) for k in ("aq", "aa", "ab") for r in range(ROUNDS)]
 
-CY, GA, WAKE = 0.83 * 1.2, 1.5, 130.0
-VB, LOOK, PW = 500.0, 150.0, 5.0
-OFFS = "imdgjjbagglflfmjmjmjfhfbjgaggadgcabadamlfgfliaaefgcgfafhhmmgbhdgalbjdeadbmabldmfkmchgagjcmfmlajmamkmafmigcmdlihghblhcckekacmgeehjbiaahifjabajfgdagjmigacmiaakjmgfhjhjlihgcaagaaajbklmmifjadkelmgdgaagflhcimfajflmfmjedhdfgaimfmmhelghmjkhkmgemfkfgejeblmlkmfjhljlmmdmaaimfeigeccjmdlblcgjkbkhikhfgfafjbggfekaddhaamfgfegllajgaamgbmlfihiiaihgjklgmjhhhghgigaaaigajlckmakmammbadbgjkmkcliejmkcmeccbjaedjkkhffmjggcmjhadmikglamgkaahmfgmfbgaimaagjfkmmddafjgaecajbflhjelammlcmdeafjmlkjmhejdhbjikaddfajkgiiafdaadfbgfggflegkjeelmfgefeeffmccdbhbegkdbagmgekechddajdfmmahfmaddllhggblmmgegmamlecmhmehgljm"
-FLEX = "----------------------------------------------------------------s-v---sv-----s---ss---------s---ss----s---s-s------------ss---------------sss--------------s--s--v------------------------s--s----------s---s--------------s--------------s---s-s---s---ss---ss----s---s----------------s-------------s---------------s------------v-----sv--s---v-------------------vs------------s---ss--ss--s-------v--s--s------s---s---sssss---ss---s-----s---s----ss---ss-----s------------------------------s------v-------s-vsv---v--s-------------------v-------------s---s----s--ss------s--s--s------------"
+CY, GA, SA_, WAKE = 0.83 * 1.25, 1.56, 3.8, 130.0
+SPARE, REACH, SLACK, SEED = 300.0, 1500.0, 200.0, 1
+PASSES = 9000
+PLAN = {}
 
 
 def add(P, cost, call, reads, writes, sem=None, val=16, after=(), lat=0.0):
@@ -81,56 +83,77 @@ def add(P, cost, call, reads, writes, sem=None, val=16, after=(), lat=0.0):
     for k in writes:
         P["last"][k] = i
         P["readers"][k] = []
-    P["ops"].append({"c": cost, "f": call, "d": sorted(deps), "sem": sem, "val": val, "lat": lat})
+    P["ops"].append({"c": cost, "f": call, "d": sorted(deps), "sem": sem, "val": val, "lat": lat, "w": writes})
     return i
 
 
+def lay(ops, pre, key, side, back):
+    n = len(ops)
+    st, en, on = [0.0] * n, [None] * n, [None] * n
+    begin, end = {e: [] for e in "vstgyn"}, {e: [] for e in "vstgyn"}
+    for first in sorted(range(n), key=lambda i: key[i]):
+        todo = [first]
+        while todo:
+            i = todo[-1]
+            if en[i] is not None:
+                todo.pop()
+                continue
+            t = 0.0
+            for j in pre[i]:
+                x = en[j]
+                if x is None: todo.append(j)
+                elif x + WAKE > t: t = x + WAKE
+            if todo[-1] != i: continue
+            o, best = ops[i], None
+            if back: t += o["lat"]
+            for e in side[i]:
+                c, s, f, a = o["c"][e], begin[e], end[e], t
+                k = len(f)
+                while k and f[k - 1] > t: k -= 1
+                while k < len(s) and s[k] < a + c - 1e-6:
+                    a = f[k]
+                    k += 1
+                x = a + c + (SPARE if e == "v" else 0.0)
+                if best is None or x < best[0]: best = (x, a, c, e, k)
+            x, a, c, e, k = best
+            if c:
+                begin[e].insert(k, a)
+                end[e].insert(k, a + c)
+            st[i], en[i], on[i] = a, a + c + (0.0 if back else o["lat"]), e
+    return st, en, on
+
+
 def order(P):
+    if "seq" in PLAN: return PLAN["seq"], PLAN["done"]
     ops = P["ops"]
     n = len(ops)
-    succ = [[] for _ in range(n)]
+    pre, succ = [o["d"] for o in ops], [[] for _ in range(n)]
     for i in range(n):
-        for j in ops[i]["d"]: succ[j].append(i)
+        for j in pre[i]: succ[j].append(i)
+
+    def twice(key, side):
+        en = lay(ops, pre, key, side, False)[1]
+        en = lay(ops, succ, [-x for x in en], side, True)[1]
+        return lay(ops, pre, [-x for x in en], side, False)
     way = [0.0] * n
     for i in range(n - 1, -1, -1):
-        best = 0.0
-        for s in succ[i]: best = max(best, way[s] + WAKE)
-        way[i] = best + min(ops[i]["c"].values()) + ops[i]["lat"]
-    way = [x + 500.0 * (ord(OFFS[i]) - 103) if i < len(OFFS) else x for i, x in enumerate(way)]
-    free = {"v": 0.0, "s": 0.0, "t": 0.0, "g": 0.0, "y": 0.0}
-    done, seq = [0.0] * n, []
-    left = [len(o["d"]) for o in ops]
-    at = {}
-
-    def open_(i):
-        at[i] = max([done[j] + WAKE for j in ops[i]["d"]], default=0.0)
-    for i in range(n):
-        if left[i] == 0: open_(i)
-    while at:
-        cand = []
-        for i, t in at.items():
-            c = ops[i]["c"]
-            if len(c) == 1:
-                e = next(iter(c))
-            elif i < len(FLEX) and FLEX[i] != "-":
-                e = FLEX[i]
-            else:
-                tv = max(t, free["v"])
-                busy = any(len(ops[j]["c"]) == 1 and "v" in ops[j]["c"] and u <= tv + c["v"] for j, u in at.items())
-                e = "s" if max(t, free["s"]) + c["s"] <= tv + c["v"] + (VB if busy else 0.0) else "v"
-            cand.append((t if e == "n" else max(t, free[e]), i, e))
-        t0 = min(x[0] for x in cand)
-        eng = max((x for x in cand if x[0] <= t0), key=lambda x: way[x[1]])[2]
-        st, i, e = max((x for x in cand if x[2] == eng and x[0] <= t0 + LOOK), key=lambda x: way[x[1]] - PW * (x[0] - t0))
-        del at[i]
-        c = ops[i]["c"][e]
-        if e != "n": free[e] = st + c
-        done[i] = st + c + ops[i]["lat"]
-        seq.append((st, i, e))
-        for s in succ[i]:
-            left[s] -= 1
-            if left[s] == 0: open_(s)
-    return seq, done
+        way[i] = min([way[s] - WAKE for s in succ[i]], default=0.0) - min(ops[i]["c"].values()) - ops[i]["lat"]
+    both = [i for i in range(n) if len(ops[i]["c"]) > 1]
+    best = now = twice(way, ["".join(o["c"]) for o in ops])
+    x = SEED
+    for p in range(PASSES):
+        key, side = list(now[0]), list(now[2])
+        for _ in range(2):
+            x = (x * 6364136223846793005 + 1442695040888963407) % 2 ** 64
+            if (x >> 60) < 6:
+                i = both[(x >> 20) % len(both)]
+                side[i] = "s" if side[i] == "v" else "v"
+            else: key[(x >> 20) % n] += REACH * ((x >> 45) % 1024 / 512 - 1)
+        new = twice(key, side)
+        if max(new[1]) <= max(now[1]) + SLACK * (1 - p / PASSES) * ((x >> 8) % 1024 / 1024) ** 2: now = new
+        if max(now[1]) < max(best[1]): best = now
+    PLAN["seq"], PLAN["done"] = sorted((best[0][i], i, best[2][i]) for i in range(n)), best[1]
+    return PLAN["seq"], PLAN["done"]
 
 
 def emit(P, g, T, seq):
@@ -190,35 +213,41 @@ def rank_program(g, core, T, topo):
 
     def F(nm, w=C, a=0, b=None, s=None): return view("rowf", C, nm, w, a, b, s)
     def B(nm, w=C, a=0, b=None, s=None): return view("rowb", C, nm, w, a, b, s)
-    def tf(nm, w=20, a=0, b=None): return view("tabf", 20, nm, w, a, b, None)
+    def tf(nm, w=20, a=0, b=None, s=None): return view("tabf", 20, nm, w, a, b, s)
     def ti(nm, w=20, a=0, b=None): return view("tabi", 20, nm, w, a, b, None)
     def tu(nm, w=20, a=0, b=None): return view("tabu", 20, nm, w, a, b, None)
 
+    def vec(n): return max(64.0, n) * CY
+    def gat(e, n): return (50.0 if e == "v" else 65.0) + n * CY * GA
+
     def ts(out, in0, s1, s2, op0, op1, rd, wr, n=20):
         def call(e): return g.vector.tensor_scalar(out, in0, s1, None, op0) if op1 is None else g.vector.tensor_scalar(out, in0, s1, s2, op0, op1)
-        return add(P, {"v": max(60.0, n * CY)}, call, rd, wr)
+        return add(P, {"v": vec(n)}, call, rd, wr)
 
     def tt(out, a, b, op, rd, wr, n=20, ind=False):
-        return add(P, {"v": 55 + n * CY * GA if ind else max(60.0, 2 * n * CY)}, lambda e: g.vector.tensor_tensor(out, a, b, op), rd, wr)
+        return add(P, {"v": gat("v", n) if ind else vec(2 * n)}, lambda e: g.vector.tensor_tensor(out, a, b, op), rd, wr)
 
     def scan(out, d0, d1, init, op0, op1, rd, wr, n=C, half=False):
-        return add(P, {"v": n * CY * (0.5 if half else 1.0)}, lambda e: g.vector.tensor_tensor_scan(out, d0, d1, init, op0, op1), rd, wr)
+        return add(P, {"v": vec(n / 2 if half else n)}, lambda e: g.vector.tensor_tensor_scan(out, d0, d1, init, op0, op1), rd, wr)
 
-    def vcopy(out, in_, rd, wr, n=20): return add(P, {"v": max(60.0, n * CY)}, lambda e: g.vector.tensor_copy(out, in_), rd, wr)
+    def vcopy(out, in_, rd, wr, n=20): return add(P, {"v": vec(n)}, lambda e: g.vector.tensor_copy(out, in_), rd, wr)
 
-    def scatter(out, in_, rd, wr): return add(P, {"v": 1300.0}, lambda e: g.vector.tensor_copy(out, in_), rd, wr)
+    def fill(out, x, wr, n=20): return add(P, {"v": vec(n)}, lambda e: g.vector.memset(out, x), [], wr)
+
+    def scatter(out, in_, rd, wr): return add(P, {"v": 50 + C * CY * SA_}, lambda e: g.vector.tensor_copy(out, in_), rd, wr)
 
     def act(out, in_, func, rd, wr, scale=1.0, bias=None, ind=False):
         def call(e): return g.scalar.activation(out, in_, func, scale=scale) if bias is None else g.scalar.activation(out, in_, func, bias=bias, scale=scale)
-        return add(P, {"s": 68 + C * CY * GA if ind else C * CY}, call, rd, wr)
+        return add(P, {"s": gat("s", C) if ind else C * CY}, call, rd, wr)
 
-    def either(call, rd, wr, ind, n=C): return add(P, {"v": 55 + n * CY * GA, "s": 68 + n * CY * GA} if ind else {"v": n * CY, "s": n * CY}, call, rd, wr)
+    def either(call, rd, wr, ind, n=C, half=False):
+        return add(P, {"v": gat("v", n), "s": gat("s", n)} if ind else {"v": vec(n / 2 if half else n), "s": n * CY}, call, rd, wr)
 
-    def move(out, in_, rd, wr, ind=False, scale=None):
+    def move(out, in_, rd, wr, ind=False, scale=None, n=C, half=False):
         def call(e):
             if e == "s": return g.scalar.activation(out, in_, AF.Copy) if scale is None else g.scalar.activation(out, in_, AF.Copy, scale=scale)
             return g.vector.tensor_copy(out, in_) if scale is None else g.vector.tensor_scalar(out, in_, scale, None, A.mult)
-        return either(call, rd, wr, ind)
+        return either(call, rd, wr, ind, n, half)
 
     def affine(out, in_, a, b, rd, wr, ind=False):
         def call(e):
@@ -232,7 +261,7 @@ def rank_program(g, core, T, topo):
             return g.vector.tensor_scalar(out, in_, x, None, A.add)
         return either(call, rd, wr, False)
 
-    def quant(q, s, in_, n, rd, wr): return add(P, {"v": 12 + 0.22 * 4 * n * 1.2}, lambda e: g.vector.quantize_mx(q, s, in_), rd, wr)
+    def quant(q, s, in_, n, rd, wr): return add(P, {"v": (12 + 0.22 * 4 * n) * CY / 0.83}, lambda e: g.vector.quantize_mx(q, s, in_), rd, wr)
 
     def bank(b): return T.ps[:, 512 * b:512 * b + C]
 
@@ -258,24 +287,45 @@ def rank_program(g, core, T, topo):
     iota(T.jm[:], [[0, 40], [1, 16]], 0, 0, ["jm"], 2 * C, True)
     iota(T.ui[:], [[16, 8]], 0, 0, ["ui"], 8, False)
     ts(B("iob"), F("iof"), -float(MID), TINY, A.add, A.mult, ["iof"], ["iob"], C)
-    pc, pf = T.pcol, T.pcolf
+    pc = T.pcol
+
+    def col(k): return T.pcolf[:, k:k + 1]
     for b in range(4):
         ts(pc[:, b + 1:b + 2], pc[:, 0:1], b, 1, A.logical_shift_right, A.bitwise_and, ["pcol"], ["pb%d" % b])
-        ts(pf[:, b:b + 1], pc[:, b + 1:b + 2], 2.0 ** (STEPB << b) - 1, 1.0, A.mult, A.add, ["pb%d" % b], ["pf%d" % b])
-    tt(pf[:, 4:5], pf[:, 0:1], pf[:, 1:2], A.mult, ["pf0", "pf1"], ["pf4"])
-    ts(pf[:, 5:6], pf[:, 2:3], 2.0 ** (102 - 15 * STEPB), None, A.mult, None, ["pf2"], ["pf5"])
-    tt(pf[:, 6:7], pf[:, 3:4], pf[:, 5:6], A.mult, ["pf3", "pf5"], ["pf6"])
-    tt(pf[:, 7:8], pf[:, 4:5], pf[:, 6:7], A.mult, ["pf4", "pf6"], ["sc"])
-    SC = pf[:, 7:8]
+        ts(col(b), pc[:, b + 1:b + 2], 2.0 ** (STEPB << b) - 1, 1.0, A.mult, A.add, ["pb%d" % b], ["pf%d" % b])
+    tt(col(4), col(0), col(1), A.mult, ["pf0", "pf1"], ["pf4"])
+    ts(col(5), col(2), 2.0 ** (102 - 15 * STEPB), None, A.mult, None, ["pf2"], ["pf5"])
+    tt(col(6), col(3), col(5), A.mult, ["pf3", "pf5"], ["pf6"])
+    tt(col(7), col(4), col(6), A.mult, ["pf4", "pf6"], ["sc"])
+    SC, PLACE, ISC, ROOT, BIG, LOW, KSW = col(7), col(8), col(9), col(10), col(11), col(12), col(13)
+    add(P, {"v": 200.0}, lambda e: g.vector.reciprocal(ISC, SC), ["sc"], ["isc"])
     ts(pc[:, 5:6], pc[:, 0:1], 15, None, A.bitwise_and, None, ["pcol"], ["p15"])
-    vcopy(pf[:, 8:9], pc[:, 5:6], ["p15"], ["p15f"])
-    ts(T.dcon[:], T.jm[:], pf[:, 8:9], 2.0 ** STEPB, A.is_gt, A.mult, ["jm", "p15f"], ["dcon"], 2 * C)
-    ts(F("lab"), F("iof"), UNIT * TINY, -(MID + 1) * TINY, A.mult, A.add, ["iof"], ["lab"], C)
-    ts(F("lab2"), F("iof"), UNIT * TINY, (UNIT - MID - 1) * TINY, A.mult, A.add, ["iof"], ["lab2"], C)
-    for h in range(2):
-        add(P, {"v": 300.0}, lambda e, h=h: g.vector.memset(F("gw%d" % h, 2 * C, 0, C + 8), 0.0), [], ["gw%d" % h])
-        add(P, {"v": 150.0}, lambda e, h=h: g.vector.memset(B("eb%d" % h, 2 * C, 0, C + 16), -MID * TINY), [], ["eb%d" % h])
-    add(P, {"v": 250.0}, lambda e: g.vector.memset(T.half[:], 0.5), [], ["half"])
+    vcopy(PLACE, pc[:, 5:6], ["p15"], ["p15f"])
+    ts(ROOT, PLACE, RISE / UNIT, 0.25 - 15 * RISE / UNIT, A.mult, A.add, ["p15f"], ["root"])
+    ts(LOW, PLACE, RISE, MID - 15 * RISE, A.mult, A.add, ["p15f"], ["low"])
+    ts(KSW, PLACE, 2.0, -30.0, A.mult, A.add, ["p15f"], ["ksw"])
+    fill(col(14), 2.0 ** 51, ["b51"])
+    ts(BIG, col(14), 2.0 ** 51, None, A.mult, None, ["b51"], ["big"])
+    ts(T.dcon[:], T.jm[:], PLACE, 2.0 ** STEPB, A.is_gt, A.mult, ["jm", "p15f"], ["dcon"], 2 * C)
+    affine(B("dkey"), T.dcon[:, 0:C], 33 * RISE * TINY / 2 ** STEPB, -32 * RISE * TINY, ["dcon"], ["dkey"])
+    affine(B("dsw"), T.dcon[:, 0:C], 66.0 / 2 ** STEPB, -64.0, ["dcon"], ["dsw"])
+    affine(F("lab"), F("iof"), UNIT * TINY, -(MID + 1) * TINY, ["iof"], ["lab"])
+    affine(F("lab2"), F("iof"), UNIT * TINY, (UNIT - MID - 1) * TINY, ["iof"], ["lab2"])
+    fill(F("gw", 2 * C, 0, 8), 0.0, ["gw"])
+    for nm in ("swk", "swgk"): fill(B(nm, 3 * C), 0.0, [nm], 3 * C / 2)
+    fill(tf("fd", 120), 0.0, ["fd1", "fd2"], 120)
+    def ua(k): return tf("ua", 160, k, 160, 8)
+    def ub(k): return tf("ub", 160, k, 160, 8)
+    def va(k): return tf("va", 100, k, 100, 5)
+    def vb(k): return tf("vb", 100, k, 100, 5)
+    fill(tf("ua", 160), 1.0, ["ua", "ua4"], 160)
+    ts(ua(1), ua(0), SC, -1 / 1024, A.mult, A.mult, ["ua", "sc"], ["ua1"])
+    ts(ua(6), ua(0), SC, None, A.mult, None, ["ua", "sc"], ["ua6"])
+    fill(ua(0), 0.0, ["ua"])
+    for k, x in ((1, 0.5 / 1024 - 0.5), (2, WHOLE), (3, -WHOLE), (6, WHOLE + MID), (7, -WHOLE)): fill(ub(k), x, ["ub%d" % k])
+    for k, x in ((0, 0.0), (2, 1.0), (3, -1.0)): fill(va(k), x, ["va%d" % k])
+    for k, x in ((1, -0.5), (2, WHOLE), (3, WHOLE)): fill(vb(k), x, ["vb%d" % k])
+    fill(T.half[:], 0.5, ["half"], 256)
     for b in range(4):
         add(P, {"g": 170 + 1024 * CY}, lambda e, b=b: g.affine_select(T.et[:, 512 * b:512 * b + 512], T.half[:], [[1, 512]], A.is_equal, 0.0, -b, -4),
             ["half"], ["et%d" % b])
@@ -284,9 +334,11 @@ def rank_program(g, core, T, topo):
     quant(T.xq0[:], T.xs0[:], T.xin[:], C, ["x"], ["X0"])
     vcopy(T.u16[:], T.ui[:], ["ui"], ["u16"])
     quant(T.uq[:], T.us[:], T.uin[:], 128, ["u"], ["uq"])
-    add(P, {"v": 250.0}, lambda e: g.vector.tensor_copy(T.up[:].bitcast(dt.uint32), T.uq[:].bitcast(dt.uint32).indirect(T.u16[:])), ["uq", "u16"], ["up"])
-    add(P, {"v": 250.0}, lambda e: g.vector.tensor_copy(T.ups[:], T.us[:].indirect(T.u16[:])), ["uq", "u16"], ["ups"])
+    add(P, {"v": gat("v", 128)}, lambda e: g.vector.tensor_copy(T.up[:].bitcast(dt.uint32), T.uq[:].bitcast(dt.uint32).indirect(T.u16[:])), ["uq", "u16"], ["up"])
+    move(T.ups[:], T.us[:].indirect(T.u16[:]), ["uq", "u16"], ["ups"], ind=True, n=128)
     quant(T.vq[:], T.vs[:], T.vin[:], 128, ["v"], ["vq"])
+
+    def kept(nm, w=1, q=0): return B(nm + "k", w * C, q * C + 15, q * C + C, 16)
 
     def compact(out, nm, bias, rd, wr, w=1):
         n = w * C
@@ -332,111 +384,107 @@ def rank_program(g, core, T, topo):
         fl_, gl_, fn_, gn_ = tu(LG, 40, 0, 20), tu(LG, 40, 20, 40), tu(LN, 40, 0, 20), tu(LN, 40, 20, 40)
         L = [FL] + [R("L%d" % k) for k in range(1, 8)]
         lists = [fl_] + [tu(k) for k in L[1:]]
-        move(B(R("fr0")), B("iob").indirect(fl_), ["iob", FL], [R("fr0")], ind=True)
-        for nm, x in (("key0", 0.0), ("w0", 1.0)):
-            affine(F(R(nm)), B("iob").indirect(fl_), UNIT, (UNIT * MID - MID + x) * TINY, ["iob", FL], [R(nm)], ind=True)
-        for k in range(9):
+        first, ahead = R("first"), 64 - MID
+        affine(F(first), B("iob").indirect(fl_), UNIT, (UNIT * MID + ahead) * TINY, ["iob", FL], [first], ind=True)
+
+        def image(out, lst, rd, wr): affine(out, F(first).indirect(lst), 1 / UNIT, (-MID - ahead / UNIT) * TINY, [first] + rd, wr, ind=True)
+        key = first
+        for k in range(8):
             if k < 7:
                 nx = R("fr%d" % (k + 1))
-                move(B(nx), B(R("fr%d" % k)).indirect(lists[k]), [R("fr%d" % k), L[k]], [nx], ind=True)
+                if k: move(B(nx), B(R("fr%d" % k)).indirect(lists[k]), [R("fr%d" % k), L[k]], [nx], ind=True)
+                else: image(B(nx), fl_, [FL], [nx])
                 compact(lists[k + 1], nx, MID + 0.25, [nx], [L[k + 1]])
-            q = k if k < 8 else 6
-            a, b = R("key%d" % (k % 2)), R("key%d" % ((k + 1) % 2))
-            w, wn = R("w%d" % (k % 2)), R("w%d" % ((k + 1) % 2))
-            tt(F(b), F(w).indirect(lists[q]), F(a), A.min, [w, L[q], a], [b], C, True)
-            if k < 8: shift(F(wn), F(b), (2.0 ** (k + 1) if k < 7 else 64.0) * TINY, [b], [wn])
-        key = R("key1")
+            w, nx = "w%d" % (k % 2), "key%d" % (k % 2)
+            shift(F(w), F(key), 2.0 ** k * TINY, [key], [w])
+            if k == 6: shift(F("near"), F(key), -64 * TINY, [key], ["near"])
+            tt(F(nx), F(w).indirect(lists[k]), F(key), A.min, [w, L[k], key], [nx], C, True)
+            key = nx
+        tt(F("key"), F(key).indirect(lists[6]), F("near"), A.min, [key, L[6], "near"], ["key"], C, True)
+        key = "key"
 
-        act(B(R("kb")), F(key), AF.Identity, [key], [R("kb")], scale=1 / UNIT, bias=-MID * TINY)
-        RL = R("RL")
-        compact(tu(RL, 40, 0, 20), R("kb"), MID + 0.25, [R("kb")], [RL + "a"])
-        ts(tu(RL, 40, 20, 40), B(R("kb") + "k", C, 15, C, 16), SC, MID + 1.25, A.mult, A.add, [R("kb") + "k", "sc"], [RL + "b"])
-        tt(F(R("mx")), F(key), F("lab"), A.max, [key, "lab"], [R("mx")], C)
-        eb, be = "eb%d" % h, R("be")
-        scan(B(eb, 2 * C, 1, C + 1), F(R("mx")), F("lab"), -MID * TINY, A.add, A.subtract, [R("mx"), "lab"], [eb])
-        gw, prow = "gw%d" % h, R("prow")
-        scan(F(gw, 2 * C, 1, C + 1), F(R("mx")), F("lab2"), 0.0, A.add, A.subtract, [R("mx"), "lab2"], [gw])
-        tt(B(prow), F(gw, 2 * C, 0, C + 1).indirect(tu(RL, 40, 0, 20)), F(key), A.add, [gw, RL + "a", key], [prow], C, True)
-        compact(tu(R("P16")), prow, MID + 0.25, [prow], [R("P16")])
-        ts(ti(R("pos")), B(prow + "k", C, 15, C, 16), SC, float(MID), A.mult, A.add, [prow + "k", "sc"], [R("pos")])
-        it = R("it")
-        move(B(be, 2 * C, 0, C), B(eb, 2 * C, 0, C + 1).indirect(tu(RL, 40, 0, 20)), [eb, RL + "a"], [be + "b"], ind=True)
-        affine(B(be, 2 * C, C, 2 * C), B(eb, 2 * C, 0, C + 1).indirect(tu(RL, 40, 20, 40)), 1.0, -TINY, [eb, RL + "b"], [be + "e"], ind=True)
-        compact(ti(it, 80, 40, 80), be, float(MID), [be + "b", be + "e"], [it + "b"], 2)
-        tt(ti(it, 80, 20, 40), ti(R("pos")), ti(it, 80, 40, 60), A.subtract, [R("pos"), it + "b"], [it + "c"])
-        tt(ti(it, 80, 0, 20), ti(it, 80, 60, 80), ti(it, 80, 40, 60), A.subtract, [it + "b"], [it + "n"])
+        RL, prow, it = R("RL"), R("prow"), R("it")
         sa, sb, SA, O16 = T["sa%d" % r], T["sb%d" % r], "sa%d" % r, "sb%d" % r
-        vcopy(sa[:], ti(it, 80), [it + "n", it + "c", it + "b"], [SA], 80)
+        scan(F("keyk"), B("dkey"), F(key), 0.0, A.add, A.max, ["dkey", key], ["keyk"])
+        ts(tu(RL), F("keyk", C, 15, C, 16), 1 / (UNIT * TINY), ROOT, A.mult, A.add, ["keyk", "root"], [RL])
+        ts(ti("ki"), F("keyk", C, 15, C, 16), BIG, LOW, A.mult, A.add, ["keyk", "big", "low"], ["ki"])
+        ts(ti(it, 80, 20, 40), ti("ki"), int(UNIT) - 1, None, A.bitwise_and, None, ["ki"], [it + "c"])
+        vcopy(sa[:, 20:40], ti(it, 80, 20, 40), [it + "c"], [SA + "c"])
+        scan(F("mx"), F(key), F("lab"), -1.0, A.max, A.max, [key, "lab"], ["mx"])
+        scan(F("gw", 2 * C, 1, C + 1), F("mx"), F("lab2"), 0.0, A.add, A.subtract, ["mx", "lab2"], ["gw"])
+        tt(B(prow), F("gw", 2 * C, 0, C + 1).indirect(tu(RL)), F(key), A.add, ["gw", RL, key], [prow], C, True)
+        compact(tu(R("P16")), prow, MID + 0.25, [prow], [R("P16")])
+        ts(ti("pos"), kept(prow), SC, float(MID), A.mult, A.add, [prow + "k", "sc"], ["pos"])
+        vcopy(ub(5), kept(prow), [prow + "k"], ["ub5"])
+        move(B(R("end")), B(prow).indirect(tu(RL)), [prow, RL], [R("end")], ind=True)
+        compact(ti(it, 80, 60, 80), R("end"), float(MID), [R("end")], [it + "e"])
+        ts(sa[:, 60:80], kept(R("end")), SC, MID + 0.25, A.mult, A.add, [R("end") + "k", "sc"], [SA + "e"])
+        tt(ti(it, 80, 40, 60), ti("pos"), ti(it, 80, 20, 40), A.subtract, ["pos", it + "c"], [it + "b"])
+        tt(ti(it, 80, 0, 20), ti(it, 80, 60, 80), ti(it, 80, 40, 60), A.subtract, [it + "e", it + "b"], [it + "n"])
+        vcopy(sa[:, 0:20], ti(it, 80, 0, 20), [it + "n"], [SA + "n"])
+        vcopy(sa[:, 40:60], ti(it, 80, 40, 60), [it + "b"], [SA + "b"])
         E16 = sa[:, 60:80]
-        send("aa%d" % r, [(T["la%d" % r][:], sa[:, 0:60])], [SA], "la%d" % r, 4500.0)
-        ts(tf(R("nf")), ti(it, 80, 0, 20), 1.0, None, A.add, None, [it + "n"], [R("nf")])
+        send("aa%d" % r, [(T["la%d" % r][:], sa[:, 0:60])], [SA + "n", SA + "c", SA + "b"], "la%d" % r, 4500.0)
+        ts(ua(4), ti(it, 80, 0, 20), 1.0, ISC, A.add, A.mult, [it + "n", "isc"], ["ua4"])
         ol = R("ol")
         scatter(B(ol).indirect(tu(R("P16"))), B("iob"), [R("P16"), "iob"], [ol])
         compact(sb[:], ol, MID + 0.25, [ol], [O16])
         send("ab%d" % r, [(T["lb%d" % r][:], sb[:])], [O16], "lb%d" % r, 4500.0)
-        act(B(R("flag")), B("iob").indirect(sa[:, 20:40]), AF.Relu, ["iob", SA], [R("flag")], scale=-2.0 ** 97, bias=(1.0 - MID) * TINY * 2.0 ** 97, ind=True)
-        act(B(R("d0")), B(R("flag")).indirect(sb[:]), AF.Copy, [R("flag"), O16], [R("d0")], scale=-2.0 ** 97, ind=True)
-        move(B(R("d1")), B(R("d0")), [R("d0")], [R("d1")], scale=-1.0)
+        act(B(R("flag")), B("iob").indirect(sa[:, 20:40]), AF.Relu, ["iob", SA + "c"], [R("flag")], scale=-2.0 ** 97, bias=(1.0 - MID) * TINY * 2.0 ** 97, ind=True)
+        move(B(R("d0")), B(R("flag")).indirect(sb[:]), [R("flag"), O16], [R("d0")], scale=-2.0 ** 97, ind=True)
+        move(B(R("d1")), B(R("d0")), [R("d0")], [R("d1")], scale=-1.0, half=True)
         fg = R("fg")
-        move(B(fg, 2 * C, 0, C), B(R("fr0")).indirect(tu("M16")), [R("fr0"), "M16"], [fg + "f"], ind=True)
+        image(B(fg, 2 * C, 0, C), tu("M16"), ["M16"], [fg + "f"])
         move(B(fg, 2 * C, C, 2 * C), B("mr").indirect(gl_), ["mr", GL], [fg + "g"], ind=True)
-        compact(tf(R("fgv"), 40), fg, MID + 0.25, [fg + "f", fg + "g"], [R("fgv")], 2)
-        ts(tf(R("fg0"), 40), tu(LG, 40), 0.25, None, A.add, None, [FL, GL], [R("fg0")], 40)
-        tt(tf(R("fgd"), 40), tf(R("fgv"), 40), tf(R("fg0"), 40), A.subtract, [R("fgv"), R("fg0")], [R("fgd")], 40)
-        ts(tf(R("fgs"), 40), tf(R("fgd"), 40), SC, None, A.mult, None, [R("fgd"), "sc"], [R("fgs")], 40)
+        compact(tf("fgv", 40), fg, MID + 0.25, [fg + "f", fg + "g"], ["fgv"], 2)
+        ts(tf("fg0", 40), tu(LG, 40), 0.25, None, A.add, None, [FL, GL], ["fg0"], 40)
+        tt(tf("fd", 120, 1, 120, 3), tf("fgv", 40), tf("fg0", 40), A.subtract, ["fgv", "fg0"], ["fd1"], 40)
+        ts(tf("fgk", 40), tf("fd", 120, 1, 120, 3), KSW, None, A.mult, None, ["fd1", "ksw"], ["fgk"], 40)
+        tt(tf("fd", 120, 2, 120, 3), tf("fgk", 40), tf("fg0", 40), A.add, ["fgk", "fg0"], ["fd2"], 40)
 
-        move(F(R("so")), F(R("s")).indirect(sb[:]), [R("s"), O16], [R("so")], ind=True)
-        scan(F(R("pm")), B(R("d0")), F(R("so")), -2.0 ** 92, A.add, A.max, [R("d0"), R("so")], [R("pm")])
-        tt(F(R("eq")), F(R("pm")).indirect(E16), F(R("s")), A.subtract, [R("pm"), SA, R("s")], [R("eq")], C, True)
-        tt(B(R("cd")), F(R("eq")).indirect(sb[:]), B(ol), A.add, [R("eq"), O16, ol], [R("cd")], C, True)
+        move(F("so"), F(R("s")).indirect(sb[:]), [R("s"), O16], ["so"], ind=True)
+        scan(F("pm"), B(R("d0")), F("so"), -2.0 ** 92, A.add, A.max, [R("d0"), "so"], ["pm"])
+        tt(F("eq"), F("pm").indirect(E16), F(R("s")), A.subtract, ["pm", SA + "e", R("s")], ["eq"], C, True)
+        tt(B(R("cd")), F("eq").indirect(sb[:]), B(ol), A.add, ["eq", O16, ol], [R("cd")], C, True)
         scan(B(R("cs")), B(R("d1")), B(R("cd")), 0.0, A.add, A.min, [R("d1"), R("cd")], [R("cs")], C, True)
-        move(B(R("gk")), B(R("cs")).indirect(E16), [R("cs"), SA], [R("gk")], ind=True)
+        move(B(R("gk")), B(R("cs")).indirect(E16), [R("cs"), SA + "e"], [R("gk")], ind=True)
         l16 = R("l16")
         compact(tu(l16), R("gk"), MID + 0.25, [R("gk")], [l16])
 
-        xa = R("xa")
+        xa, lb, LB = R("xa"), T["lb%d" % r][:], "lb%d" % r
         for q in range(3):
             move(B(xa, 3 * C, C * q, C * q + C), B("iob").indirect(T["la%d" % r][:, 20 * q:20 * q + 20]), ["iob", "la%d" % r], [xa + str(q)], ind=True)
-        move(B(R("oe")), B("iob").indirect(T["lb%d" % r][:]), ["iob", "lb%d" % r], [R("oe")], ind=True)
-        move(B(R("xn")), B(xa, 3 * C, 0, C).indirect(tu(l16)), [xa + "0", l16], [R("xn")], ind=True)
-        compact(ti(R("xni")), R("xn"), MID + 1.0, [R("xn")], [R("xni")])
-        xd = R("xd")
-        for q in (1, 2): move(B(xd, 2 * C, C * q - C, C * q), B(xa, 3 * C, C * q, C * q + C).indirect(tu(l16)), [xa + str(q), l16], [xd + str(q)], ind=True)
-        compact(None, xd, 0.0, [xd + "1", xd + "2"], None, 2)
-        ts(tf(R("xb")), B(xd + "k", 2 * C, C + 15, 2 * C, 16), SC, float(MID), A.mult, A.add, [xd + "k", "sc"], [R("xb")])
-        move(B(R("xp")), B(R("prow")).indirect(tu(l16)), [R("prow"), l16], [R("xp")], ind=True)
-        compact(None, R("xp"), 0.0, [R("xp")], None)
-        tt(tf(R("dl")), B(R("xp") + "k", C, 15, C, 16), B(prow + "k", C, 15, C, 16), A.subtract, [R("xp") + "k", prow + "k"], [R("dl")])
-        ts(tf(R("ng")), tf(R("dl")), SC, -0.5, A.mult, A.is_lt, [R("dl"), "sc"], [R("ng")])
-        tt(tf(R("nn")), tf(R("ng")), tf(R("nf")), A.mult, [R("ng"), R("nf")], [R("nn")])
-        vcopy(tf(R("ne")), ti(R("xni")), [R("xni")], [R("ne")])
-        add(P, {"v": 300.0}, lambda e, a=R("rn"), b=R("ne"): g.vector.reciprocal(tf(a), tf(b)), [R("ne")], [R("rn")])
-        tt(tf(R("zr")), B(xd + "k", 2 * C, 15, C, 16), tf(R("dl")), A.subtract, [xd + "k", R("dl")], [R("zr")])
-        ts(tf(R("z0")), tf(R("zr")), SC, MID + 0.5, A.mult, A.add, [R("zr"), "sc"], [R("z0")])
-        tt(tf(R("zh")), tf(R("z0")), tf(R("nn")), A.subtract, [R("z0"), R("nn")], [R("zh")])
-        tt(tf(R("tq")), tf(R("zh")), tf(R("rn")), A.mult, [R("zh"), R("rn")], [R("tq")])
-        ts(ti(R("qi")), tf(R("tq")), -0.5, None, A.add, None, [R("tq")], [R("qi")])
-        tt(tf(R("zb")), tf(R("zh")), tf(R("xb")), A.add, [R("zh"), R("xb")], [R("zb")])
-        tt(tf(R("m1")), ti(R("qi")), tf(R("ne")), A.mult, [R("qi"), R("ne")], [R("m1")])
-        tt(tf(R("pp")), tf(R("zb")), tf(R("m1")), A.subtract, [R("zb"), R("m1")], [R("pp")])
-        ts(tu(R("PL")), tf(R("pp")), -0.25, None, A.add, None, [R("pp")], [R("PL")])
-        move(B(R("tr")), B(R("oe")).indirect(tu(R("PL"))), [R("oe"), R("PL")], [R("tr")], ind=True)
-        T16 = R("T16")
+        move(B(R("oe")), B("iob").indirect(lb), ["iob", LB], [R("oe")], ind=True)
+        move(F("se"), F(R("s")).indirect(lb), [R("s"), LB], ["se"], ind=True)
+        for q, nm in enumerate(("xn", "xc", "xb")):
+            move(B(nm), B(xa, 3 * C, C * q, C * q + C).indirect(tu(l16)), [xa + str(q), l16], [nm], ind=True)
+        move(B("xp"), B(prow).indirect(tu(l16)), [prow, l16], ["xp"], ind=True)
+        compact(ti("xni"), "xn", MID + 1.0, ["xn"], ["xni"])
+        vcopy(va(4), ti("xni"), ["xni"], ["va4"])
+        add(P, {"v": 190 + 120 * CY}, lambda e: g.vector.reciprocal(va(1), va(4)), ["va4"], ["va1"])
+        compact(tf("xbt"), "xb", MID + 0.25, ["xb"], ["xbt"])
+        for nm in ("xp", "xc"): compact(None, nm, 0.0, [nm], None)
+        tt(ub(0), kept(prow), kept("xp"), A.subtract, ["xpk", prow + "k"], ["ub0"])
+        tt(ub(4), kept("xc"), kept("xp"), A.subtract, ["xpk", "xck"], ["ub4"])
+        scan(tf("uo", 160), tf("ua", 160), tf("ub", 160), 0.0, A.mult, A.add, ["ua", "ua1", "ua4", "ua6"] + ["ub%d" % k for k in range(8)], ["uo"], 160)
+        ts(vb(0), tf("uo", 160, 7, 160, 8), 0.5, None, A.add, None, ["uo"], ["vb0"])
+        tt(vb(4), tf("uo", 160, 7, 160, 8), tf("xbt"), A.add, ["uo", "xbt"], ["vb4"])
+        scan(tf("vo", 100), tf("va", 100), tf("vb", 100), 0.0, A.mult, A.add, ["va%d" % k for k in range(5)] + ["vb%d" % k for k in range(5)], ["vo"], 100)
+        PL, T16 = R("PL"), R("T16")
+        vcopy(tu(PL), tf("vo", 100, 4, 100, 5), ["vo"], [PL])
+        move(B(R("tr")), B(R("oe")).indirect(tu(PL)), [R("oe"), PL], [R("tr")], ind=True)
         compact(tu(T16), R("tr"), MID + 0.25, [R("tr")], [T16])
 
-        tt(F(R("st")), F(R("s")).indirect(tu(T16)), F("sg"), A.mult, [R("s"), T16, "sg"], [R("st")], C, True)
+        tt(F("st"), F("se").indirect(tu(PL)), F("sg"), A.mult, ["se", PL, "sg"], ["st"], C, True)
         for c in range(2):
             a, b = C // 2 * c, C // 2 * c + C // 2
-            either(lambda e, o=F(R("su"), C, a, b), i=F(R("st"), C, a, b): g.vector.tensor_copy(o, i) if e == "v" else g.scalar.activation(o, i, AF.Copy),
-                   [R("st")], [R("su") + "ab"[c]], False, C // 2)
-        tt(F(R("sv")), F(R("st")).indirect(tu("M16")), F(R("su")), A.add, [R("st"), R("su") + "a", R("su") + "b", "M16"], [R("sv")], C, True)
-        ts(B(R("sw")), F(R("sv")), 0.0, TINY, A.is_lt, A.mult, [R("sv")], [R("sw")], C)
-        move(B(R("swg")), B(R("sw")).indirect(gl_), [R("sw"), GL], [R("swg")], ind=True)
-        for nm, a, out, kk in (("sw", 0, fn_, FN), ("swg", 20, gn_, GN)):
-            compact(None, R(nm), 0.0, [R(nm)], None)
-            tt(tf(R(nm + "x")), B(R(nm) + "k", C, 15, C, 16), tf(R("fgs"), 40, a, a + 20), A.mult, [R(nm) + "k", R("fgs")], [R(nm + "x")])
-            tt(tf(R(nm + "y")), tf(R(nm + "x")), tf(R("fg0"), 40, a, a + 20), A.add, [R(nm + "x"), R("fg0")], [R(nm + "y")])
-            vcopy(out, tf(R(nm + "y")), [R(nm + "y")], [kk])
+            move(F("su", C, a, b), F("st", C, a, b), ["st"], ["su" + "ab"[c]], scale=-1.0, n=C // 2)
+        tt(B("sw"), F("st").indirect(tu("M16")), F("su"), A.is_lt, ["st", "sua", "sub", "M16"], ["sw"], C, True)
+        move(B("swg"), B("sw").indirect(gl_), ["sw", GL], ["swg"], ind=True)
+        for nm, a, out, kk in (("sw", 0, fn_, FN), ("swg", 60, gn_, GN)):
+            scan(B(nm + "k", 3 * C, 0, 3 * C, 3), B("dsw"), B(nm), 0.0, A.add, A.max, ["dsw", nm], [nm + "k"], C, True)
+            scan(tf(nm + "o", 60), B(nm + "k", 3 * C, 13, 3 * C, 16), tf("fd", 120, a, a + 60), 0.0, A.mult, A.add, [nm + "k", "fd1", "fd2"], [nm + "o"], 60)
+            vcopy(out, tf(nm + "o", 60, 2, 60, 3), [nm + "o"], [kk])
 
         fh, fs, gp, zt, xt, rs = [T["%s%d" % (k, h)] for k in ("fh", "fs", "gp", "zt", "xt", "rs")]
         for b in range(4):

@@ -19,7 +19,6 @@ SCRATCH = {
     "tabu": ("sbuf", [128, 20 * NU], "uint16"),
     "fli": ("sbuf", [128, 20], "int32"),
     "mli": ("sbuf", [128, 20], "int32"),
-    "jm": ("sbuf", [128, 2 * C], "float32"),
     "dcon": ("sbuf", [128, 2 * C], "bfloat16"),
     "pcol": ("sbuf", [128, 8], "int32"),
     "pcolf": ("sbuf", [128, 32], "float32"),
@@ -40,6 +39,7 @@ SCRATCH = {
     "vs": ("sbuf", [128, 128], "uint8"),
     "wq": ("sbuf", [128, 512], "float8_e4m3fn_x4"),
     "wsc": ("sbuf", [128, 512], "uint8"),
+    "pp": ("sbuf", [128, 4 * C], "float32"),
     "ys": ("sbuf", [128, C], "float32"),
     "nls": ("sbuf", [128, C], "float32"),
     "ps": ("psum", [128, 512 * 8], "float32"),
@@ -66,8 +66,11 @@ SEMAPHORES = ["ev", "es", "et", "eg", "rl"] + ["ld_" + n for n in LOADS] + ["st_
     + ["%s%d" % (k, r) for k in ("aq", "aa", "ab") for r in range(ROUNDS)]
 
 CY, GA, SA_, WAKE = 0.83 * 1.25, 1.56, 3.8, 130.0
-SPARE, REACH, SLACK, SEED = 300.0, 1500.0, 200.0, 1
-PASSES = 9000
+LOAD, LISTS, CODES = 1700.0, 3200.0, 7500.0
+SPARE, REACH, SLACK, SEED = 300.0, 1500.0, 400.0, 1
+PASSES = 14000
+HALVES = ("so", "gk", "base")
+APART = (4, 4, 1)
 PLAN = {}
 
 
@@ -132,26 +135,50 @@ def order(P):
         for j in pre[i]: succ[j].append(i)
 
     def twice(key, side):
-        en = lay(ops, pre, key, side, False)[1]
-        en = lay(ops, succ, [-x for x in en], side, True)[1]
-        return lay(ops, pre, [-x for x in en], side, False)
+        a = lay(ops, pre, key, side, False)
+        en = lay(ops, succ, [-x for x in a[1]], side, True)[1]
+        b = lay(ops, pre, [-x for x in en], side, False)
+        return b if max(b[1]) <= max(a[1]) else a
+
+    def held(st, en, on):
+        before, last = {}, {}
+        for i in sorted(range(n), key=lambda i: st[i]):
+            before[i], last[on[i]] = last.get(on[i]), i
+        i, out = max(range(n), key=lambda i: en[i]), []
+        while st[i] > 0:
+            needs = [j for j in pre[i] if abs(en[j] + WAKE - st[i]) < 1e-3]
+            if not needs: out.append((before[i], i))
+            i = needs[0] if needs else before[i]
+        return out
+    state = [SEED]
+
+    def draw():
+        state[0] = (state[0] * 6364136223846793005 + 1442695040888963407) % 2 ** 64
+        return (state[0] >> 11) / 2.0 ** 53
     way = [0.0] * n
     for i in range(n - 1, -1, -1):
         way[i] = min([way[s] - WAKE for s in succ[i]], default=0.0) - min(ops[i]["c"].values()) - ops[i]["lat"]
     both = [i for i in range(n) if len(ops[i]["c"]) > 1]
+    other = {"s": "v", "v": "s"}
     best = now = twice(way, ["".join(o["c"]) for o in ops])
-    x = SEED
+    hold = held(*now)
     for p in range(PASSES):
         key, side = list(now[0]), list(now[2])
-        for _ in range(2):
-            x = (x * 6364136223846793005 + 1442695040888963407) % 2 ** 64
-            if (x >> 60) < 6:
-                i = both[(x >> 20) % len(both)]
-                side[i] = "s" if side[i] == "v" else "v"
-            else: key[(x >> 20) % n] += REACH * ((x >> 45) % 1024 / 512 - 1)
+        u, v = draw(), draw()
+        if u < 0.6 and hold:
+            a, b = hold[int(draw() * len(hold))]
+            if v < 0.3 and len(ops[a]["c"]) > 1: side[a] = other[side[a]]
+            elif v < 0.5 and len(ops[b]["c"]) > 1: side[b] = other[side[b]]
+            elif v < 0.75: key[a] = key[b] + draw() * REACH
+            else: key[a] -= 2 * draw() * REACH
+        elif u < 0.76:
+            i = both[int(v * len(both))]
+            side[i] = other[side[i]]
+        else: key[int(v * n)] += REACH * (2 * draw() - 1)
         new = twice(key, side)
-        if max(new[1]) <= max(now[1]) + SLACK * (1 - p / PASSES) * ((x >> 8) % 1024 / 1024) ** 2: now = new
-        if max(now[1]) < max(best[1]): best = now
+        if max(new[1]) <= max(now[1]) + SLACK * (1 - p / PASSES) * draw() ** 2:
+            now, hold = new, held(*new)
+            if max(now[1]) < max(best[1]): best = now
     PLAN["seq"], PLAN["done"] = sorted((best[0][i], i, best[2][i]) for i in range(n)), best[1]
     return PLAN["seq"], PLAN["done"]
 
@@ -249,11 +276,15 @@ def rank_program(g, core, T, topo):
             return g.vector.tensor_copy(out, in_) if scale is None else g.vector.tensor_scalar(out, in_, scale, None, A.mult)
         return either(call, rd, wr, ind, n, half)
 
-    def affine(out, in_, a, b, rd, wr, ind=False):
+    def affine(out, in_, a, b, rd, wr, ind=False, half=False, n=C):
         def call(e):
             if e == "s": return g.scalar.activation(out, in_, AF.Identity, bias=b, scale=a)
             return g.vector.tensor_scalar(out, in_, a, b, A.mult, A.add)
-        return either(call, rd, wr, ind)
+        return either(call, rd, wr, ind, n, half)
+
+    def gather(row, nm, win, lst, rd, halves):
+        if not halves: return move(row(nm), win.indirect(lst(0, 20)), rd, [nm + "0", nm + "1"], ind=True)
+        for q in range(2): move(row(nm, C, q * C // 2, q * C // 2 + C // 2), win.indirect(lst(10 * q, 10 * q + 10)), rd, [nm + str(q)], ind=True, n=C // 2)
 
     def shift(out, in_, x, rd, wr):
         def call(e):
@@ -269,7 +300,7 @@ def rank_program(g, core, T, topo):
         return add(P, {"t": 1.4 * 0.83 * (C + 16)}, lambda e: g.tensor.matmul_mx(bank(b), w, ws, x, xs, True, True), rd, ["ps%d" % b])
 
     def load(q, nm, out, in_):
-        return add(P, {q: 60.0}, lambda e: (g.sync if e == "y" else g.scalar).dma_start(out, in_), [], [nm], sem="ld_" + nm, lat=2300.0)
+        return add(P, {q: 60.0}, lambda e: (g.sync if e == "y" else g.scalar).dma_start(out, in_), [], [nm], sem="ld_" + nm, lat=LOAD)
 
     load("y", "fl", T.fli[:], T.fl[:, :])
     load("y", "ml", T.mli[:], T.ml[:, :])
@@ -283,10 +314,10 @@ def rank_program(g, core, T, topo):
         def call(e): return g.iota(out, pat, base, cm, allow_small_or_imprecise_dtypes=True) if fl else g.iota(out, pat, base, cm)
         return add(P, {"g": 130 + 2 * n * CY}, call, [], wr)
     iota(T.pcol[:, 0:1], [[1, 1]], 0, 1, ["pcol"], 1, False)
-    iota(F("iof"), [[1, C]], 0, 0, ["iof"], C, True)
-    iota(T.jm[:], [[0, 40], [1, 16]], 0, 0, ["jm"], 2 * C, True)
+    iota(B("jm"), [[0, C // 16], [1, 16]], 0, 0, ["jm"], C, True)
     iota(T.ui[:], [[16, 8]], 0, 0, ["ui"], 8, False)
-    ts(B("iob"), F("iof"), -float(MID), TINY, A.add, A.mult, ["iof"], ["iob"], C)
+    fill(B("step"), TINY / 2, ["step"], C / 2)
+    scan(B("iob"), B("step"), B("step"), -(MID + 1) * TINY, A.add, A.add, ["step"], ["iob"], C, True)
     pc = T.pcol
 
     def col(k): return T.pcolf[:, k:k + 1]
@@ -297,32 +328,30 @@ def rank_program(g, core, T, topo):
     ts(col(5), col(2), 2.0 ** (102 - 15 * STEPB), None, A.mult, None, ["pf2"], ["pf5"])
     tt(col(6), col(3), col(5), A.mult, ["pf3", "pf5"], ["pf6"])
     tt(col(7), col(4), col(6), A.mult, ["pf4", "pf6"], ["sc"])
-    SC, PLACE, ISC, ROOT, BIG, LOW, KSW = col(7), col(8), col(9), col(10), col(11), col(12), col(13)
+    SC, PLACE, ISC, BIG, BIG2, LOW, LOW2, KSW, LEAD, ROOT = [col(k) for k in range(7, 16)] + [16]
     add(P, {"v": 200.0}, lambda e: g.vector.reciprocal(ISC, SC), ["sc"], ["isc"])
     ts(pc[:, 5:6], pc[:, 0:1], 15, None, A.bitwise_and, None, ["pcol"], ["p15"])
     vcopy(PLACE, pc[:, 5:6], ["p15"], ["p15f"])
-    ts(ROOT, PLACE, RISE / UNIT, 0.25 - 15 * RISE / UNIT, A.mult, A.add, ["p15f"], ["root"])
-    ts(LOW, PLACE, RISE, MID - 15 * RISE, A.mult, A.add, ["p15f"], ["low"])
-    ts(KSW, PLACE, 2.0, -30.0, A.mult, A.add, ["p15f"], ["ksw"])
-    fill(col(14), 2.0 ** 51, ["b51"])
-    ts(BIG, col(14), 2.0 ** 51, None, A.mult, None, ["b51"], ["big"])
-    ts(T.dcon[:], T.jm[:], PLACE, 2.0 ** STEPB, A.is_gt, A.mult, ["jm", "p15f"], ["dcon"], 2 * C)
-    affine(B("dkey"), T.dcon[:, 0:C], 33 * RISE * TINY / 2 ** STEPB, -32 * RISE * TINY, ["dcon"], ["dkey"])
-    affine(B("dsw"), T.dcon[:, 0:C], 66.0 / 2 ** STEPB, -64.0, ["dcon"], ["dsw"])
-    affine(F("lab"), F("iof"), UNIT * TINY, -(MID + 1) * TINY, ["iof"], ["lab"])
-    affine(F("lab2"), F("iof"), UNIT * TINY, (UNIT - MID - 1) * TINY, ["iof"], ["lab2"])
-    fill(F("gw", 2 * C, 0, 8), 0.0, ["gw"])
+    for out, a, b, nm in ((col(ROOT), RISE / UNIT, 0.25, "root0"), (col(ROOT + 1), RISE / UNIT, 1.25, "root1"), (LEAD, RISE / UNIT, MID + 0.125, "lead"),
+                          (LOW, RISE, MID, "low"), (LOW2, RISE, MID * UNIT + 1, "low2"), (KSW, 2.0, 0.0, "ksw")):
+        ts(out, PLACE, a, b - 15 * a, A.mult, A.add, ["p15f"], [nm])
+    fill(col(18), 2.0 ** 51, ["b51"])
+    ts(BIG, col(18), 2.0 ** 51, None, A.mult, None, ["b51"], ["big"])
+    ts(BIG2, col(18), 2.0 ** 51 * UNIT, None, A.mult, None, ["b51"], ["big2"])
+    for q in range(2): ts(T.dcon[:, C * q:C * q + C], B("jm"), PLACE, 2.0 ** STEPB, A.is_gt, A.mult, ["jm", "p15f"], ["dcon%d" % q], C / 2)
+    for nm, x in (("dkey", RISE * TINY), ("dgk", RISE * TINY / UNIT), ("dsw", 2.0)):
+        affine(B(nm), T.dcon[:, 0:C], 33 * x / 2 ** STEPB, -32 * x, ["dcon0"], [nm], half=True)
+    affine(F("lab"), B("iob"), UNIT, (MID * UNIT - MID - 1) * TINY, ["iob"], ["lab"])
+    fill(B("sum", 2 * C, 0, 16), -MID * TINY, ["sum"])
     for nm in ("swk", "swgk"): fill(B(nm, 3 * C), 0.0, [nm], 3 * C / 2)
     fill(tf("fd", 120), 0.0, ["fd1", "fd2"], 120)
-    def ua(k): return tf("ua", 160, k, 160, 8)
-    def ub(k): return tf("ub", 160, k, 160, 8)
+    def ua(k): return tf("ua", 80, k, 80, 4)
+    def ub(k): return tf("ub", 80, k, 80, 4)
     def va(k): return tf("va", 100, k, 100, 5)
     def vb(k): return tf("vb", 100, k, 100, 5)
-    fill(tf("ua", 160), 1.0, ["ua", "ua4"], 160)
-    ts(ua(1), ua(0), SC, -1 / 1024, A.mult, A.mult, ["ua", "sc"], ["ua1"])
-    ts(ua(6), ua(0), SC, None, A.mult, None, ["ua", "sc"], ["ua6"])
+    fill(tf("ua", 80), 1.0, ["ua", "ua1"], 80)
+    for out, x, nm in ((ua(2), 1.0, "ua2"), (ub(2), -MID - 0.5, "ub2"), (ub(3), 0.25, "ub3")): ts(out, ua(0), ISC, x, A.mult, A.mult, ["ua", "isc"], [nm])
     fill(ua(0), 0.0, ["ua"])
-    for k, x in ((1, 0.5 / 1024 - 0.5), (2, WHOLE), (3, -WHOLE), (6, WHOLE + MID), (7, -WHOLE)): fill(ub(k), x, ["ub%d" % k])
     for k, x in ((0, 0.0), (2, 1.0), (3, -1.0)): fill(va(k), x, ["va%d" % k])
     for k, x in ((1, -0.5), (2, WHOLE), (3, WHOLE)): fill(vb(k), x, ["vb%d" % k])
     fill(T.half[:], 0.5, ["half"], 256)
@@ -342,7 +371,7 @@ def rank_program(g, core, T, topo):
 
     def compact(out, nm, bias, rd, wr, w=1):
         n = w * C
-        scan(B(nm + "k", n), T.dcon[:, 0:n], B(nm, n), 0.0, A.mult, A.add, rd + ["dcon"], [nm + "k"], n, True)
+        scan(B(nm + "k", n), T.dcon[:, 0:n], B(nm, n), 0.0, A.mult, A.add, rd + ["dcon0", "dcon1"][:w], [nm + "k"], n, True)
         if out is not None: ts(out, B(nm + "k", n, 15, n, 16), SC, bias, A.mult, A.add, [nm + "k", "sc"], wr, 20 * w)
 
     vcopy(tu("LG0", 40, 0, 20), T.fli[:], ["fl"], ["L0_0"])
@@ -361,17 +390,19 @@ def rank_program(g, core, T, topo):
         R = lambda nm: "%s_%d" % (nm, h)
         partner = T.cores[rank ^ MASKS[r]]
         rid, pid, _s = topo.addr(partner)
-        msk, ne = sum(1 << e for e in common), len(common)
         X, Xq, Xs = "X%d" % r, T["xq%d" % r], T["xs%d" % r]
 
-        def send(sem, pieces, rd, key, lat):
+        def send(sem, pieces, rd, key, lat, engines):
+            msk, ne = sum(1 << e for e in engines), len(engines)
             for dst, src in pieces:
                 last = add(P, {"g": 300.0}, lambda e, dst=dst, src=src, sem=sem, rid=rid, pid=pid, msk=msk: g.remote_dma(dst, src, T.sem[sem], T.sem.rl, pid, rid, msk),
                            rd, ["net"], sem="rl", val=0)
                 sent[0] += ne
             add(P, {"n": 0.0}, None, [], [key], sem=sem, val=ne * len(pieces), after=[last], lat=lat)
 
-        send("aq%d" % r, [(T["lq%d" % r][:].bitcast(dt.uint8), Xq[:].bitcast(dt.uint8)), (T["ls%d" % r][:], Xs[:])], [X], "Y%d" % r, 9000.0)
+        def send_codes():
+            send("aq%d" % r, [(T["lq%d" % r][:].bitcast(dt.uint8), Xq[:].bitcast(dt.uint8)), (T["ls%d" % r][:], Xs[:])], [X], "Y%d" % r, CODES, common[0::2])
+        if r == 0: send_codes()
 
         mm(0, T.up[:], T.ups[:], Xq[:], Xs[:], ["up", "ups", X])
         move(F(R("s")), bank(0), ["ps0"], [R("s")])
@@ -403,36 +434,34 @@ def rank_program(g, core, T, topo):
         tt(F("key"), F(key).indirect(lists[6]), F("near"), A.min, [key, L[6], "near"], ["key"], C, True)
         key = "key"
 
-        RL, prow, it = R("RL"), R("prow"), R("it")
         sa, sb, SA, O16 = T["sa%d" % r], T["sb%d" % r], "sa%d" % r, "sb%d" % r
         scan(F("keyk"), B("dkey"), F(key), 0.0, A.add, A.max, ["dkey", key], ["keyk"])
-        ts(tu(RL), F("keyk", C, 15, C, 16), 1 / (UNIT * TINY), ROOT, A.mult, A.add, ["keyk", "root"], [RL])
+        for q in range(2): ts(tu("RL", 40, 20 * q, 20 * q + 20), F("keyk", C, 15, C, 16), 1 / (UNIT * TINY), col(ROOT + q), A.mult, A.add, ["keyk", "root%d" % q], ["RL%d" % q])
         ts(ti("ki"), F("keyk", C, 15, C, 16), BIG, LOW, A.mult, A.add, ["keyk", "big", "low"], ["ki"])
-        ts(ti(it, 80, 20, 40), ti("ki"), int(UNIT) - 1, None, A.bitwise_and, None, ["ki"], [it + "c"])
-        vcopy(sa[:, 20:40], ti(it, 80, 20, 40), [it + "c"], [SA + "c"])
+        ts(ti("ci"), ti("ki"), int(UNIT) - 1, None, A.bitwise_and, None, ["ki"], ["ci"])
+        vcopy(sa[:, 20:40], ti("ci"), ["ci"], [SA + "c"])
+        ts(tf("craw"), ti("ci"), ISC, None, A.mult, None, ["ci", "isc"], ["craw"])
         scan(F("mx"), F(key), F("lab"), -1.0, A.max, A.max, [key, "lab"], ["mx"])
-        scan(F("gw", 2 * C, 1, C + 1), F("mx"), F("lab2"), 0.0, A.add, A.subtract, ["mx", "lab2"], ["gw"])
-        tt(B(prow), F("gw", 2 * C, 0, C + 1).indirect(tu(RL)), F(key), A.add, ["gw", RL, key], [prow], C, True)
-        compact(tu(R("P16")), prow, MID + 0.25, [prow], [R("P16")])
-        ts(ti("pos"), kept(prow), SC, float(MID), A.mult, A.add, [prow + "k", "sc"], ["pos"])
-        vcopy(ub(5), kept(prow), [prow + "k"], ["ub5"])
-        move(B(R("end")), B(prow).indirect(tu(RL)), [prow, RL], [R("end")], ind=True)
-        compact(ti(it, 80, 60, 80), R("end"), float(MID), [R("end")], [it + "e"])
-        ts(sa[:, 60:80], kept(R("end")), SC, MID + 0.25, A.mult, A.add, [R("end") + "k", "sc"], [SA + "e"])
-        tt(ti(it, 80, 40, 60), ti("pos"), ti(it, 80, 20, 40), A.subtract, ["pos", it + "c"], [it + "b"])
-        tt(ti(it, 80, 0, 20), ti(it, 80, 60, 80), ti(it, 80, 40, 60), A.subtract, [it + "e", it + "b"], [it + "n"])
-        vcopy(sa[:, 0:20], ti(it, 80, 0, 20), [it + "n"], [SA + "n"])
-        vcopy(sa[:, 40:60], ti(it, 80, 40, 60), [it + "b"], [SA + "b"])
-        E16 = sa[:, 60:80]
-        send("aa%d" % r, [(T["la%d" % r][:], sa[:, 0:60])], [SA + "n", SA + "c", SA + "b"], "la%d" % r, 4500.0)
-        ts(ua(4), ti(it, 80, 0, 20), 1.0, ISC, A.add, A.mult, [it + "n", "isc"], ["ua4"])
+        scan(B("sum", 2 * C, 1, C + 1), F("mx"), F("lab"), -MID * TINY, A.add, A.subtract, ["mx", "lab"], ["sum"])
+        gather(B, "base", B("sum", 2 * C, 0, C + 1), lambda a, b: tu("RL", 40, a, b), ["sum", "RL0"], "base" in HALVES)
+        compact(None, "base", 0.0, ["base0", "base1"], None)
+        tt(tf("praw"), kept("base"), tf("craw"), A.add, ["basek", "craw"], ["praw"])
+        ts(sa[:, 40:60], tf("praw"), SC, MID + 0.25, A.mult, A.add, ["praw", "sc"], [SA + "p"])
+        affine(B("end"), B("sum", 2 * C, 0, C + 1).indirect(tu("RL", 40, 20, 40)), 1.0, -TINY, ["sum", "RL1"], ["end"], ind=True)
+        compact(sa[:, 60:80], "end", MID + 0.25, ["end"], [SA + "e"])
+        tt(tf("nraw"), kept("end"), kept("base"), A.subtract, ["basek", "endk"], ["nraw"])
+        ts(sa[:, 0:20], tf("nraw"), SC, 0.25, A.mult, A.add, ["nraw", "sc"], [SA + "n"])
+        send("aa%d" % r, [(T["la%d" % r][:], sa[:, 0:60])], [SA + "n", SA + "c", SA + "p"], "la%d" % r, LISTS, common[1::2])
+        if r: send_codes()
+        ts(ua(1), sa[:, 0:20], 1.0, None, A.add, None, [SA + "n"], ["ua1"])
+        tt(tf("left"), ua(1), ti("ci"), A.subtract, ["ua1", "ci"], ["left"])
         ol = R("ol")
-        scatter(B(ol).indirect(tu(R("P16"))), B("iob"), [R("P16"), "iob"], [ol])
+        scatter(B(ol).indirect(sa[:, 40:60]), B("iob"), [SA + "p", "iob"], [ol])
         compact(sb[:], ol, MID + 0.25, [ol], [O16])
-        send("ab%d" % r, [(T["lb%d" % r][:], sb[:])], [O16], "lb%d" % r, 4500.0)
+        send("ab%d" % r, [(T["lb%d" % r][:], sb[:])], [O16], "lb%d" % r, LISTS, common[1::2])
         act(B(R("flag")), B("iob").indirect(sa[:, 20:40]), AF.Relu, ["iob", SA + "c"], [R("flag")], scale=-2.0 ** 97, bias=(1.0 - MID) * TINY * 2.0 ** 97, ind=True)
         move(B(R("d0")), B(R("flag")).indirect(sb[:]), [R("flag"), O16], [R("d0")], scale=-2.0 ** 97, ind=True)
-        move(B(R("d1")), B(R("d0")), [R("d0")], [R("d1")], scale=-1.0, half=True)
+        affine(B(R("d1")), B(R("d0")), -1.0, TINY / UNIT, [R("d0")], [R("d1")], half=True)
         fg = R("fg")
         image(B(fg, 2 * C, 0, C), tu("M16"), ["M16"], [fg + "f"])
         move(B(fg, 2 * C, C, 2 * C), B("mr").indirect(gl_), ["mr", GL], [fg + "g"], ind=True)
@@ -442,14 +471,20 @@ def rank_program(g, core, T, topo):
         ts(tf("fgk", 40), tf("fd", 120, 1, 120, 3), KSW, None, A.mult, None, ["fd1", "ksw"], ["fgk"], 40)
         tt(tf("fd", 120, 2, 120, 3), tf("fgk", 40), tf("fg0", 40), A.add, ["fgk", "fg0"], ["fd2"], 40)
 
-        move(F("so"), F(R("s")).indirect(sb[:]), [R("s"), O16], ["so"], ind=True)
-        scan(F("pm"), B(R("d0")), F("so"), -2.0 ** 92, A.add, A.max, [R("d0"), "so"], ["pm"])
-        tt(F("eq"), F("pm").indirect(E16), F(R("s")), A.subtract, ["pm", SA + "e", R("s")], ["eq"], C, True)
+        gather(F, "so", F(R("s")), lambda a, b: sb[:, a:b], [R("s"), O16], "so" in HALVES)
+        scan(F("pm"), B(R("d0")), F("so"), -2.0 ** 92, A.add, A.max, [R("d0"), "so0", "so1"], ["pm"])
+        tt(F("eq"), F("pm").indirect(sa[:, 60:80]), F(R("s")), A.subtract, ["pm", SA + "e", R("s")], ["eq"], C, True)
         tt(B(R("cd")), F("eq").indirect(sb[:]), B(ol), A.add, ["eq", O16, ol], [R("cd")], C, True)
-        scan(B(R("cs")), B(R("d1")), B(R("cd")), 0.0, A.add, A.min, [R("d1"), R("cd")], [R("cs")], C, True)
-        move(B(R("gk")), B(R("cs")).indirect(E16), [R("cs"), SA + "e"], [R("gk")], ind=True)
+        scan(F("cs"), B(R("d1")), B(R("cd")), 0.0, A.add, A.min, [R("d1"), R("cd")], ["cs"])
+        gather(F, "gk", F("cs"), lambda a, b: sa[:, 60 + a:60 + b], ["cs", SA + "e"], "gk" in HALVES)
+        scan(F("gkk"), B("dgk"), F("gk"), 0.0, A.add, A.max, ["dgk", "gk0", "gk1"], ["gkk"])
         l16 = R("l16")
-        compact(tu(l16), R("gk"), MID + 0.25, [R("gk")], [l16])
+        ts(tu(l16), F("gkk", C, 15, C, 16), BIG, LEAD, A.mult, A.add, ["gkk", "big", "lead"], [l16])
+        ts(ti("li"), F("gkk", C, 15, C, 16), BIG2, LOW2, A.mult, A.add, ["gkk", "big2", "low2"], ["li"])
+        ts(ti("lj"), ti("li"), int(UNIT) - 1, None, A.bitwise_and, None, ["li"], ["lj"])
+        tt(ub(1), tf("left"), ti("lj"), A.subtract, ["left", "lj"], ["ub1"])
+        ts(ub(0), ub(1), -0.5, None, A.is_lt, None, ["ub1"], ["ub0"])
+        scan(tf("uo", 80), tf("ua", 80), tf("ub", 80), 0.0, A.mult, A.add, ["ua", "ua1", "ua2"] + ["ub%d" % k for k in range(4)], ["uo"], 80)
 
         xa, lb, LB = R("xa"), T["lb%d" % r][:], "lb%d" % r
         for q in range(3):
@@ -458,20 +493,15 @@ def rank_program(g, core, T, topo):
         move(F("se"), F(R("s")).indirect(lb), [R("s"), LB], ["se"], ind=True)
         for q, nm in enumerate(("xn", "xc", "xb")):
             move(B(nm), B(xa, 3 * C, C * q, C * q + C).indirect(tu(l16)), [xa + str(q), l16], [nm], ind=True)
-        move(B("xp"), B(prow).indirect(tu(l16)), [prow, l16], ["xp"], ind=True)
         compact(ti("xni"), "xn", MID + 1.0, ["xn"], ["xni"])
-        vcopy(va(4), ti("xni"), ["xni"], ["va4"])
+        ts(va(4), ti("xni"), ISC, None, A.mult, None, ["xni", "isc"], ["va4"])
         add(P, {"v": 190 + 120 * CY}, lambda e: g.vector.reciprocal(va(1), va(4)), ["va4"], ["va1"])
-        compact(tf("xbt"), "xb", MID + 0.25, ["xb"], ["xbt"])
-        for nm in ("xp", "xc"): compact(None, nm, 0.0, [nm], None)
-        tt(ub(0), kept(prow), kept("xp"), A.subtract, ["xpk", prow + "k"], ["ub0"])
-        tt(ub(4), kept("xc"), kept("xp"), A.subtract, ["xpk", "xck"], ["ub4"])
-        scan(tf("uo", 160), tf("ua", 160), tf("ub", 160), 0.0, A.mult, A.add, ["ua", "ua1", "ua4", "ua6"] + ["ub%d" % k for k in range(8)], ["uo"], 160)
-        ts(vb(0), tf("uo", 160, 7, 160, 8), 0.5, None, A.add, None, ["uo"], ["vb0"])
-        tt(vb(4), tf("uo", 160, 7, 160, 8), tf("xbt"), A.add, ["uo", "xbt"], ["vb4"])
+        for k, nm in ((0, "xc"), (4, "xb")):
+            compact(None, nm, 0.0, [nm], None)
+            tt(vb(k), kept(nm), tf("uo", 80, 2 + k // 4, 80, 4), A.subtract, [nm + "k", "uo"], ["vb%d" % k])
         scan(tf("vo", 100), tf("va", 100), tf("vb", 100), 0.0, A.mult, A.add, ["va%d" % k for k in range(5)] + ["vb%d" % k for k in range(5)], ["vo"], 100)
         PL, T16 = R("PL"), R("T16")
-        vcopy(tu(PL), tf("vo", 100, 4, 100, 5), ["vo"], [PL])
+        ts(tu(PL), tf("vo", 100, 4, 100, 5), SC, None, A.mult, None, ["vo", "sc"], [PL])
         move(B(R("tr")), B(R("oe")).indirect(tu(PL)), [R("oe"), PL], [R("tr")], ind=True)
         compact(tu(T16), R("tr"), MID + 0.25, [R("tr")], [T16])
 
@@ -499,13 +529,19 @@ def rank_program(g, core, T, topo):
             c = slice(C * b, C * b + C)
             mm(1 + b, T.wq[:, 128 * b:128 * b + 128], T.wsc[:, 128 * b:128 * b + 128], zq[:], zs[:], ["wc", "ws", "zq%d" % h])
             move(rs[:, c], bank(1 + b), ["ps%d" % (1 + b)], ["rs%d%d" % (h, b)], scale=2.0 ** -6)
-            tt(xt[:, b:4 * C:4], rs[:, c].indirect(gn_), fh[:, c], A.add, ["rs%d%d" % (h, b), GN, "fh%d%d" % (h, b)], ["xt%d%d" % (h, b)], C, True)
+            if b < APART[r]:
+                bk = (5, 6, 7, 0)[b]
+                mm(bk, T.eq[:, 128 * b:128 * b + 128], T.es[:, 128 * b:128 * b + 128], Xq[:], Xs[:], ["eq%d" % b, X])
+                move(T.pp[:, c], rs[:, c].indirect(gn_), ["rs%d%d" % (h, b), GN], ["pp%d" % b], ind=True)
+                tt(xt[:, b:4 * C:4], T.pp[:, c], bank(bk), A.add, ["pp%d" % b, "ps%d" % bk], ["xt%d%d" % (h, b)], C / 2)
+            else:
+                tt(xt[:, b:4 * C:4], rs[:, c].indirect(gn_), fh[:, c], A.add, ["rs%d%d" % (h, b), GN, "fh%d%d" % (h, b)], ["xt%d%d" % (h, b)], C, True)
         quant(T["xq%d" % (r + 1)][:], T["xs%d" % (r + 1)][:], xt[:], C, ["xt%d%d" % (h, b) for b in range(4)], ["X%d" % (r + 1)])
 
     q, s, X = T["xq%d" % ROUNDS], T["xs%d" % ROUNDS], "X%d" % ROUNDS
 
     def store(nm, out, in_, rd): add(P, {"y": 60.0}, lambda e: g.sync.dma_start(out, in_), rd, [], sem="st_" + nm, lat=2000.0)
-    act(T.nls[:], F("iof").indirect(tu("LG%d" % ROUNDS, 40, 0, 20)), AF.Copy, ["iof", "L0_%d" % ROUNDS], ["nls"], ind=True)
+    affine(T.nls[:], B("iob").indirect(tu("LG%d" % ROUNDS, 40, 0, 20)), BIG, float(MID), ["iob", "big", "L0_%d" % ROUNDS], ["nls"], ind=True)
     store("nl", T.nl[:, :], T.nls[0:128:16, :], ["nls"])
     mm(1, T.vq[:], T.vs[:], q[:], s[:], ["vq", X])
     move(T.ys[:], bank(1), ["ps1"], ["ys"])

@@ -1,3 +1,4 @@
+import math
 from concourse.mybir import dt, AluOpType as A, ActivationFunctionType as AF
 
 C = 320
@@ -10,7 +11,7 @@ UNIT = 1024.0
 RISE = 512 * UNIT
 WHOLE = 1.5 * 2.0 ** 23
 
-NF, NB, NT, NI, NU = 36, 126, 90, 18, 36
+NF, NB, NT, NI, NU = 36, 110, 90, 18, 48
 SCRATCH = {
     "rowf": ("sbuf", [128, C * NF], "float32"),
     "rowb": ("sbuf", [128, C * NB], "bfloat16"),
@@ -28,6 +29,7 @@ SCRATCH = {
     "et": ("sbuf", [128, 2048], "bfloat16"),
     "eq": ("sbuf", [128, 512], "float8_e4m3fn_x4"),
     "es": ("sbuf", [128, 512], "uint8"),
+    "pp": ("sbuf", [128, 4 * C], "float32"),
     "uin": ("sbuf", [128, 512], "bfloat16"),
     "vin": ("sbuf", [128, 512], "bfloat16"),
     "xin": ("sbuf", [128, 4 * C], "bfloat16"),
@@ -39,7 +41,6 @@ SCRATCH = {
     "vs": ("sbuf", [128, 128], "uint8"),
     "wq": ("sbuf", [128, 512], "float8_e4m3fn_x4"),
     "wsc": ("sbuf", [128, 512], "uint8"),
-    "pp": ("sbuf", [128, 4 * C], "float32"),
     "ys": ("sbuf", [128, C], "float32"),
     "nls": ("sbuf", [128, C], "float32"),
     "ps": ("psum", [128, 512 * 8], "float32"),
@@ -65,12 +66,15 @@ STORES = ("oc", "os0", "os1", "os2", "os3", "y", "nl")
 SEMAPHORES = ["ev", "es", "et", "eg", "rl"] + ["ld_" + n for n in LOADS] + ["st_" + n for n in STORES] \
     + ["%s%d" % (k, r) for k in ("aq", "aa", "ab") for r in range(ROUNDS)]
 
-CY, GA, SA_, WAKE = 0.83 * 1.25, 1.56, 3.8, 130.0
-LOAD, LISTS, CODES = 1700.0, 3200.0, 7500.0
-SPARE, REACH, SLACK, SEED = 300.0, 1500.0, 400.0, 1
-PASSES = 14000
-HALVES = ("so", "gk", "base")
-APART = (4, 4, 1)
+HALVES = ("so", "gk")
+PARTS = (2, 1, 1)
+LATE = (1, 2)
+APART = (4, 4, 2)
+LAYER, TAIL = 192, 192
+
+CY, GA, SA_, PE, WAKE, ISSUE = 0.83 * 1.25, 1.56, 3.8, 1.4 * 0.83, 140.0, 450.0
+LOAD, LISTS, ORDER, CODES = 1800.0, 3000.0, 3700.0, 6400.0
+SPARE, REACH, NEAR, PAIR, WIDTH, TRIES, SLACK, SWEEPS, SEED = 300.0, 12, 8, 0.33, 100, 300, (110.0, 8.0), 330, 7
 PLAN = {}
 
 
@@ -90,96 +94,152 @@ def add(P, cost, call, reads, writes, sem=None, val=16, after=(), lat=0.0):
     return i
 
 
-def lay(ops, pre, key, side, back):
-    n = len(ops)
-    st, en, on = [0.0] * n, [None] * n, [None] * n
-    begin, end = {e: [] for e in "vstgyn"}, {e: [] for e in "vstgyn"}
-    for first in sorted(range(n), key=lambda i: key[i]):
-        todo = [first]
-        while todo:
-            i = todo[-1]
-            if en[i] is not None:
-                todo.pop()
-                continue
-            t = 0.0
-            for j in pre[i]:
-                x = en[j]
-                if x is None: todo.append(j)
-                elif x + WAKE > t: t = x + WAKE
-            if todo[-1] != i: continue
-            o, best = ops[i], None
-            if back: t += o["lat"]
-            for e in side[i]:
-                c, s, f, a = o["c"][e], begin[e], end[e], t
-                k = len(f)
-                while k and f[k - 1] > t: k -= 1
-                while k < len(s) and s[k] < a + c - 1e-6:
-                    a = f[k]
-                    k += 1
-                x = a + c + (SPARE if e == "v" else 0.0)
-                if best is None or x < best[0]: best = (x, a, c, e, k)
-            x, a, c, e, k = best
-            if c:
-                begin[e].insert(k, a)
-                end[e].insert(k, a + c)
-            st[i], en[i], on[i] = a, a + c + (0.0 if back else o["lat"]), e
-    return st, en, on
+QUEUES = "vstgyn"
+
+
+def lay(cost, tail, pre, way):
+    n = len(cost)
+    st, ready, on = [0.0] * n, [0.0] * n, [0] * n
+    busy = [[] for _ in QUEUES]
+    for i in sorted(range(n), key=lambda i: -way[i]):
+        t, best = max([ready[j] for j in pre[i]], default=0.0), None
+        for e, c in cost[i].items():
+            a = t
+            for x, y in busy[e]:
+                if y > a and x < a + c: a = y
+            if best is None or a + c + (SPARE if e == 0 else 0.0) < best[0]: best = (a + c + (SPARE if e == 0 else 0.0), a, c, e)
+        _, st[i], c, on[i] = best
+        if c: busy[on[i]] = sorted(busy[on[i]] + [(st[i], st[i] + c)])
+        ready[i] = st[i] + c + tail[i]
+    return sorted(range(n), key=lambda i: st[i]), on
 
 
 def order(P):
     if "seq" in PLAN: return PLAN["seq"], PLAN["done"]
     ops = P["ops"]
     n = len(ops)
+    cost = [{QUEUES.index(e): c for e, c in o["c"].items()} for o in ops]
+    tail = [o["lat"] + WAKE for o in ops]
     pre, succ = [o["d"] for o in ops], [[] for _ in range(n)]
     for i in range(n):
         for j in pre[i]: succ[j].append(i)
+    way = [0.0] * n
+    for i in range(n - 1, -1, -1): way[i] = min(cost[i].values()) + tail[i] + max([way[s] for s in succ[i]], default=0.0)
+    seq, on = lay(cost, tail, pre, way)
+    ready, st, by, zero = [0.0] * n, [0.0] * n, [-1] * n, [0.0] * n
 
-    def twice(key, side):
-        a = lay(ops, pre, key, side, False)
-        en = lay(ops, succ, [-x for x in a[1]], side, True)[1]
-        b = lay(ops, pre, [-x for x in en], side, False)
-        return b if max(b[1]) <= max(a[1]) else a
+    def run(part, free, beyond, first):
+        free, last = list(free), [-1] * 6
+        end, who = 0.0, -1
+        for i in part:
+            e = on[i]
+            t, b = free[e], last[e]
+            for j in pre[i]:
+                if ready[j] > t: t, b = ready[j], j
+            by[i], st[i] = b, t
+            if e != 5:
+                t += cost[i][e]
+                free[e], last[e] = t, i
+            t += tail[i]
+            ready[i] = t
+            if t + beyond[i] > end: end, who = t + beyond[i], i
+        for e in range(5):
+            if free[e] + first[e] > end: end, who = free[e] + first[e], last[e]
+        return end, who, free
 
-    def held(st, en, on):
-        before, last = {}, {}
-        for i in sorted(range(n), key=lambda i: st[i]):
-            before[i], last[on[i]] = last.get(on[i]), i
-        i, out = max(range(n), key=lambda i: en[i]), []
-        while st[i] > 0:
-            needs = [j for j in pre[i] if abs(en[j] + WAKE - st[i]) < 1e-3]
-            if not needs: out.append((before[i], i))
-            i = needs[0] if needs else before[i]
+    def states(part, free):
+        free, out = list(free), []
+        for i in part:
+            out.append(tuple(free))
+            if on[i] != 5: free[on[i]] = ready[i] - tail[i]
         return out
+
+    def within(part, free, beyond, first, limit):
+        free, mine = list(free), list(ready)
+        for i in part:
+            e = on[i]
+            t = free[e]
+            for j in pre[i]:
+                if mine[j] > t: t = mine[j]
+            if e != 5: free[e] = t = t + cost[i][e]
+            t += tail[i]
+            if t + beyond[i] > limit: return False
+            mine[i] = t
+        return all(free[e] + first[e] <= limit for e in range(5))
     state = [SEED]
 
     def draw():
         state[0] = (state[0] * 6364136223846793005 + 1442695040888963407) % 2 ** 64
-        return (state[0] >> 11) / 2.0 ** 53
-    way = [0.0] * n
-    for i in range(n - 1, -1, -1):
-        way[i] = min([way[s] - WAKE for s in succ[i]], default=0.0) - min(ops[i]["c"].values()) - ops[i]["lat"]
-    both = [i for i in range(n) if len(ops[i]["c"]) > 1]
-    other = {"s": "v", "v": "s"}
-    best = now = twice(way, ["".join(o["c"]) for o in ops])
-    hold = held(*now)
-    for p in range(PASSES):
-        key, side = list(now[0]), list(now[2])
-        u, v = draw(), draw()
-        if u < 0.6 and hold:
-            a, b = hold[int(draw() * len(hold))]
-            if v < 0.3 and len(ops[a]["c"]) > 1: side[a] = other[side[a]]
-            elif v < 0.5 and len(ops[b]["c"]) > 1: side[b] = other[side[b]]
-            elif v < 0.75: key[a] = key[b] + draw() * REACH
-            else: key[a] -= 2 * draw() * REACH
-        elif u < 0.76:
-            i = both[int(v * len(both))]
-            side[i] = other[side[i]]
-        else: key[int(v * n)] += REACH * (2 * draw() - 1)
-        new = twice(key, side)
-        if max(new[1]) <= max(now[1]) + SLACK * (1 - p / PASSES) * draw() ** 2:
-            now, hold = new, held(*new)
-            if max(now[1]) < max(best[1]): best = now
-    PLAN["seq"], PLAN["done"] = sorted((best[0][i], i, best[2][i]) for i in range(n)), best[1]
+        return ((state[0] >> 11) + 1) / 2.0 ** 53
+
+    def held(i, inside):
+        out = []
+        while i in inside and by[i] in inside:
+            if by[i] not in pre[i]: out.append((by[i], i))
+            i = by[i]
+        return out
+
+    def moved(part, i, d):
+        k = 1 + int(draw() ** 2 * REACH)
+        x = at = part.index(i)
+        near = succ if d > 0 else pre
+        block, keep, go = set(near[i]), [], [i]
+        while k and 0 <= x + d < len(part):
+            x += d
+            j = part[x]
+            if j in block:
+                go.append(j)
+                block.update(near[j])
+            else:
+                keep.append(j)
+                k -= on[j] == on[i]
+        return (at, part[:at] + keep + go + part[x + 1:]) if d > 0 else (x, part[:x] + go[::-1] + keep[::-1] + part[at + 1:])
+    best = None
+    for sweep in range(SWEEPS + 1):
+        slack = SLACK[0] * (SLACK[1] / SLACK[0]) ** (sweep / max(SWEEPS, 1))
+        for a in range(-int(draw() * WIDTH / 2), n, WIDTH // 2):
+            lo, hi = max(a, 0), min(n, a + WIDTH)
+            end = run(seq, [0.0] * 6, zero, [0.0] * 6)[0]
+            if best is None or end < best[0]: best = (end, list(seq), list(on))
+            if sweep == SWEEPS: break
+            seq.sort(key=lambda i: st[i])
+            rest, first = [0.0] * n, [0.0] * 6
+            for i in seq[hi:][::-1]:
+                rest[i] = tail[i] + max([rest[s] for s in succ[i]], default=0.0)
+                if on[i] != 5: rest[i] = first[on[i]] = cost[i][on[i]] + max(rest[i], first[on[i]])
+            beyond = [max([rest[s] for s in succ[i]], default=0.0) for i in range(n)]
+            free = run(seq[:lo], [0.0] * 6, zero, [0.0] * 6)[2]
+            floor = max([ready[i] + beyond[i] for i in seq[:lo]], default=0.0)
+            part = seq[lo:hi]
+            inside, both = set(part), [i for i in part if len(cost[i]) > 1]
+            now, who, _ = run(part, free, beyond, first)
+            now, hold, before = max(now, floor), held(who, inside), states(part, free)
+            for _ in range(TRIES):
+                u, v, flip = draw(), draw(), None
+                if u < 0.7 and hold:
+                    x, y = hold[int(draw() * len(hold)) % len(hold)]
+                    if v < 0.25 and len(cost[x]) > 1: flip = x
+                    elif v < 0.4 and len(cost[y]) > 1: flip = y
+                    else: at, new = moved(part, x, 1) if v < 0.6 else moved(part, y if v < 0.8 else x, -1)
+                elif u < 0.79 and both: flip = both[int(v * len(both)) % len(both)]
+                else: at, new = moved(part, part[int(v * len(part)) % len(part)], 1 if draw() < 0.5 else -1)
+                if flip is not None:
+                    at, new, w = part.index(flip), part, draw()
+                    flip = [flip] + ([j for j in part[max(0, at - NEAR):at + NEAR] if len(cost[j]) > 1 and on[j] != on[flip]] if w < PAIR else [])
+                    if len(flip) > 1: flip = [flip[0], flip[1 + int(draw() * (len(flip) - 1)) % (len(flip) - 1)]]
+                    for j in flip: on[j] = 1 - on[j]
+                    if w > 1 - PAIR: at, new = moved(part, flip[0], 1 if draw() < 0.5 else -1)
+                    at = min([at] + [part.index(j) for j in flip])
+                if within(new[at:], before[at], beyond, first, now - slack * math.log(draw())):
+                    end, who, _ = run(new, free, beyond, first)
+                    now, hold, part = max(end, floor), held(who, inside), sorted(new, key=lambda i: st[i])
+                    before = states(part, free)
+                else:
+                    for j in flip or []: on[j] = 1 - on[j]
+            seq[lo:hi] = part
+    seq, on[:] = best[1], best[2]
+    run(seq, [0.0] * 6, zero, [0.0] * 6)
+    PLAN["seq"], PLAN["done"] = sorted((st[i], i, QUEUES[on[i]]) for i in range(n)), ready
     return PLAN["seq"], PLAN["done"]
 
 
@@ -235,12 +295,13 @@ def rank_program(g, core, T, topo):
             d[nm] = top[buf]
             top[buf] += (w + unit - 1) // unit * unit
         o = d[nm]
+        assert top[buf] <= SCRATCH[buf][1][1], buf
         b = w if b is None else b
         return T[buf][:, o + a:o + b:s] if s else T[buf][:, o + a:o + b]
 
     def F(nm, w=C, a=0, b=None, s=None): return view("rowf", C, nm, w, a, b, s)
     def B(nm, w=C, a=0, b=None, s=None): return view("rowb", C, nm, w, a, b, s)
-    def tf(nm, w=20, a=0, b=None, s=None): return view("tabf", 20, nm, w, a, b, s)
+    def tf(nm, w=20, a=0, b=None, s=None): return view("tabf", 8, nm, w, a, b, s)
     def ti(nm, w=20, a=0, b=None): return view("tabi", 20, nm, w, a, b, None)
     def tu(nm, w=20, a=0, b=None): return view("tabu", 20, nm, w, a, b, None)
 
@@ -282,22 +343,24 @@ def rank_program(g, core, T, topo):
             return g.vector.tensor_scalar(out, in_, a, b, A.mult, A.add)
         return either(call, rd, wr, ind, n, half)
 
-    def gather(row, nm, win, lst, rd, halves):
-        if not halves: return move(row(nm), win.indirect(lst(0, 20)), rd, [nm + "0", nm + "1"], ind=True)
-        for q in range(2): move(row(nm, C, q * C // 2, q * C // 2 + C // 2), win.indirect(lst(10 * q, 10 * q + 10)), rd, [nm + str(q)], ind=True, n=C // 2)
+    def gather(row, nm, win, lst, rd, halves, line=None):
+        for a, b, wr in ((0, 10, [nm + "0"]), (10, 20, [nm + "1"])) if halves else ((0, 20, [nm + "0", nm + "1"]),):
+            out, in_ = row(nm, C, 16 * a, 16 * b), win.indirect(lst(a, b))
+            if line: affine(out, in_, line[0], line[1], rd, wr, ind=True, n=16 * (b - a))
+            else: move(out, in_, rd, wr, ind=True, n=16 * (b - a))
 
-    def shift(out, in_, x, rd, wr):
+    def shift(out, in_, x, rd, wr, n=C):
         def call(e):
             if e == "s": return g.scalar.activation(out, in_, AF.Identity, bias=x)
             return g.vector.tensor_scalar(out, in_, x, None, A.add)
-        return either(call, rd, wr, False)
+        return either(call, rd, wr, False, n)
 
     def quant(q, s, in_, n, rd, wr): return add(P, {"v": (12 + 0.22 * 4 * n) * CY / 0.83}, lambda e: g.vector.quantize_mx(q, s, in_), rd, wr)
 
-    def bank(b): return T.ps[:, 512 * b:512 * b + C]
+    def bank(b, lo=0, hi=C): return T.ps[:, 512 * b + lo:512 * b + hi]
 
-    def mm(b, w, ws, x, xs, rd):
-        return add(P, {"t": 1.4 * 0.83 * (C + 16)}, lambda e: g.tensor.matmul_mx(bank(b), w, ws, x, xs, True, True), rd, ["ps%d" % b])
+    def mm(b, w, ws, x, xs, rd, n=C):
+        return add(P, {"t": PE * (n + 16)}, lambda e: g.tensor.matmul_mx(bank(b, 0, n), w, ws, x, xs, True, True), rd, ["ps%d" % b])
 
     def load(q, nm, out, in_):
         return add(P, {q: 60.0}, lambda e: (g.sync if e == "y" else g.scalar).dma_start(out, in_), [], [nm], sem="ld_" + nm, lat=LOAD)
@@ -321,44 +384,44 @@ def rank_program(g, core, T, topo):
     pc = T.pcol
 
     def col(k): return T.pcolf[:, k:k + 1]
-    for b in range(4):
-        ts(pc[:, b + 1:b + 2], pc[:, 0:1], b, 1, A.logical_shift_right, A.bitwise_and, ["pcol"], ["pb%d" % b])
-        ts(col(b), pc[:, b + 1:b + 2], 2.0 ** (STEPB << b) - 1, 1.0, A.mult, A.add, ["pb%d" % b], ["pf%d" % b])
-    tt(col(4), col(0), col(1), A.mult, ["pf0", "pf1"], ["pf4"])
-    ts(col(5), col(2), 2.0 ** (102 - 15 * STEPB), None, A.mult, None, ["pf2"], ["pf5"])
-    tt(col(6), col(3), col(5), A.mult, ["pf3", "pf5"], ["pf6"])
-    tt(col(7), col(4), col(6), A.mult, ["pf4", "pf6"], ["sc"])
     SC, PLACE, ISC, BIG, BIG2, LOW, LOW2, KSW, LEAD, ROOT = [col(k) for k in range(7, 16)] + [16]
-    add(P, {"v": 200.0}, lambda e: g.vector.reciprocal(ISC, SC), ["sc"], ["isc"])
     ts(pc[:, 5:6], pc[:, 0:1], 15, None, A.bitwise_and, None, ["pcol"], ["p15"])
     vcopy(PLACE, pc[:, 5:6], ["p15"], ["p15f"])
+    ts(tf("fall", 20, 0, 16), B("jm", C, 0, 16), PLACE, 2.0 ** (-STEPB / 2), A.is_le, A.max, ["jm", "p15f"], ["fall"])
+    scan(tf("fell", 20, 0, 16), tf("fall", 20, 0, 16), tf("fall", 20, 0, 16), 2.0 ** 96, A.mult, A.mult, ["fall"], ["fell"], 16)
+    ts(SC, tf("fell", 20, 15, 16), 2.0 ** 6, None, A.mult, None, ["fell"], ["sc"])
+    add(P, {"v": 200.0}, lambda e: g.vector.reciprocal(ISC, SC), ["sc"], ["isc"])
     for out, a, b, nm in ((col(ROOT), RISE / UNIT, 0.25, "root0"), (col(ROOT + 1), RISE / UNIT, 1.25, "root1"), (LEAD, RISE / UNIT, MID + 0.125, "lead"),
                           (LOW, RISE, MID, "low"), (LOW2, RISE, MID * UNIT + 1, "low2"), (KSW, 2.0, 0.0, "ksw")):
-        ts(out, PLACE, a, b - 15 * a, A.mult, A.add, ["p15f"], [nm])
-    fill(col(18), 2.0 ** 51, ["b51"])
-    ts(BIG, col(18), 2.0 ** 51, None, A.mult, None, ["b51"], ["big"])
-    ts(BIG2, col(18), 2.0 ** 51 * UNIT, None, A.mult, None, ["b51"], ["big2"])
+        affine(out, PLACE, a, b - 15 * a, ["p15f"], [nm], n=64)
+    affine(col(18), PLACE, 0.0, 2.0 ** 51, ["p15f"], ["b51"], n=64)
+    move(BIG, col(18), ["b51"], ["big"], scale=2.0 ** 51, n=64)
+    move(BIG2, col(18), ["b51"], ["big2"], scale=2.0 ** 51 * UNIT, n=64)
     for q in range(2): ts(T.dcon[:, C * q:C * q + C], B("jm"), PLACE, 2.0 ** STEPB, A.is_gt, A.mult, ["jm", "p15f"], ["dcon%d" % q], C / 2)
     for nm, x in (("dkey", RISE * TINY), ("dgk", RISE * TINY / UNIT), ("dsw", 2.0)):
         affine(B(nm), T.dcon[:, 0:C], 33 * x / 2 ** STEPB, -32 * x, ["dcon0"], [nm], half=True)
     affine(F("lab"), B("iob"), UNIT, (MID * UNIT - MID - 1) * TINY, ["iob"], ["lab"])
-    fill(B("sum", 2 * C, 0, 16), -MID * TINY, ["sum"])
-    for nm in ("swk", "swgk"): fill(B(nm, 3 * C), 0.0, [nm], 3 * C / 2)
-    fill(tf("fd", 120), 0.0, ["fd1", "fd2"], 120)
+    if LATE: affine(F("lab2"), B("iob"), UNIT, (MID * UNIT + 65 - MID) * TINY, ["iob"], ["lab2"])
+    move(B("sum", 2 * C, 0, 1), B("iob", C, 0, 1), ["iob"], ["sum"], n=64)
+
+    def whole(out, x, wr, n=20): return iota(out, [[0, n]], int(x), 0, wr, n, True)
+    for nm in ("swk", "swgk"): whole(B(nm, 3 * C, 13, 3 * C, 16), 0, [nm], 60)
+    whole(tf("fd", 120, 0, 120, 3), 0, ["fd0"], 40)
     def ua(k): return tf("ua", 80, k, 80, 4)
     def ub(k): return tf("ub", 80, k, 80, 4)
     def va(k): return tf("va", 100, k, 100, 5)
     def vb(k): return tf("vb", 100, k, 100, 5)
-    fill(tf("ua", 80), 1.0, ["ua", "ua1"], 80)
-    for out, x, nm in ((ua(2), 1.0, "ua2"), (ub(2), -MID - 0.5, "ub2"), (ub(3), 0.25, "ub3")): ts(out, ua(0), ISC, x, A.mult, A.mult, ["ua", "isc"], [nm])
-    fill(ua(0), 0.0, ["ua"])
-    for k, x in ((0, 0.0), (2, 1.0), (3, -1.0)): fill(va(k), x, ["va%d" % k])
-    for k, x in ((1, -0.5), (2, WHOLE), (3, WHOLE)): fill(vb(k), x, ["vb%d" % k])
+    for out, x, nm in ((ua(0), 0, "ua0"), (ua(3), 1, "ua3"), (va(0), 0, "va0"), (va(2), 1, "va2"), (va(3), -1, "va3"), (vb(2), WHOLE, "vb2"), (vb(3), WHOLE, "vb3")):
+        whole(out, x, [nm])
+    move(ua(2), ua(3), ["ua3", "isc"], ["ua2"], scale=ISC, n=64)
+    for out, x, nm in ((ub(2), -MID - 0.5, "ub2"), (ub(3), 0.25, "ub3")): move(out, ua(2), ["ua2"], [nm], scale=x, n=64)
+    move(vb(1), ua(3), ["ua3"], ["vb1"], scale=-0.5, n=64)
+    def unit(b): return T.eq[:, 128 * b:128 * b + 128], T.es[:, 128 * b:128 * b + 128]
     fill(T.half[:], 0.5, ["half"], 256)
     for b in range(4):
         add(P, {"g": 170 + 1024 * CY}, lambda e, b=b: g.affine_select(T.et[:, 512 * b:512 * b + 512], T.half[:], [[1, 512]], A.is_equal, 0.0, -b, -4),
             ["half"], ["et%d" % b])
-        quant(T.eq[:, 128 * b:128 * b + 128], T.es[:, 128 * b:128 * b + 128], T.et[:, 512 * b:512 * b + 512], 128, ["et%d" % b], ["eq%d" % b])
+        quant(*unit(b), T.et[:, 512 * b:512 * b + 512], 128, ["et%d" % b], ["eq%d" % b])
 
     quant(T.xq0[:], T.xs0[:], T.xin[:], C, ["x"], ["X0"])
     vcopy(T.u16[:], T.ui[:], ["ui"], ["u16"])
@@ -376,12 +439,14 @@ def rank_program(g, core, T, topo):
 
     vcopy(tu("LG0", 40, 0, 20), T.fli[:], ["fl"], ["L0_0"])
     vcopy(tu("M16"), T.mli[:], ["ml"], ["M16"])
-    scatter(B("gl0").indirect(tu("LG0", 40, 0, 20)), B("iob"), ["L0_0", "iob"], ["gl0"])
-    compact(tu("LG0", 40, 20, 40), "gl0", MID + 0.25, ["gl0"], ["GL_0"])
     move(B("mr"), B("iob").indirect(tu("M16")), ["iob", "M16"], ["mr"], ind=True)
-    tt(F("sgd"), B("mr"), B("iob"), A.subtract, ["mr", "iob"], ["sgd"], C)
-    act(F("sg"), F("sgd"), AF.Sign, ["sgd"], ["sg"], scale=2.0 ** 97)
+    iota(ti("blk"), [[16, 20]], 0, 0, ["blk"], 20, False)
+    tt(tf("md"), T.mli[:], ti("blk"), A.subtract, ["ml", "blk"], ["md"])
+    ts(tu("up"), tf("md"), PLACE, None, A.is_gt, None, ["md", "p15f"], ["up16"])
+    affine(F("sg"), B("jm").indirect(tu("up")), 2.0, -1.0, ["jm", "up16"], ["sg"], ind=True)
 
+    ends = [[(0, 0, C)], [(0, 0, TAIL), (1, TAIL, C)]]
+    mids = [[(0, 0, C)], [(0, 0, LAYER), (1, LAYER, C)]]
     sent = [0]
     peers = [T.cores[rank ^ m] for m in MASKS]
     common = [e for e in topo.engines(core, peers[0]) if all(e in topo.engines(core, p) and e in topo.engines(p, core) for p in peers)]
@@ -395,19 +460,19 @@ def rank_program(g, core, T, topo):
         def send(sem, pieces, rd, key, lat, engines):
             msk, ne = sum(1 << e for e in engines), len(engines)
             for dst, src in pieces:
-                last = add(P, {"g": 300.0}, lambda e, dst=dst, src=src, sem=sem, rid=rid, pid=pid, msk=msk: g.remote_dma(dst, src, T.sem[sem], T.sem.rl, pid, rid, msk),
-                           rd, ["net"], sem="rl", val=0)
+                last = add(P, {"g": ISSUE}, lambda e, dst=dst, src=src, sem=sem, rid=rid, pid=pid, msk=msk: g.remote_dma(dst, src, T.sem[sem], T.sem.rl, pid, rid, msk),
+                           rd, ["net" + key], sem="rl", val=0)
                 sent[0] += ne
             add(P, {"n": 0.0}, None, [], [key], sem=sem, val=ne * len(pieces), after=[last], lat=lat)
 
-        def send_codes():
-            send("aq%d" % r, [(T["lq%d" % r][:].bitcast(dt.uint8), Xq[:].bitcast(dt.uint8)), (T["ls%d" % r][:], Xs[:])], [X], "Y%d" % r, CODES, common[0::2])
-        if r == 0: send_codes()
+        def send_codes(rd):
+            send("aq%d" % r, [(T["lq%d" % r][:].bitcast(dt.uint8), Xq[:].bitcast(dt.uint8)), (T["ls%d" % r][:], Xs[:])], [X] + rd, "Y%d" % r, CODES, common[0::2])
+        if r == 0: send_codes([])
 
         mm(0, T.up[:], T.ups[:], Xq[:], Xs[:], ["up", "ups", X])
         move(F(R("s")), bank(0), ["ps0"], [R("s")])
         for b in range(4):
-            mm(1 + b, T.eq[:, 128 * b:128 * b + 128], T.es[:, 128 * b:128 * b + 128], Xq[:], Xs[:], ["eq%d" % b, X])
+            mm(1 + b, *unit(b), Xq[:], Xs[:], ["eq%d" % b, X])
             move(T["fh%d" % h][:, C * b:C * b + C], bank(1 + b), ["ps%d" % (1 + b)], ["fh%d%d" % (h, b)])
 
         LG, LN = "LG%d" % r, "LG%d" % (r + 1)
@@ -416,22 +481,30 @@ def rank_program(g, core, T, topo):
         L = [FL] + [R("L%d" % k) for k in range(1, 8)]
         lists = [fl_] + [tu(k) for k in L[1:]]
         first, ahead = R("first"), 64 - MID
-        affine(F(first), B("iob").indirect(fl_), UNIT, (UNIT * MID + ahead) * TINY, ["iob", FL], [first], ind=True)
+        gather(F, first, B("iob"), lambda a, b: tu(LG, 40, a, b), ["iob", FL], "first" in HALVES, (UNIT, (UNIT * MID + ahead) * TINY))
 
-        def image(out, lst, rd, wr): affine(out, F(first).indirect(lst), 1 / UNIT, (-MID - ahead / UNIT) * TINY, [first] + rd, wr, ind=True)
+        def image(out, lst, rd, wr, n=C):
+            affine(out, F(first).indirect(lst), 1 / UNIT, (-MID - ahead / UNIT) * TINY, [first + "0", first + "1"] + rd, wr, ind=True, n=n)
+        m = PARTS[r]
+        parts = [(q, q * C // m, (q + 1) * C // m) for q in range(m)]
+        every = lambda nm: [nm + str(q) for q in range(m)]
         key = first
         for k in range(8):
-            if k < 7:
-                nx = R("fr%d" % (k + 1))
-                if k: move(B(nx), B(R("fr%d" % k)).indirect(lists[k]), [R("fr%d" % k), L[k]], [nx], ind=True)
-                else: image(B(nx), fl_, [FL], [nx])
-                compact(lists[k + 1], nx, MID + 0.25, [nx], [L[k + 1]])
-            w, nx = "w%d" % (k % 2), "key%d" % (k % 2)
-            shift(F(w), F(key), 2.0 ** k * TINY, [key], [w])
+            for q, a, b in parts if k < 7 else []:
+                fr, nx = R("fr%d" % k), R("fr%d" % (k + 1))
+                if k: move(B(nx, C, a, b), B(fr).indirect(tu(L[k], 20, a // 16, b // 16)), every(fr) + [L[k] + str(q)], [nx + str(q)], ind=True, n=b - a)
+                else: image(B(nx, C, a, b), tu(LG, 40, a // 16, b // 16), [FL], [nx + str(q)], b - a)
+                scan(B(nx + "k", C, a, b), T.dcon[:, a:b], B(nx, C, a, b), 0.0, A.mult, A.add, [nx + str(q), "dcon0"], [nx + "k" + str(q)], b - a, True)
+                ts(tu(L[k + 1], 20, a // 16, b // 16), B(nx + "k", C, a + 15, b, 16), SC, MID + 0.25, A.mult, A.add, [nx + "k" + str(q), "sc"], [L[k + 1] + str(q)])
+            w, nx, have = "w%d" % (k % 2), "key%d" % (k % 2), [key] if k else [first + "0", first + "1"]
+            if k == 0 and r in LATE:
+                tt(F(nx), F("lab2").indirect(lists[1]), F(key), A.min, ["lab2"] + have + every(L[1]), [nx], C, True)
+            else:
+                for q, a, b in parts: shift(F(w, C, a, b), F(key, C, a, b), 2.0 ** k * TINY, have, [w + str(q)] if m > 1 else [w + "0", w + "1"], b - a)
+                tt(F(nx), F(w).indirect(lists[k]), F(key), A.min, [w + "0", w + "1"] + have + (every(L[k]) if k else [FL]), [nx], C, True)
             if k == 6: shift(F("near"), F(key), -64 * TINY, [key], ["near"])
-            tt(F(nx), F(w).indirect(lists[k]), F(key), A.min, [w, L[k], key], [nx], C, True)
             key = nx
-        tt(F("key"), F(key).indirect(lists[6]), F("near"), A.min, [key, L[6], "near"], ["key"], C, True)
+        tt(F("key"), F(key).indirect(lists[6]), F("near"), A.min, [key, "near"] + every(L[6]), ["key"], C, True)
         key = "key"
 
         sa, sb, SA, O16 = T["sa%d" % r], T["sb%d" % r], "sa%d" % r, "sb%d" % r
@@ -451,24 +524,32 @@ def rank_program(g, core, T, topo):
         compact(sa[:, 60:80], "end", MID + 0.25, ["end"], [SA + "e"])
         tt(tf("nraw"), kept("end"), kept("base"), A.subtract, ["basek", "endk"], ["nraw"])
         ts(sa[:, 0:20], tf("nraw"), SC, 0.25, A.mult, A.add, ["nraw", "sc"], [SA + "n"])
-        send("aa%d" % r, [(T["la%d" % r][:], sa[:, 0:60])], [SA + "n", SA + "c", SA + "p"], "la%d" % r, LISTS, common[1::2])
-        if r: send_codes()
+        send("aa%d" % r, [(T["la%d" % r][:], sa[:, 0:60])], [SA + "n", SA + "c", SA + "p"], "la%d" % r, LISTS, common)
+        if r: send_codes(["netla%d" % r])
         ts(ua(1), sa[:, 0:20], 1.0, None, A.add, None, [SA + "n"], ["ua1"])
         tt(tf("left"), ua(1), ti("ci"), A.subtract, ["ua1", "ci"], ["left"])
         ol = R("ol")
         scatter(B(ol).indirect(sa[:, 40:60]), B("iob"), [SA + "p", "iob"], [ol])
         compact(sb[:], ol, MID + 0.25, [ol], [O16])
-        send("ab%d" % r, [(T["lb%d" % r][:], sb[:])], [O16], "lb%d" % r, LISTS, common[1::2])
+        send("ab%d" % r, [(T["lb%d" % r][:], sb[:])], [O16], "lb%d" % r, ORDER, common[1::2])
+        if r == 0:
+            ts(tf("wrap"), tf("left"), 1.5, ISC, A.is_lt, A.mult, ["left", "isc"], ["wrap"])
+            tt(tf("back"), tf("wrap"), ua(1), A.mult, ["wrap", "ua1"], ["back"])
+            tt(tf("next"), tf("praw"), tf("back"), A.subtract, ["praw", "back"], ["next"])
+            ts(tu("N16"), tf("next"), SC, MID + 1.25, A.mult, A.add, ["next", "sc"], ["N16"])
+            move(B("gl0"), B(ol).indirect(tu("N16")), [ol, "N16"], ["gl0"], ind=True)
+            compact(gl_, "gl0", MID + 0.25, ["gl0"], [GL])
         act(B(R("flag")), B("iob").indirect(sa[:, 20:40]), AF.Relu, ["iob", SA + "c"], [R("flag")], scale=-2.0 ** 97, bias=(1.0 - MID) * TINY * 2.0 ** 97, ind=True)
         move(B(R("d0")), B(R("flag")).indirect(sb[:]), [R("flag"), O16], [R("d0")], scale=-2.0 ** 97, ind=True)
         affine(B(R("d1")), B(R("d0")), -1.0, TINY / UNIT, [R("d0")], [R("d1")], half=True)
         fg = R("fg")
         image(B(fg, 2 * C, 0, C), tu("M16"), ["M16"], [fg + "f"])
         move(B(fg, 2 * C, C, 2 * C), B("mr").indirect(gl_), ["mr", GL], [fg + "g"], ind=True)
-        compact(tf("fgv", 40), fg, MID + 0.25, [fg + "f", fg + "g"], ["fgv"], 2)
+        compact(None, fg, 0.0, [fg + "f", fg + "g"], None, 2)
+        affine(tf("fgv", 40), B(fg + "k", 2 * C, 15, 2 * C, 16), SC, MID + 0.25, [fg + "k", "sc"], ["fgv"], n=64)
         ts(tf("fg0", 40), tu(LG, 40), 0.25, None, A.add, None, [FL, GL], ["fg0"], 40)
         tt(tf("fd", 120, 1, 120, 3), tf("fgv", 40), tf("fg0", 40), A.subtract, ["fgv", "fg0"], ["fd1"], 40)
-        ts(tf("fgk", 40), tf("fd", 120, 1, 120, 3), KSW, None, A.mult, None, ["fd1", "ksw"], ["fgk"], 40)
+        move(tf("fgk", 40), tf("fd", 120, 1, 120, 3), ["fd1", "ksw"], ["fgk"], scale=KSW, n=64)
         tt(tf("fd", 120, 2, 120, 3), tf("fgk", 40), tf("fg0", 40), A.add, ["fgk", "fg0"], ["fd2"], 40)
 
         gather(F, "so", F(R("s")), lambda a, b: sb[:, a:b], [R("s"), O16], "so" in HALVES)
@@ -484,7 +565,7 @@ def rank_program(g, core, T, topo):
         ts(ti("lj"), ti("li"), int(UNIT) - 1, None, A.bitwise_and, None, ["li"], ["lj"])
         tt(ub(1), tf("left"), ti("lj"), A.subtract, ["left", "lj"], ["ub1"])
         ts(ub(0), ub(1), -0.5, None, A.is_lt, None, ["ub1"], ["ub0"])
-        scan(tf("uo", 80), tf("ua", 80), tf("ub", 80), 0.0, A.mult, A.add, ["ua", "ua1", "ua2"] + ["ub%d" % k for k in range(4)], ["uo"], 80)
+        scan(tf("uo", 80), tf("ua", 80), tf("ub", 80), 0.0, A.mult, A.add, ["u%s%d" % (x, k) for x in "ab" for k in range(4)], ["uo"], 80)
 
         xa, lb, LB = R("xa"), T["lb%d" % r][:], "lb%d" % r
         for q in range(3):
@@ -492,12 +573,12 @@ def rank_program(g, core, T, topo):
         move(B(R("oe")), B("iob").indirect(lb), ["iob", LB], [R("oe")], ind=True)
         move(F("se"), F(R("s")).indirect(lb), [R("s"), LB], ["se"], ind=True)
         for q, nm in enumerate(("xn", "xc", "xb")):
-            move(B(nm), B(xa, 3 * C, C * q, C * q + C).indirect(tu(l16)), [xa + str(q), l16], [nm], ind=True)
-        compact(ti("xni"), "xn", MID + 1.0, ["xn"], ["xni"])
+            gather(B, nm, B(xa, 3 * C, C * q, C * q + C), lambda a, b: tu(l16, 20, a, b), [xa + str(q), l16], nm in HALVES)
+        compact(ti("xni"), "xn", MID + 1.0, ["xn0", "xn1"], ["xni"])
         ts(va(4), ti("xni"), ISC, None, A.mult, None, ["xni", "isc"], ["va4"])
         add(P, {"v": 190 + 120 * CY}, lambda e: g.vector.reciprocal(va(1), va(4)), ["va4"], ["va1"])
         for k, nm in ((0, "xc"), (4, "xb")):
-            compact(None, nm, 0.0, [nm], None)
+            compact(None, nm, 0.0, [nm + "0", nm + "1"], None)
             tt(vb(k), kept(nm), tf("uo", 80, 2 + k // 4, 80, 4), A.subtract, [nm + "k", "uo"], ["vb%d" % k])
         scan(tf("vo", 100), tf("va", 100), tf("vb", 100), 0.0, A.mult, A.add, ["va%d" % k for k in range(5)] + ["vb%d" % k for k in range(5)], ["vo"], 100)
         PL, T16 = R("PL"), R("T16")
@@ -510,44 +591,57 @@ def rank_program(g, core, T, topo):
             a, b = C // 2 * c, C // 2 * c + C // 2
             move(F("su", C, a, b), F("st", C, a, b), ["st"], ["su" + "ab"[c]], scale=-1.0, n=C // 2)
         tt(B("sw"), F("st").indirect(tu("M16")), F("su"), A.is_lt, ["st", "sua", "sub", "M16"], ["sw"], C, True)
-        move(B("swg"), B("sw").indirect(gl_), ["sw", GL], ["swg"], ind=True)
-        for nm, a, out, kk in (("sw", 0, fn_, FN), ("swg", 60, gn_, GN)):
+
+        def choose(nm, pairs, rd, out, wr):
             scan(B(nm + "k", 3 * C, 0, 3 * C, 3), B("dsw"), B(nm), 0.0, A.add, A.max, ["dsw", nm], [nm + "k"], C, True)
-            scan(tf(nm + "o", 60), B(nm + "k", 3 * C, 13, 3 * C, 16), tf("fd", 120, a, a + 60), 0.0, A.mult, A.add, [nm + "k", "fd1", "fd2"], [nm + "o"], 60)
-            vcopy(out, tf(nm + "o", 60, 2, 60, 3), [nm + "o"], [kk])
+            scan(tf(nm + "o", 60), B(nm + "k", 3 * C, 13, 3 * C, 16), pairs, 0.0, A.mult, A.add, [nm + "k"] + rd, [nm + "o"], 60)
+            vcopy(out, tf(nm + "o", 60, 2, 60, 3), [nm + "o"], [wr])
+        move(B("swg"), B("sw").indirect(gl_), ["sw", GL], ["swg"], ind=True)
+        for nm, a, out, kk in (("sw", 0, fn_, FN), ("swg", 60, gn_, GN)): choose(nm, tf("fd", 120, a, a + 60), ["fd0", "fd1", "fd2"], out, kk)
 
         fh, fs, gp, zt, xt, rs = [T["%s%d" % (k, h)] for k in ("fh", "fs", "gp", "zt", "xt", "rs")]
         for b in range(4):
             bk, c = (5, 6, 7, 0)[b], slice(C * b, C * b + C)
-            mm(bk, T.eq[:, 128 * b:128 * b + 128], T.es[:, 128 * b:128 * b + 128], T["lq%d" % r][:], T["ls%d" % r][:], ["eq%d" % b, "Y%d" % r])
+            mm(bk, *unit(b), T["lq%d" % r][:], T["ls%d" % r][:], ["eq%d" % b, "Y%d" % r])
             move(fs[:, c], bank(bk), ["ps%d" % bk], ["fs%d%d" % (h, b)])
-            move(gp[:, c], fs[:, c].indirect(tu(T16)), ["fs%d%d" % (h, b), T16], ["gp%d%d" % (h, b)], ind=True)
-            tt(zt[:, b:4 * C:4], fh[:, c].indirect(fn_), gp[:, c], A.add, ["fh%d%d" % (h, b), FN, "gp%d%d" % (h, b)], ["zt%d%d" % (h, b)], C, True)
+            for q, lo, hi in mids[r == ROUNDS - 1]:
+                part = slice(C * b + lo, C * b + hi)
+                move(gp[:, part], fs[:, c].indirect(tu(T16, 20, lo // 16, hi // 16)), ["fs%d%d" % (h, b), T16], ["gp%d%d%d" % (h, b, q)], ind=True, n=hi - lo)
+                tt(zt[:, 4 * lo + b:4 * hi:4], fh[:, c].indirect(tu(LN, 40, lo // 16, hi // 16)), gp[:, part], A.add,
+                   ["fh%d%d" % (h, b), FN, "gp%d%d%d" % (h, b, q)], ["zt%d%d%d" % (h, b, q)], hi - lo, True)
         zq, zs = T["zq%d" % h], T["zs%d" % h]
-        quant(zq[:], zs[:], zt[:], C, ["zt%d%d" % (h, b) for b in range(4)], ["zq%d" % h])
+        for q, lo, hi in mids[r == ROUNDS - 1]:
+            quant(zq[:, lo:hi], zs[:, lo:hi], zt[:, 4 * lo:4 * hi], hi - lo, ["zt%d%d%d" % (h, b, q) for b in range(4)], ["zq%d%d" % (h, q)])
         for b in range(4):
-            c = slice(C * b, C * b + C)
-            mm(1 + b, T.wq[:, 128 * b:128 * b + 128], T.wsc[:, 128 * b:128 * b + 128], zq[:], zs[:], ["wc", "ws", "zq%d" % h])
-            move(rs[:, c], bank(1 + b), ["ps%d" % (1 + b)], ["rs%d%d" % (h, b)], scale=2.0 ** -6)
-            if b < APART[r]:
-                bk = (5, 6, 7, 0)[b]
-                mm(bk, T.eq[:, 128 * b:128 * b + 128], T.es[:, 128 * b:128 * b + 128], Xq[:], Xs[:], ["eq%d" % b, X])
-                move(T.pp[:, c], rs[:, c].indirect(gn_), ["rs%d%d" % (h, b), GN], ["pp%d" % b], ind=True)
-                tt(xt[:, b:4 * C:4], T.pp[:, c], bank(bk), A.add, ["pp%d" % b, "ps%d" % bk], ["xt%d%d" % (h, b)], C / 2)
-            else:
-                tt(xt[:, b:4 * C:4], rs[:, c].indirect(gn_), fh[:, c], A.add, ["rs%d%d" % (h, b), GN, "fh%d%d" % (h, b)], ["xt%d%d" % (h, b)], C, True)
-        quant(T["xq%d" % (r + 1)][:], T["xs%d" % (r + 1)][:], xt[:], C, ["xt%d%d" % (h, b) for b in range(4)], ["X%d" % (r + 1)])
+            bk, c = (5, 6, 7, 0)[b], slice(C * b, C * b + C)
+            for q, lo, hi in mids[r == ROUNDS - 1]:
+                at = ((1, 2, 3, 4), (6, 7, 0, 1))[q][b]
+                mm(at, T.wq[:, 128 * b:128 * b + 128], T.wsc[:, 128 * b:128 * b + 128], zq[:, lo:hi], zs[:, lo:hi], ["wc", "ws", "zq%d%d" % (h, q)], hi - lo)
+                move(rs[:, C * b + lo:C * b + hi], bank(at, 0, hi - lo), ["ps%d" % at], ["rs%d%d%d" % (h, b, q)], scale=2.0 ** -6, n=hi - lo)
+            made = ["rs%d%d%d" % (h, b, q) for q, lo, hi in mids[r == ROUNDS - 1]] + [GN]
+            if b < APART[r]: mm(bk, *unit(b), Xq[:], Xs[:], ["eq%d" % b, X])
+            for q, lo, hi in ends[r == ROUNDS - 1]:
+                out, lst, part, xk = xt[:, 4 * lo + b:4 * hi:4], tu(LN, 40, 20 + lo // 16, 20 + hi // 16), slice(C * b + lo, C * b + hi), "xt%d%d%d" % (h, b, q)
+                if b < APART[r]:
+                    move(T.pp[:, part], rs[:, c].indirect(lst), made, ["pp%d%d" % (b, q)], ind=True, n=hi - lo)
+                    tt(out, T.pp[:, part], bank(bk, lo, hi), A.add, ["pp%d%d" % (b, q), "ps%d" % bk], [xk], (hi - lo) / 2)
+                else:
+                    tt(out, rs[:, c].indirect(lst), fh[:, part], A.add, made + ["fh%d%d" % (h, b)], [xk], hi - lo, True)
+        for q, lo, hi in ends[r == ROUNDS - 1]:
+            quant(T["xq%d" % (r + 1)][:, lo:hi], T["xs%d" % (r + 1)][:, lo:hi], xt[:, 4 * lo:4 * hi], hi - lo, ["xt%d%d%d" % (h, b, q) for b in range(4)],
+                  ["X%d" % (r + 1) + "ab"[q] * (r == ROUNDS - 1)])
 
-    q, s, X = T["xq%d" % ROUNDS], T["xs%d" % ROUNDS], "X%d" % ROUNDS
+    xq, xs, X = T["xq%d" % ROUNDS], T["xs%d" % ROUNDS], ["X%d" % ROUNDS + "ab"[q] for q, lo, hi in ends[1]]
 
     def store(nm, out, in_, rd): add(P, {"y": 60.0}, lambda e: g.sync.dma_start(out, in_), rd, [], sem="st_" + nm, lat=2000.0)
     affine(T.nls[:], B("iob").indirect(tu("LG%d" % ROUNDS, 40, 0, 20)), BIG, float(MID), ["iob", "big", "L0_%d" % ROUNDS], ["nls"], ind=True)
     store("nl", T.nl[:, :], T.nls[0:128:16, :], ["nls"])
-    mm(1, T.vq[:], T.vs[:], q[:], s[:], ["vq", X])
-    move(T.ys[:], bank(1), ["ps1"], ["ys"])
-    store("oc", T.oc[:, :], q[:].bitcast(dt.uint8), [X])
-    for k in range(4): store("os%d" % k, T.osc[4 * k:4 * k + 4, :], s[32 * k:32 * k + 4, :], [X])
-    store("y", T.y[:, :], T.ys[:], ["ys"])
+    for q, lo, hi in ends[1]:
+        mm(1 + q, T.vq[:], T.vs[:], xq[:, lo:hi], xs[:, lo:hi], ["vq", X[q]], hi - lo)
+        move(T.ys[:, lo:hi], bank(1 + q, 0, hi - lo), ["ps%d" % (1 + q)], ["ys%d" % q], n=hi - lo)
+    store("oc", T.oc[:, :], xq[:].bitcast(dt.uint8), X)
+    for k in range(4): store("os%d" % k, T.osc[4 * k:4 * k + 4, :], xs[32 * k:32 * k + 4, :], X)
+    store("y", T.y[:, :], T.ys[:], ["ys%d" % q for q, lo, hi in ends[1]])
 
     seq, done = order(P)
     count = emit(P, g, T, seq)

import math
from concourse.mybir import dt, AluOpType as A, ActivationFunctionType as AF

C = 320
ROUNDS = 3
MASKS = (1, 2, 4)
MID = 160
TINY = 2.0 ** -102
STEPB = 12
UNIT = 1024.0
RISE = 512 * UNIT
WHOLE = 1.5 * 2.0 ** 23

NF, NB, NT, NI, NU = 36, 110, 90, 18, 48
SCRATCH = {
    "rowf": ("sbuf", [128, C * NF], "float32"),
    "rowb": ("sbuf", [128, C * NB], "bfloat16"),
    "tabf": ("sbuf", [128, 20 * NT], "float32"),
    "tabi": ("sbuf", [128, 20 * NI], "int32"),
    "tabu": ("sbuf", [128, 20 * NU], "uint16"),
    "fli": ("sbuf", [128, 20], "int32"),
    "mli": ("sbuf", [128, 20], "int32"),
    "dcon": ("sbuf", [128, 2 * C], "bfloat16"),
    "pcol": ("sbuf", [128, 8], "int32"),
    "pcolf": ("sbuf", [128, 32], "float32"),
    "ui": ("sbuf", [128, 8], "int32"),
    "u16": ("sbuf", [128, 8], "uint16"),
    "half": ("sbuf", [128, 512], "bfloat16"),
    "et": ("sbuf", [128, 2048], "bfloat16"),
    "eq": ("sbuf", [128, 512], "float8_e4m3fn_x4"),
    "es": ("sbuf", [128, 512], "uint8"),
    "pp": ("sbuf", [128, 4 * C], "float32"),
    "uin": ("sbuf", [128, 512], "bfloat16"),
    "vin": ("sbuf", [128, 512], "bfloat16"),
    "xin": ("sbuf", [128, 4 * C], "bfloat16"),
    "uq": ("sbuf", [128, 128], "float8_e4m3fn_x4"),
    "us": ("sbuf", [128, 128], "uint8"),
    "up": ("sbuf", [128, 128], "float8_e4m3fn_x4"),
    "ups": ("sbuf", [128, 128], "uint8"),
    "vq": ("sbuf", [128, 128], "float8_e4m3fn_x4"),
    "vs": ("sbuf", [128, 128], "uint8"),
    "wq": ("sbuf", [128, 512], "float8_e4m3fn_x4"),
    "wsc": ("sbuf", [128, 512], "uint8"),
    "ys": ("sbuf", [128, C], "float32"),
    "nls": ("sbuf", [128, C], "float32"),
    "ps": ("psum", [128, 512 * 8], "float32"),
}
for _r in range(ROUNDS + 1):
    SCRATCH["xq%d" % _r] = ("sbuf", [128, C], "float8_e4m3fn_x4")
    SCRATCH["xs%d" % _r] = ("sbuf", [128, C], "uint8")
for _r in range(ROUNDS):
    SCRATCH["lq%d" % _r] = ("sbuf", [128, C], "float8_e4m3fn_x4")
    SCRATCH["ls%d" % _r] = ("sbuf", [128, C], "uint8")
    SCRATCH["la%d" % _r] = ("sbuf", [128, 60], "uint16")
    SCRATCH["lb%d" % _r] = ("sbuf", [128, 20], "uint16")
    SCRATCH["sa%d" % _r] = ("sbuf", [128, 80], "uint16")
    SCRATCH["sb%d" % _r] = ("sbuf", [128, 20], "uint16")
for _h in range(2):
    for _k in ("fh", "fs", "gp", "zt", "xt"): SCRATCH["%s%d" % (_k, _h)] = ("sbuf", [128, 4 * C], "bfloat16")
    SCRATCH["rs%d" % _h] = ("sbuf", [128, 4 * C], "float32")
    SCRATCH["zq%d" % _h] = ("sbuf", [128, C], "float8_e4m3fn_x4")
    SCRATCH["zs%d" % _h] = ("sbuf", [128, C], "uint8")

LOADS = ("fl", "ml", "x", "u", "v", "wc", "ws")
STORES = ("oc", "os0", "os1", "os2", "os3", "y", "nl")
SEMAPHORES = ["ev", "es", "et", "eg", "rl"] + ["ld_" + n for n in LOADS] + ["st_" + n for n in STORES] \
    + ["%s%d" % (k, r) for k in ("aq", "aa", "ab") for r in range(ROUNDS)]

HALVES = ("so", "gk")
PARTS = (2, 1, 1)
LATE = (1, 2)
APART = (4, 4, 2)
LAYER, TAIL = 192, 192

CY, GA, SA_, PE, WAKE, ISSUE = 0.83 * 1.25, 1.56, 3.8, 1.4 * 0.83, 140.0, 450.0
LOAD, LISTS, ORDER, CODES = 1800.0, 3000.0, 3700.0, 6400.0
SPARE, REACH, NEAR, PAIR, WIDTH, TRIES, SLACK, SWEEPS, SEED = 300.0, 12, 8, 0.33, 100, 300, (110.0, 8.0), 330, 7
PLAN = {}


def add(P, cost, call, reads, writes, sem=None, val=16, after=(), lat=0.0):
    i = len(P["ops"])
    deps = set(after)
    for k in reads:
        if k in P["last"]: deps.add(P["last"][k])
    for k in writes:
        deps.update(P["readers"].get(k, []))
        if k in P["last"]: deps.add(P["last"][k])
    for k in reads: P["readers"].setdefault(k, []).append(i)
    for k in writes:
        P["last"][k] = i
        P["readers"][k] = []
    P["ops"].append({"c": cost, "f": call, "d": sorted(deps), "sem": sem, "val": val, "lat": lat, "w": writes})
    return i


QUEUES = "vstgyn"


def lay(cost, tail, pre, way):
    n = len(cost)
    st, ready, on = [0.0] * n, [0.0] * n, [0] * n
    busy = [[] for _ in QUEUES]
    for i in sorted(range(n), key=lambda i: -way[i]):
        t, best = max([ready[j] for j in pre[i]], default=0.0), None
        for e, c in cost[i].items():
            a = t
            for x, y in busy[e]:
                if y > a and x < a + c: a = y
            if best is None or a + c + (SPARE if e == 0 else 0.0) < best[0]: best = (a + c + (SPARE if e == 0 else 0.0), a, c, e)
        _, st[i], c, on[i] = best
        if c: busy[on[i]] = sorted(busy[on[i]] + [(st[i], st[i] + c)])
        ready[i] = st[i] + c + tail[i]
    return sorted(range(n), key=lambda i: st[i]), on


def order(P):
    if "seq" in PLAN: return PLAN["seq"], PLAN["done"]
    ops = P["ops"]
    n = len(ops)
    cost = [{QUEUES.index(e): c for e, c in o["c"].items()} for o in ops]
    tail = [o["lat"] + WAKE for o in ops]
    pre, succ = [o["d"] for o in ops], [[] for _ in range(n)]
    for i in range(n):
        for j in pre[i]: succ[j].append(i)
    way = [0.0] * n
    for i in range(n - 1, -1, -1): way[i] = min(cost[i].values()) + tail[i] + max([way[s] for s in succ[i]], default=0.0)
    seq, on = lay(cost, tail, pre, way)
    ready, st, by, zero = [0.0] * n, [0.0] * n, [-1] * n, [0.0] * n

    def run(part, free, beyond, first):
        free, last = list(free), [-1] * 6
        end, who = 0.0, -1
        for i in part:
            e = on[i]
            t, b = free[e], last[e]
            for j in pre[i]:
                if ready[j] > t: t, b = ready[j], j
            by[i], st[i] = b, t
            if e != 5:
                t += cost[i][e]
                free[e], last[e] = t, i
            t += tail[i]
            ready[i] = t
            if t + beyond[i] > end: end, who = t + beyond[i], i
        for e in range(5):
            if free[e] + first[e] > end: end, who = free[e] + first[e], last[e]
        return end, who, free

    def states(part, free):
        free, out = list(free), []
        for i in part:
            out.append(tuple(free))
            if on[i] != 5: free[on[i]] = ready[i] - tail[i]
        return out

    def within(part, free, beyond, first, limit):
        free, mine = list(free), list(ready)
        for i in part:
            e = on[i]
            t = free[e]
            for j in pre[i]:
                if mine[j] > t: t = mine[j]
            if e != 5: free[e] = t = t + cost[i][e]
            t += tail[i]
            if t + beyond[i] > limit: return False
            mine[i] = t
        return all(free[e] + first[e] <= limit for e in range(5))
    state = [SEED]

    def draw():
        state[0] = (state[0] * 6364136223846793005 + 1442695040888963407) % 2 ** 64
        return ((state[0] >> 11) + 1) / 2.0 ** 53

    def held(i, inside):
        out = []
        while i in inside and by[i] in inside:
            if by[i] not in pre[i]: out.append((by[i], i))
            i = by[i]
        return out

    def moved(part, i, d):
        k = 1 + int(draw() ** 2 * REACH)
        x = at = part.index(i)
        near = succ if d > 0 else pre
        block, keep, go = set(near[i]), [], [i]
        while k and 0 <= x + d < len(part):
            x += d
            j = part[x]
            if j in block:
                go.append(j)
                block.update(near[j])
            else:
                keep.append(j)
                k -= on[j] == on[i]
        return (at, part[:at] + keep + go + part[x + 1:]) if d > 0 else (x, part[:x] + go[::-1] + keep[::-1] + part[at + 1:])
    best = None
    for sweep in range(SWEEPS + 1):
        slack = SLACK[0] * (SLACK[1] / SLACK[0]) ** (sweep / max(SWEEPS, 1))
        for a in range(-int(draw() * WIDTH / 2), n, WIDTH // 2):
            lo, hi = max(a, 0), min(n, a + WIDTH)
            end = run(seq, [0.0] * 6, zero, [0.0] * 6)[0]
            if best is None or end < best[0]: best = (end, list(seq), list(on))
            if sweep == SWEEPS: break
            seq.sort(key=lambda i: st[i])
            rest, first = [0.0] * n, [0.0] * 6
            for i in seq[hi:][::-1]:
                rest[i] = tail[i] + max([rest[s] for s in succ[i]], default=0.0)
                if on[i] != 5: rest[i] = first[on[i]] = cost[i][on[i]] + max(rest[i], first[on[i]])
            beyond = [max([rest[s] for s in succ[i]], default=0.0) for i in range(n)]
            free = run(seq[:lo], [0.0] * 6, zero, [0.0] * 6)[2]
            floor = max([ready[i] + beyond[i] for i in seq[:lo]], default=0.0)
            part = seq[lo:hi]
            inside, both = set(part), [i for i in part if len(cost[i]) > 1]
            now, who, _ = run(part, free, beyond, first)
            now, hold, before = max(now, floor), held(who, inside), states(part, free)
            for _ in range(TRIES):
                u, v, flip = draw(), draw(), None
                if u < 0.7 and hold:
                    x, y = hold[int(draw() * len(hold)) % len(hold)]
                    if v < 0.25 and len(cost[x]) > 1: flip = x
                    elif v < 0.4 and len(cost[y]) > 1: flip = y
                    else: at, new = moved(part, x, 1) if v < 0.6 else moved(part, y if v < 0.8 else x, -1)
                elif u < 0.79 and both: flip = both[int(v * len(both)) % len(both)]
                else: at, new = moved(part, part[int(v * len(part)) % len(part)], 1 if draw() < 0.5 else -1)
                if flip is not None:
                    at, new, w = part.index(flip), part, draw()
                    flip = [flip] + ([j for j in part[max(0, at - NEAR):at + NEAR] if len(cost[j]) > 1 and on[j] != on[flip]] if w < PAIR else [])
                    if len(flip) > 1: flip = [flip[0], flip[1 + int(draw() * (len(flip) - 1)) % (len(flip) - 1)]]
                    for j in flip: on[j] = 1 - on[j]
                    if w > 1 - PAIR: at, new = moved(part, flip[0], 1 if draw() < 0.5 else -1)
                    at = min([at] + [part.index(j) for j in flip])
                if within(new[at:], before[at], beyond, first, now - slack * math.log(draw())):
                    end, who, _ = run(new, free, beyond, first)
                    now, hold, part = max(end, floor), held(who, inside), sorted(new, key=lambda i: st[i])
                    before = states(part, free)
                else:
                    for j in flip or []: on[j] = 1 - on[j]
            seq[lo:hi] = part
    seq, on[:] = best[1], best[2]
    run(seq, [0.0] * 6, zero, [0.0] * 6)
    PLAN["seq"], PLAN["done"] = sorted((st[i], i, QUEUES[on[i]]) for i in range(n)), ready
    return PLAN["seq"], PLAN["done"]


def emit(P, g, T, seq):
    ops = P["ops"]
    queue = {"v": g.vector, "s": g.scalar, "t": g.tensor, "g": g, "y": g.sync}
    name = {"v": "ev", "s": "es", "t": "et", "g": "eg"}
    count = {e: 0 for e in name}
    know = {e: {} for e in queue}
    clock, own = {}, {}
    for st, i, e in seq:
        o = ops[i]
        if e == "n":
            clock[i], own[i] = {o["sem"]: o["val"]}, (o["sem"], o["val"])
            continue
        want = {}
        for j in o["d"]:
            s, v = own[j]
            if v and know[e].get(s, 0) < v: want[s] = max(want.get(s, 0), v)
        for j in o["d"]:
            s, v = own[j]
            if want.get(s, 0) >= v > 0:
                for k, x in clock[j].items():
                    if k != s and k in want and want[k] <= x: del want[k]
        for s, v in want.items():
            queue[e].wait_ge(T.sem[s], v)
            know[e][s] = v
        for j in o["d"]:
            for k, x in clock[j].items(): know[e][k] = max(know[e].get(k, 0), x)
        ins = o["f"](e)
        clock[i] = dict(know[e])
        if o["sem"] is None:
            count[e] += 1
            own[i] = (name[e], count[e])
            ins.then_inc(T.sem[name[e]], 1)
        else:
            own[i] = (o["sem"], o["val"])
            if o["val"]: ins.then_inc(T.sem[o["sem"]], o["val"])
        if own[i][1]: clock[i][own[i][0]] = own[i][1]
    return count


def rank_program(g, core, T, topo):
    rank = T.rank_of(core)
    if rank is None: return
    P = {"ops": [], "last": {}, "readers": {}}
    slots = {"rowf": {}, "rowb": {}, "tabf": {}, "tabi": {}, "tabu": {}}
    top = {k: 0 for k in slots}

    def view(buf, unit, nm, w, a, b, s):
        d = slots[buf]
        if nm not in d:
            d[nm] = top[buf]
            top[buf] += (w + unit - 1) // unit * unit
        o = d[nm]
        assert top[buf] <= SCRATCH[buf][1][1], buf
        b = w if b is None else b
        return T[buf][:, o + a:o + b:s] if s else T[buf][:, o + a:o + b]

    def F(nm, w=C, a=0, b=None, s=None): return view("rowf", C, nm, w, a, b, s)
    def B(nm, w=C, a=0, b=None, s=None): return view("rowb", C, nm, w, a, b, s)
    def tf(nm, w=20, a=0, b=None, s=None): return view("tabf", 8, nm, w, a, b, s)
    def ti(nm, w=20, a=0, b=None): return view("tabi", 20, nm, w, a, b, None)
    def tu(nm, w=20, a=0, b=None): return view("tabu", 20, nm, w, a, b, None)

    def vec(n): return max(64.0, n) * CY
    def gat(e, n): return (50.0 if e == "v" else 65.0) + n * CY * GA

    def ts(out, in0, s1, s2, op0, op1, rd, wr, n=20):
        def call(e): return g.vector.tensor_scalar(out, in0, s1, None, op0) if op1 is None else g.vector.tensor_scalar(out, in0, s1, s2, op0, op1)
        return add(P, {"v": vec(n)}, call, rd, wr)

    def tt(out, a, b, op, rd, wr, n=20, ind=False):
        return add(P, {"v": gat("v", n) if ind else vec(2 * n)}, lambda e: g.vector.tensor_tensor(out, a, b, op), rd, wr)

    def scan(out, d0, d1, init, op0, op1, rd, wr, n=C, half=False):
        return add(P, {"v": vec(n / 2 if half else n)}, lambda e: g.vector.tensor_tensor_scan(out, d0, d1, init, op0, op1), rd, wr)

    def vcopy(out, in_, rd, wr, n=20): return add(P, {"v": vec(n)}, lambda e: g.vector.tensor_copy(out, in_), rd, wr)

    def fill(out, x, wr, n=20): return add(P, {"v": vec(n)}, lambda e: g.vector.memset(out, x), [], wr)

    def scatter(out, in_, rd, wr): return add(P, {"v": 50 + C * CY * SA_}, lambda e: g.vector.tensor_copy(out, in_), rd, wr)

    def act(out, in_, func, rd, wr, scale=1.0, bias=None, ind=False):
        def call(e): return g.scalar.activation(out, in_, func, scale=scale) if bias is None else g.scalar.activation(out, in_, func, bias=bias, scale=scale)
        return add(P, {"s": gat("s", C) if ind else C * CY}, call, rd, wr)

    def either(call, rd, wr, ind, n=C, half=False):
        return add(P, {"v": gat("v", n), "s": gat("s", n)} if ind else {"v": vec(n / 2 if half else n), "s": n * CY}, call, rd, wr)

    def move(out, in_, rd, wr, ind=False, scale=None, n=C, half=False):
        def call(e):
            if e == "s": return g.scalar.activation(out, in_, AF.Copy) if scale is None else g.scalar.activation(out, in_, AF.Copy, scale=scale)
            return g.vector.tensor_copy(out, in_) if scale is None else g.vector.tensor_scalar(out, in_, scale, None, A.mult)
        return either(call, rd, wr, ind, n, half)

    def affine(out, in_, a, b, rd, wr, ind=False, half=False, n=C):
        def call(e):
            if e == "s": return g.scalar.activation(out, in_, AF.Identity, bias=b, scale=a)
            return g.vector.tensor_scalar(out, in_, a, b, A.mult, A.add)
        return either(call, rd, wr, ind, n, half)

    def gather(row, nm, win, lst, rd, halves, line=None):
        for a, b, wr in ((0, 10, [nm + "0"]), (10, 20, [nm + "1"])) if halves else ((0, 20, [nm + "0", nm + "1"]),):
            out, in_ = row(nm, C, 16 * a, 16 * b), win.indirect(lst(a, b))
            if line: affine(out, in_, line[0], line[1], rd, wr, ind=True, n=16 * (b - a))
            else: move(out, in_, rd, wr, ind=True, n=16 * (b - a))

    def shift(out, in_, x, rd, wr, n=C):
        def call(e):
            if e == "s": return g.scalar.activation(out, in_, AF.Identity, bias=x)
            return g.vector.tensor_scalar(out, in_, x, None, A.add)
        return either(call, rd, wr, False, n)

    def quant(q, s, in_, n, rd, wr): return add(P, {"v": (12 + 0.22 * 4 * n) * CY / 0.83}, lambda e: g.vector.quantize_mx(q, s, in_), rd, wr)

    def bank(b, lo=0, hi=C): return T.ps[:, 512 * b + lo:512 * b + hi]

    def mm(b, w, ws, x, xs, rd, n=C):
        return add(P, {"t": PE * (n + 16)}, lambda e: g.tensor.matmul_mx(bank(b, 0, n), w, ws, x, xs, True, True), rd, ["ps%d" % b])

    def load(q, nm, out, in_):
        return add(P, {q: 60.0}, lambda e: (g.sync if e == "y" else g.scalar).dma_start(out, in_), [], [nm], sem="ld_" + nm, lat=LOAD)

    load("y", "fl", T.fli[:], T.fl[:, :])
    load("y", "ml", T.mli[:], T.ml[:, :])
    load("s", "x", T.xin[:], T.x[:, :])
    load("y", "u", T.uin[:], T.u[:, :])
    load("y", "wc", T.wq[:].bitcast(dt.uint8), T.wc[:, :])
    load("y", "ws", T.wsc[:], T.ws[:, :])
    load("y", "v", T.vin[:], T.v[:, :])

    def iota(out, pat, base, cm, wr, n, fl):
        def call(e): return g.iota(out, pat, base, cm, allow_small_or_imprecise_dtypes=True) if fl else g.iota(out, pat, base, cm)
        return add(P, {"g": 130 + 2 * n * CY}, call, [], wr)
    iota(T.pcol[:, 0:1], [[1, 1]], 0, 1, ["pcol"], 1, False)
    iota(B("jm"), [[0, C // 16], [1, 16]], 0, 0, ["jm"], C, True)
    iota(T.ui[:], [[16, 8]], 0, 0, ["ui"], 8, False)
    fill(B("step"), TINY / 2, ["step"], C / 2)
    scan(B("iob"), B("step"), B("step"), -(MID + 1) * TINY, A.add, A.add, ["step"], ["iob"], C, True)
    pc = T.pcol

    def col(k): return T.pcolf[:, k:k + 1]
    SC, PLACE, ISC, BIG, BIG2, LOW, LOW2, KSW, LEAD, ROOT = [col(k) for k in range(7, 16)] + [16]
    ts(pc[:, 5:6], pc[:, 0:1], 15, None, A.bitwise_and, None, ["pcol"], ["p15"])
    vcopy(PLACE, pc[:, 5:6], ["p15"], ["p15f"])
    ts(tf("fall", 20, 0, 16), B("jm", C, 0, 16), PLACE, 2.0 ** (-STEPB / 2), A.is_le, A.max, ["jm", "p15f"], ["fall"])
    scan(tf("fell", 20, 0, 16), tf("fall", 20, 0, 16), tf("fall", 20, 0, 16), 2.0 ** 96, A.mult, A.mult, ["fall"], ["fell"], 16)
    ts(SC, tf("fell", 20, 15, 16), 2.0 ** 6, None, A.mult, None, ["fell"], ["sc"])
    add(P, {"v": 200.0}, lambda e: g.vector.reciprocal(ISC, SC), ["sc"], ["isc"])
    for out, a, b, nm in ((col(ROOT), RISE / UNIT, 0.25, "root0"), (col(ROOT + 1), RISE / UNIT, 1.25, "root1"), (LEAD, RISE / UNIT, MID + 0.125, "lead"),
                          (LOW, RISE, MID, "low"), (LOW2, RISE, MID * UNIT + 1, "low2"), (KSW, 2.0, 0.0, "ksw")):
        affine(out, PLACE, a, b - 15 * a, ["p15f"], [nm], n=64)
    affine(col(18), PLACE, 0.0, 2.0 ** 51, ["p15f"], ["b51"], n=64)
    move(BIG, col(18), ["b51"], ["big"], scale=2.0 ** 51, n=64)
    move(BIG2, col(18), ["b51"], ["big2"], scale=2.0 ** 51 * UNIT, n=64)
    for q in range(2): ts(T.dcon[:, C * q:C * q + C], B("jm"), PLACE, 2.0 ** STEPB, A.is_gt, A.mult, ["jm", "p15f"], ["dcon%d" % q], C / 2)
    for nm, x in (("dkey", RISE * TINY), ("dgk", RISE * TINY / UNIT), ("dsw", 2.0)):
        affine(B(nm), T.dcon[:, 0:C], 33 * x / 2 ** STEPB, -32 * x, ["dcon0"], [nm], half=True)
    affine(F("lab"), B("iob"), UNIT, (MID * UNIT - MID - 1) * TINY, ["iob"], ["lab"])
    if LATE: affine(F("lab2"), B("iob"), UNIT, (MID * UNIT + 65 - MID) * TINY, ["iob"], ["lab2"])
    move(B("sum", 2 * C, 0, 1), B("iob", C, 0, 1), ["iob"], ["sum"], n=64)

    def whole(out, x, wr, n=20): return iota(out, [[0, n]], int(x), 0, wr, n, True)
    for nm in ("swk", "swgk"): whole(B(nm, 3 * C, 13, 3 * C, 16), 0, [nm], 60)
    whole(tf("fd", 120, 0, 120, 3), 0, ["fd0"], 40)
    def ua(k): return tf("ua", 80, k, 80, 4)
    def ub(k): return tf("ub", 80, k, 80, 4)
    def va(k): return tf("va", 100, k, 100, 5)
    def vb(k): return tf("vb", 100, k, 100, 5)
    for out, x, nm in ((ua(0), 0, "ua0"), (ua(3), 1, "ua3"), (va(0), 0, "va0"), (va(2), 1, "va2"), (va(3), -1, "va3"), (vb(2), WHOLE, "vb2"), (vb(3), WHOLE, "vb3")):
        whole(out, x, [nm])
    move(ua(2), ua(3), ["ua3", "isc"], ["ua2"], scale=ISC, n=64)
    for out, x, nm in ((ub(2), -MID - 0.5, "ub2"), (ub(3), 0.25, "ub3")): move(out, ua(2), ["ua2"], [nm], scale=x, n=64)
    move(vb(1), ua(3), ["ua3"], ["vb1"], scale=-0.5, n=64)
    def unit(b): return T.eq[:, 128 * b:128 * b + 128], T.es[:, 128 * b:128 * b + 128]
    fill(T.half[:], 0.5, ["half"], 256)
    for b in range(4):
        add(P, {"g": 170 + 1024 * CY}, lambda e, b=b: g.affine_select(T.et[:, 512 * b:512 * b + 512], T.half[:], [[1, 512]], A.is_equal, 0.0, -b, -4),
            ["half"], ["et%d" % b])
        quant(*unit(b), T.et[:, 512 * b:512 * b + 512], 128, ["et%d" % b], ["eq%d" % b])

    quant(T.xq0[:], T.xs0[:], T.xin[:], C, ["x"], ["X0"])
    vcopy(T.u16[:], T.ui[:], ["ui"], ["u16"])
    quant(T.uq[:], T.us[:], T.uin[:], 128, ["u"], ["uq"])
    add(P, {"v": gat("v", 128)}, lambda e: g.vector.tensor_copy(T.up[:].bitcast(dt.uint32), T.uq[:].bitcast(dt.uint32).indirect(T.u16[:])), ["uq", "u16"], ["up"])
    move(T.ups[:], T.us[:].indirect(T.u16[:]), ["uq", "u16"], ["ups"], ind=True, n=128)
    quant(T.vq[:], T.vs[:], T.vin[:], 128, ["v"], ["vq"])

    def kept(nm, w=1, q=0): return B(nm + "k", w * C, q * C + 15, q * C + C, 16)

    def compact(out, nm, bias, rd, wr, w=1):
        n = w * C
        scan(B(nm + "k", n), T.dcon[:, 0:n], B(nm, n), 0.0, A.mult, A.add, rd + ["dcon0", "dcon1"][:w], [nm + "k"], n, True)
        if out is not None: ts(out, B(nm + "k", n, 15, n, 16), SC, bias, A.mult, A.add, [nm + "k", "sc"], wr, 20 * w)

    vcopy(tu("LG0", 40, 0, 20), T.fli[:], ["fl"], ["L0_0"])
    vcopy(tu("M16"), T.mli[:], ["ml"], ["M16"])
    move(B("mr"), B("iob").indirect(tu("M16")), ["iob", "M16"], ["mr"], ind=True)
    iota(ti("blk"), [[16, 20]], 0, 0, ["blk"], 20, False)
    tt(tf("md"), T.mli[:], ti("blk"), A.subtract, ["ml", "blk"], ["md"])
    ts(tu("up"), tf("md"), PLACE, None, A.is_gt, None, ["md", "p15f"], ["up16"])
    affine(F("sg"), B("jm").indirect(tu("up")), 2.0, -1.0, ["jm", "up16"], ["sg"], ind=True)

    ends = [[(0, 0, C)], [(0, 0, TAIL), (1, TAIL, C)]]
    mids = [[(0, 0, C)], [(0, 0, LAYER), (1, LAYER, C)]]
    sent = [0]
    peers = [T.cores[rank ^ m] for m in MASKS]
    common = [e for e in topo.engines(core, peers[0]) if all(e in topo.engines(core, p) and e in topo.engines(p, core) for p in peers)]
    for r in range(ROUNDS):
        h = r % 2
        R = lambda nm: "%s_%d" % (nm, h)
        partner = T.cores[rank ^ MASKS[r]]
        rid, pid, _s = topo.addr(partner)
        X, Xq, Xs = "X%d" % r, T["xq%d" % r], T["xs%d" % r]

        def send(sem, pieces, rd, key, lat, engines):
            msk, ne = sum(1 << e for e in engines), len(engines)
            for dst, src in pieces:
                last = add(P, {"g": ISSUE}, lambda e, dst=dst, src=src, sem=sem, rid=rid, pid=pid, msk=msk: g.remote_dma(dst, src, T.sem[sem], T.sem.rl, pid, rid, msk),
                           rd, ["net" + key], sem="rl", val=0)
                sent[0] += ne
            add(P, {"n": 0.0}, None, [], [key], sem=sem, val=ne * len(pieces), after=[last], lat=lat)

        def send_codes(rd):
            send("aq%d" % r, [(T["lq%d" % r][:].bitcast(dt.uint8), Xq[:].bitcast(dt.uint8)), (T["ls%d" % r][:], Xs[:])], [X] + rd, "Y%d" % r, CODES, common[0::2])
        if r == 0: send_codes([])

        mm(0, T.up[:], T.ups[:], Xq[:], Xs[:], ["up", "ups", X])
        move(F(R("s")), bank(0), ["ps0"], [R("s")])
        for b in range(4):
            mm(1 + b, *unit(b), Xq[:], Xs[:], ["eq%d" % b, X])
            move(T["fh%d" % h][:, C * b:C * b + C], bank(1 + b), ["ps%d" % (1 + b)], ["fh%d%d" % (h, b)])

        LG, LN = "LG%d" % r, "LG%d" % (r + 1)
        FL, GL, FN, GN = "L0_%d" % r, "GL_%d" % r, "L0_%d" % (r + 1), "GL_%d" % (r + 1)
        fl_, gl_, fn_, gn_ = tu(LG, 40, 0, 20), tu(LG, 40, 20, 40), tu(LN, 40, 0, 20), tu(LN, 40, 20, 40)
        L = [FL] + [R("L%d" % k) for k in range(1, 8)]
        lists = [fl_] + [tu(k) for k in L[1:]]
        first, ahead = R("first"), 64 - MID
        gather(F, first, B("iob"), lambda a, b: tu(LG, 40, a, b), ["iob", FL], "first" in HALVES, (UNIT, (UNIT * MID + ahead) * TINY))

        def image(out, lst, rd, wr, n=C):
            affine(out, F(first).indirect(lst), 1 / UNIT, (-MID - ahead / UNIT) * TINY, [first + "0", first + "1"] + rd, wr, ind=True, n=n)
        m = PARTS[r]
        parts = [(q, q * C // m, (q + 1) * C // m) for q in range(m)]
        every = lambda nm: [nm + str(q) for q in range(m)]
        key = first
        for k in range(8):
            for q, a, b in parts if k < 7 else []:
                fr, nx = R("fr%d" % k), R("fr%d" % (k + 1))
                if k: move(B(nx, C, a, b), B(fr).indirect(tu(L[k], 20, a // 16, b // 16)), every(fr) + [L[k] + str(q)], [nx + str(q)], ind=True, n=b - a)
                else: image(B(nx, C, a, b), tu(LG, 40, a // 16, b // 16), [FL], [nx + str(q)], b - a)
                scan(B(nx + "k", C, a, b), T.dcon[:, a:b], B(nx, C, a, b), 0.0, A.mult, A.add, [nx + str(q), "dcon0"], [nx + "k" + str(q)], b - a, True)
                ts(tu(L[k + 1], 20, a // 16, b // 16), B(nx + "k", C, a + 15, b, 16), SC, MID + 0.25, A.mult, A.add, [nx + "k" + str(q), "sc"], [L[k + 1] + str(q)])
            w, nx, have = "w%d" % (k % 2), "key%d" % (k % 2), [key] if k else [first + "0", first + "1"]
            if k == 0 and r in LATE:
                tt(F(nx), F("lab2").indirect(lists[1]), F(key), A.min, ["lab2"] + have + every(L[1]), [nx], C, True)
            else:
                for q, a, b in parts: shift(F(w, C, a, b), F(key, C, a, b), 2.0 ** k * TINY, have, [w + str(q)] if m > 1 else [w + "0", w + "1"], b - a)
                tt(F(nx), F(w).indirect(lists[k]), F(key), A.min, [w + "0", w + "1"] + have + (every(L[k]) if k else [FL]), [nx], C, True)
            if k == 6: shift(F("near"), F(key), -64 * TINY, [key], ["near"])
            key = nx
        tt(F("key"), F(key).indirect(lists[6]), F("near"), A.min, [key, "near"] + every(L[6]), ["key"], C, True)
        key = "key"

        sa, sb, SA, O16 = T["sa%d" % r], T["sb%d" % r], "sa%d" % r, "sb%d" % r
        scan(F("keyk"), B("dkey"), F(key), 0.0, A.add, A.max, ["dkey", key], ["keyk"])
        for q in range(2): ts(tu("RL", 40, 20 * q, 20 * q + 20), F("keyk", C, 15, C, 16), 1 / (UNIT * TINY), col(ROOT + q), A.mult, A.add, ["keyk", "root%d" % q], ["RL%d" % q])
        ts(ti("ki"), F("keyk", C, 15, C, 16), BIG, LOW, A.mult, A.add, ["keyk", "big", "low"], ["ki"])
        ts(ti("ci"), ti("ki"), int(UNIT) - 1, None, A.bitwise_and, None, ["ki"], ["ci"])
        vcopy(sa[:, 20:40], ti("ci"), ["ci"], [SA + "c"])
        ts(tf("craw"), ti("ci"), ISC, None, A.mult, None, ["ci", "isc"], ["craw"])
        scan(F("mx"), F(key), F("lab"), -1.0, A.max, A.max, [key, "lab"], ["mx"])
        scan(B("sum", 2 * C, 1, C + 1), F("mx"), F("lab"), -MID * TINY, A.add, A.subtract, ["mx", "lab"], ["sum"])
        gather(B, "base", B("sum", 2 * C, 0, C + 1), lambda a, b: tu("RL", 40, a, b), ["sum", "RL0"], "base" in HALVES)
        compact(None, "base", 0.0, ["base0", "base1"], None)
        tt(tf("praw"), kept("base"), tf("craw"), A.add, ["basek", "craw"], ["praw"])
        ts(sa[:, 40:60], tf("praw"), SC, MID + 0.25, A.mult, A.add, ["praw", "sc"], [SA + "p"])
        affine(B("end"), B("sum", 2 * C, 0, C + 1).indirect(tu("RL", 40, 20, 40)), 1.0, -TINY, ["sum", "RL1"], ["end"], ind=True)
        compact(sa[:, 60:80], "end", MID + 0.25, ["end"], [SA + "e"])
        tt(tf("nraw"), kept("end"), kept("base"), A.subtract, ["basek", "endk"], ["nraw"])
        ts(sa[:, 0:20], tf("nraw"), SC, 0.25, A.mult, A.add, ["nraw", "sc"], [SA + "n"])
        send("aa%d" % r, [(T["la%d" % r][:], sa[:, 0:60])], [SA + "n", SA + "c", SA + "p"], "la%d" % r, LISTS, common)
        if r: send_codes(["netla%d" % r])
        ts(ua(1), sa[:, 0:20], 1.0, None, A.add, None, [SA + "n"], ["ua1"])
        tt(tf("left"), ua(1), ti("ci"), A.subtract, ["ua1", "ci"], ["left"])
        ol = R("ol")
        scatter(B(ol).indirect(sa[:, 40:60]), B("iob"), [SA + "p", "iob"], [ol])
        compact(sb[:], ol, MID + 0.25, [ol], [O16])
        send("ab%d" % r, [(T["lb%d" % r][:], sb[:])], [O16], "lb%d" % r, ORDER, common[1::2])
        if r == 0:
            ts(tf("wrap"), tf("left"), 1.5, ISC, A.is_lt, A.mult, ["left", "isc"], ["wrap"])
            tt(tf("back"), tf("wrap"), ua(1), A.mult, ["wrap", "ua1"], ["back"])
            tt(tf("next"), tf("praw"), tf("back"), A.subtract, ["praw", "back"], ["next"])
            ts(tu("N16"), tf("next"), SC, MID + 1.25, A.mult, A.add, ["next", "sc"], ["N16"])
            move(B("gl0"), B(ol).indirect(tu("N16")), [ol, "N16"], ["gl0"], ind=True)
            compact(gl_, "gl0", MID + 0.25, ["gl0"], [GL])
        act(B(R("flag")), B("iob").indirect(sa[:, 20:40]), AF.Relu, ["iob", SA + "c"], [R("flag")], scale=-2.0 ** 97, bias=(1.0 - MID) * TINY * 2.0 ** 97, ind=True)
        move(B(R("d0")), B(R("flag")).indirect(sb[:]), [R("flag"), O16], [R("d0")], scale=-2.0 ** 97, ind=True)
        affine(B(R("d1")), B(R("d0")), -1.0, TINY / UNIT, [R("d0")], [R("d1")], half=True)
        fg = R("fg")
        image(B(fg, 2 * C, 0, C), tu("M16"), ["M16"], [fg + "f"])
        move(B(fg, 2 * C, C, 2 * C), B("mr").indirect(gl_), ["mr", GL], [fg + "g"], ind=True)
        compact(None, fg, 0.0, [fg + "f", fg + "g"], None, 2)
        affine(tf("fgv", 40), B(fg + "k", 2 * C, 15, 2 * C, 16), SC, MID + 0.25, [fg + "k", "sc"], ["fgv"], n=64)
        ts(tf("fg0", 40), tu(LG, 40), 0.25, None, A.add, None, [FL, GL], ["fg0"], 40)
        tt(tf("fd", 120, 1, 120, 3), tf("fgv", 40), tf("fg0", 40), A.subtract, ["fgv", "fg0"], ["fd1"], 40)
        move(tf("fgk", 40), tf("fd", 120, 1, 120, 3), ["fd1", "ksw"], ["fgk"], scale=KSW, n=64)
        tt(tf("fd", 120, 2, 120, 3), tf("fgk", 40), tf("fg0", 40), A.add, ["fgk", "fg0"], ["fd2"], 40)

        gather(F, "so", F(R("s")), lambda a, b: sb[:, a:b], [R("s"), O16], "so" in HALVES)
        scan(F("pm"), B(R("d0")), F("so"), -2.0 ** 92, A.add, A.max, [R("d0"), "so0", "so1"], ["pm"])
        tt(F("eq"), F("pm").indirect(sa[:, 60:80]), F(R("s")), A.subtract, ["pm", SA + "e", R("s")], ["eq"], C, True)
        tt(B(R("cd")), F("eq").indirect(sb[:]), B(ol), A.add, ["eq", O16, ol], [R("cd")], C, True)
        scan(F("cs"), B(R("d1")), B(R("cd")), 0.0, A.add, A.min, [R("d1"), R("cd")], ["cs"])
        gather(F, "gk", F("cs"), lambda a, b: sa[:, 60 + a:60 + b], ["cs", SA + "e"], "gk" in HALVES)
        scan(F("gkk"), B("dgk"), F("gk"), 0.0, A.add, A.max, ["dgk", "gk0", "gk1"], ["gkk"])
        l16 = R("l16")
        ts(tu(l16), F("gkk", C, 15, C, 16), BIG, LEAD, A.mult, A.add, ["gkk", "big", "lead"], [l16])
        ts(ti("li"), F("gkk", C, 15, C, 16), BIG2, LOW2, A.mult, A.add, ["gkk", "big2", "low2"], ["li"])
        ts(ti("lj"), ti("li"), int(UNIT) - 1, None, A.bitwise_and, None, ["li"], ["lj"])
        tt(ub(1), tf("left"), ti("lj"), A.subtract, ["left", "lj"], ["ub1"])
        ts(ub(0), ub(1), -0.5, None, A.is_lt, None, ["ub1"], ["ub0"])
        scan(tf("uo", 80), tf("ua", 80), tf("ub", 80), 0.0, A.mult, A.add, ["u%s%d" % (x, k) for x in "ab" for k in range(4)], ["uo"], 80)

        xa, lb, LB = R("xa"), T["lb%d" % r][:], "lb%d" % r
        for q in range(3):
            move(B(xa, 3 * C, C * q, C * q + C), B("iob").indirect(T["la%d" % r][:, 20 * q:20 * q + 20]), ["iob", "la%d" % r], [xa + str(q)], ind=True)
        move(B(R("oe")), B("iob").indirect(lb), ["iob", LB], [R("oe")], ind=True)
        move(F("se"), F(R("s")).indirect(lb), [R("s"), LB], ["se"], ind=True)
        for q, nm in enumerate(("xn", "xc", "xb")):
            gather(B, nm, B(xa, 3 * C, C * q, C * q + C), lambda a, b: tu(l16, 20, a, b), [xa + str(q), l16], nm in HALVES)
        compact(ti("xni"), "xn", MID + 1.0, ["xn0", "xn1"], ["xni"])
        ts(va(4), ti("xni"), ISC, None, A.mult, None, ["xni", "isc"], ["va4"])
        add(P, {"v": 190 + 120 * CY}, lambda e: g.vector.reciprocal(va(1), va(4)), ["va4"], ["va1"])
        for k, nm in ((0, "xc"), (4, "xb")):
            compact(None, nm, 0.0, [nm + "0", nm + "1"], None)
            tt(vb(k), kept(nm), tf("uo", 80, 2 + k // 4, 80, 4), A.subtract, [nm + "k", "uo"], ["vb%d" % k])
        scan(tf("vo", 100), tf("va", 100), tf("vb", 100), 0.0, A.mult, A.add, ["va%d" % k for k in range(5)] + ["vb%d" % k for k in range(5)], ["vo"], 100)
        PL, T16 = R("PL"), R("T16")
        ts(tu(PL), tf("vo", 100, 4, 100, 5), SC, None, A.mult, None, ["vo", "sc"], [PL])
        move(B(R("tr")), B(R("oe")).indirect(tu(PL)), [R("oe"), PL], [R("tr")], ind=True)
        compact(tu(T16), R("tr"), MID + 0.25, [R("tr")], [T16])

        tt(F("st"), F("se").indirect(tu(PL)), F("sg"), A.mult, ["se", PL, "sg"], ["st"], C, True)
        for c in range(2):
            a, b = C // 2 * c, C // 2 * c + C // 2
            move(F("su", C, a, b), F("st", C, a, b), ["st"], ["su" + "ab"[c]], scale=-1.0, n=C // 2)
        tt(B("sw"), F("st").indirect(tu("M16")), F("su"), A.is_lt, ["st", "sua", "sub", "M16"], ["sw"], C, True)

        def choose(nm, pairs, rd, out, wr):
            scan(B(nm + "k", 3 * C, 0, 3 * C, 3), B("dsw"), B(nm), 0.0, A.add, A.max, ["dsw", nm], [nm + "k"], C, True)
            scan(tf(nm + "o", 60), B(nm + "k", 3 * C, 13, 3 * C, 16), pairs, 0.0, A.mult, A.add, [nm + "k"] + rd, [nm + "o"], 60)
            vcopy(out, tf(nm + "o", 60, 2, 60, 3), [nm + "o"], [wr])
        move(B("swg"), B("sw").indirect(gl_), ["sw", GL], ["swg"], ind=True)
        for nm, a, out, kk in (("sw", 0, fn_, FN), ("swg", 60, gn_, GN)): choose(nm, tf("fd", 120, a, a + 60), ["fd0", "fd1", "fd2"], out, kk)

        fh, fs, gp, zt, xt, rs = [T["%s%d" % (k, h)] for k in ("fh", "fs", "gp", "zt", "xt", "rs")]
        for b in range(4):
            bk, c = (5, 6, 7, 0)[b], slice(C * b, C * b + C)
            mm(bk, *unit(b), T["lq%d" % r][:], T["ls%d" % r][:], ["eq%d" % b, "Y%d" % r])
            move(fs[:, c], bank(bk), ["ps%d" % bk], ["fs%d%d" % (h, b)])
            for q, lo, hi in mids[r == ROUNDS - 1]:
                part = slice(C * b + lo, C * b + hi)
                move(gp[:, part], fs[:, c].indirect(tu(T16, 20, lo // 16, hi // 16)), ["fs%d%d" % (h, b), T16], ["gp%d%d%d" % (h, b, q)], ind=True, n=hi - lo)
                tt(zt[:, 4 * lo + b:4 * hi:4], fh[:, c].indirect(tu(LN, 40, lo // 16, hi // 16)), gp[:, part], A.add,
                   ["fh%d%d" % (h, b), FN, "gp%d%d%d" % (h, b, q)], ["zt%d%d%d" % (h, b, q)], hi - lo, True)
        zq, zs = T["zq%d" % h], T["zs%d" % h]
        for q, lo, hi in mids[r == ROUNDS - 1]:
            quant(zq[:, lo:hi], zs[:, lo:hi], zt[:, 4 * lo:4 * hi], hi - lo, ["zt%d%d%d" % (h, b, q) for b in range(4)], ["zq%d%d" % (h, q)])
        for b in range(4):
            bk, c = (5, 6, 7, 0)[b], slice(C * b, C * b + C)
            for q, lo, hi in mids[r == ROUNDS - 1]:
                at = ((1, 2, 3, 4), (6, 7, 0, 1))[q][b]
                mm(at, T.wq[:, 128 * b:128 * b + 128], T.wsc[:, 128 * b:128 * b + 128], zq[:, lo:hi], zs[:, lo:hi], ["wc", "ws", "zq%d%d" % (h, q)], hi - lo)
                move(rs[:, C * b + lo:C * b + hi], bank(at, 0, hi - lo), ["ps%d" % at], ["rs%d%d%d" % (h, b, q)], scale=2.0 ** -6, n=hi - lo)
            made = ["rs%d%d%d" % (h, b, q) for q, lo, hi in mids[r == ROUNDS - 1]] + [GN]
            if b < APART[r]: mm(bk, *unit(b), Xq[:], Xs[:], ["eq%d" % b, X])
            for q, lo, hi in ends[r == ROUNDS - 1]:
                out, lst, part, xk = xt[:, 4 * lo + b:4 * hi:4], tu(LN, 40, 20 + lo // 16, 20 + hi // 16), slice(C * b + lo, C * b + hi), "xt%d%d%d" % (h, b, q)
                if b < APART[r]:
                    move(T.pp[:, part], rs[:, c].indirect(lst), made, ["pp%d%d" % (b, q)], ind=True, n=hi - lo)
                    tt(out, T.pp[:, part], bank(bk, lo, hi), A.add, ["pp%d%d" % (b, q), "ps%d" % bk], [xk], (hi - lo) / 2)
                else:
                    tt(out, rs[:, c].indirect(lst), fh[:, part], A.add, made + ["fh%d%d" % (h, b)], [xk], hi - lo, True)
        for q, lo, hi in ends[r == ROUNDS - 1]:
            quant(T["xq%d" % (r + 1)][:, lo:hi], T["xs%d" % (r + 1)][:, lo:hi], xt[:, 4 * lo:4 * hi], hi - lo, ["xt%d%d%d" % (h, b, q) for b in range(4)],
                  ["X%d" % (r + 1) + "ab"[q] * (r == ROUNDS - 1)])

    xq, xs, X = T["xq%d" % ROUNDS], T["xs%d" % ROUNDS], ["X%d" % ROUNDS + "ab"[q] for q, lo, hi in ends[1]]

    def store(nm, out, in_, rd): add(P, {"y": 60.0}, lambda e: g.sync.dma_start(out, in_), rd, [], sem="st_" + nm, lat=2000.0)
    affine(T.nls[:], B("iob").indirect(tu("LG%d" % ROUNDS, 40, 0, 20)), BIG, float(MID), ["iob", "big", "L0_%d" % ROUNDS], ["nls"], ind=True)
    store("nl", T.nl[:, :], T.nls[0:128:16, :], ["nls"])
    for q, lo, hi in ends[1]:
        mm(1 + q, T.vq[:], T.vs[:], xq[:, lo:hi], xs[:, lo:hi], ["vq", X[q]], hi - lo)
        move(T.ys[:, lo:hi], bank(1 + q, 0, hi - lo), ["ps%d" % (1 + q)], ["ys%d" % q], n=hi - lo)
    store("oc", T.oc[:, :], xq[:].bitcast(dt.uint8), X)
    for k in range(4): store("os%d" % k, T.osc[4 * k:4 * k + 4, :], xs[32 * k:32 * k + 4, :], X)
    store("y", T.y[:, :], T.ys[:], ["ys%d" % q for q, lo, hi in ends[1]])

    seq, done = order(P)
    count = emit(P, g, T, seq)
    for nm in STORES: g.sync.wait_ge(T.sem["st_" + nm], 16)
    g.wait_ge(T.sem.rl, sent[0])
    for e, nm in (("v", "ev"), ("s", "es"), ("t", "et"), ("g", "eg")): g.sync.wait_ge(T.sem[nm], count[e])
